import numpy as np
import ml_dtypes


def mxq(x, axis, fmt="e4m3"):
    dtype, down = {"e4m3": (ml_dtypes.float8_e4m3fn, 7), "e5m2": (ml_dtypes.float8_e5m2, 14)}[fmt]
    v = np.moveaxis(np.asarray(x, np.float32).astype(ml_dtypes.bfloat16).astype(np.float64), axis, -1)
    blocks = v.reshape(v.shape[:-1] + (-1, 32))
    amax = np.abs(blocks).max(-1, keepdims=True)
    byte = np.maximum(np.where(amax > 0, np.frexp(amax)[1] - 1 + 127, 0) - down, 1)
    scale = np.exp2(byte - 127.0)
    codes = (blocks / scale).astype(np.float32).astype(dtype).astype(np.float64)
    return np.moveaxis((codes * scale).reshape(v.shape), -1, axis)


WIDE = False


def mx_kscale(k):
    if not WIDE:
        return np.ones(k)
    levels = np.array([10, -10, 5, -5, 0])
    if k % 512:
        return np.exp2(np.random.permutation(np.resize(levels, k // 32))).repeat(32)
    a = np.empty((k // 512, 16))
    for p in range(k // 512):
        a[p, :8] = np.random.permutation(np.resize(levels, 8))
        for g in range(8):
            far = levels[np.abs(levels - a[p, g]) >= 10]
            a[p, g + 8] = far[np.random.randint(len(far))]
    return np.exp2(a.ravel()).repeat(32)


def f64(x):
    return np.asarray(x).astype(np.float64)


def striped(idx):
    return np.tile(np.asarray(idx).reshape(-1, 16).T, (8, 1)).astype(np.uint16)


def unstriped(offs):
    return offs[:16].T.reshape(-1).astype(np.int64)


B, N, T, D, DV, NQ = 2, 512, 2048, 512, 256, 256
PAGE = 64


def setup_inputs():
    n = np.random.standard_normal
    pages = np.random.permutation(T // PAGE)[:B * N // PAGE]
    idx = (pages[:, None] * PAGE + np.arange(PAGE)[None, :]).reshape(-1)
    s = mx_kscale(D)[:, None]
    u = np.ones(T)
    u[idx] = mx_kscale(B * N)
    r = np.random.uniform(0.5, 2.0, T)
    k = n((D, T)) / s
    v = n((DV, T)) / (u * r)
    return {
        "qT": (n((B, D, NQ)) * s * (1.00 / np.sqrt(D))).astype(np.float32),
        "kT": k.astype(np.float32),
        "vT": v.astype(np.float32),
        "vs": np.tile(u * r, (128, 1)).astype(np.float32),
        "kb": np.tile(n(T), (128, 1)).astype(np.float32),
        "offs": striped(idx),
    }


def reference(qT, kT, vT, vs, kb, offs):
    idx = unstriped(offs)
    k = f64(kT)
    v = f64(vT)
    pick = lambda x: x[:, idx].reshape(x.shape[0], B, N).transpose(1, 0, 2)
    q = f64(qT)
    score = mxq(q, 1, "e4m3").transpose(0, 2, 1) @ mxq(pick(k), 1, "e4m3")
    score = score + pick(f64(kb))[:, :1, :]
    p = 1.0 / (1.0 + np.exp(-score))
    w = p * pick(f64(vs))[:, :1, :]
    y = mxq(w, 2, "e4m3") @ mxq(pick(v).transpose(0, 2, 1), 1, "e4m3")
    y = y / 16.0
    return y

@@ -1,0 +1,191 @@
+from contextlib import ExitStack
+
+import concourse.mybir as mybir
+from concourse.masks import make_identity
+
+B, NQ, D, DV, N, T = 2, 256, 512, 256, 512, 2048
+P = 128
+PACK = 4
+FLOPS = 2 * B * NQ * N * (D + DV)
+BYTES = 4 * (B * D * NQ + D * T + DV * T + 2 * T + B * NQ * DV) + 2 * P * (B * N // 16)
+
+F32 = mybir.dt.float32
+BF16 = mybir.dt.bfloat16
+U32 = mybir.dt.uint32
+I32 = mybir.dt.int32
+U16 = mybir.dt.uint16
+U8 = mybir.dt.uint8
+FP8X4 = mybir.dt.float8_e4m3fn_x4
+COPY = mybir.ActivationFunctionType.Copy
+SIGMOID = mybir.ActivationFunctionType.Sigmoid
+MULT = mybir.AluOpType.mult
+
+CHUNKS = (((0, 1024, 640), (1024, 1024, 640)), ((0, 1024, 640), (1024, 1024, 384)))
+
+
+def tile_attend_sigmoid_kernel(tc, qT, kT, vT, vs, kb, offs, out):
+    nc = tc.nc
+    with ExitStack() as ctx:
+        keep = ctx.enter_context(tc.tile_pool(name="keep", bufs=1))
+        psum_s = ctx.enter_context(tc.psum_pool(name="psum_s", bufs=4))
+        psum_t = ctx.enter_context(tc.psum_pool(name="psum_t", bufs=2))
+        psum_y = ctx.enter_context(tc.psum_pool(name="psum_y", bufs=2))
+
+        lists = keep.tile([P, B * N // 16], U16, name="lists")
+        nc.sync.dma_start(lists[:], offs)
+
+        k_rows = kT.rearrange("(p j) n -> p j n", j=PACK)
+        staged = {}
+        for c in range(2):
+            for h, (n0, width, _) in enumerate(CHUNKS[c]):
+                raw = keep.tile([P, 2, width], F32, name=f"k_raw{c}{h}")
+                nc.sync.dma_start(out=raw[:], in_=k_rows[:, 2 * c : 2 * c + 2, n0 : n0 + width])
+                staged[c, h] = raw
+        q_rows = qT.rearrange("b (p j) q -> b p j q", j=PACK)
+        q_raw = []
+        for b in range(B):
+            raw = keep.tile([P, PACK, NQ], F32, name=f"q_raw{b}")
+            nc.sync.dma_start(out=raw[:], in_=q_rows[b])
+            q_raw.append(raw)
+        v_rows = vT.rearrange("(e p) n -> e p n", p=P)
+        v_win = []
+        for e in range(2):
+            win = keep.tile([P, T], F32, name=f"v_win{e}")
+            nc.sync.dma_start(out=win[:], in_=v_rows[e])
+            v_win.append(win)
+
+        warm = keep.tile([P, 1], F32, name="warm")
+        nc.vector.memset(warm[:], 0.0)
+        warmed = keep.tile([P, 1], F32, name="warmed")
+        nc.scalar.activation(warmed[:], warm[:], SIGMOID)
+
+        kb_win = keep.tile([P, T], F32, name="kb_win")
+        vs_win = keep.tile([P, T], F32, name="vs_win")
+        nc.vector.memset(kb_win[:], 0.0)
+        nc.vector.memset(vs_win[:], 0.0)
+        nc.scalar.dma_start(out=kb_win[0:1, :], in_=kb[0:1, :])
+        nc.scalar.dma_start(out=vs_win[0:1, :], in_=vs[0:1, :])
+        ident = keep.tile([P, P], F32, name="ident")
+        make_identity(nc, ident[:])
+
+        cols = []
+        for name, win in (("kb", kb_win), ("vs", vs_win)):
+            got = keep.tile([P, B * N], F32, name=f"{name}_got")
+            nc.vector.tensor_copy(got[:], win[:].indirect(lists[:]))
+            col = keep.tile([P, B, PACK], F32, name=f"{name}_col")
+            for b in range(B):
+                turned = psum_t.tile([P, PACK, P], F32, name="turned")
+                for t in range(PACK):
+                    nc.tensor.transpose(turned[:, t, :], got[:, b * N + t : (b + 1) * N : PACK], ident[:])
+                nc.vector.tensor_copy(col[:, b, :], turned[:, :, 0])
+            cols.append(col)
+        kb_col, vs_col = cols
+
+        words = []
+        for b in range(B):
+            got = keep.tile([P, 2 * 2 * N], BF16, name=f"k_got{b}", align_bytes=64)
+            words.append(got)
+        for c in range(2):
+            pool_words = keep.tile([P, 2 * T], BF16, name=f"k_pool{c}", align_bytes=64)
+            for h, (n0, width, split) in enumerate(CHUNKS[c]):
+                raw = staged[c, h]
+                dst = pool_words[:, 2 * n0 : 2 * (n0 + width)].rearrange("p (c i e) -> p c e i", i=4, e=2)
+                src = raw[:].rearrange("p e (c i) -> p c e i", i=4)
+                g = split // 4
+                nc.scalar.activation(dst[:, :g], src[:, :g], COPY)
+                nc.vector.tensor_copy(dst[:, g:], src[:, g:])
+            for b in range(B):
+                nc.vector.tensor_copy(
+                    words[b][:].bitcast(U32)[:, c * N : (c + 1) * N],
+                    pool_words[:].bitcast(U32).indirect(lists[:, b * (N // 16) : (b + 1) * (N // 16)]),
+                )
+
+        q_codes = keep.tile([P, B * NQ], U32, name="q_codes", align_bytes=64)
+        q_scales = keep.tile([P, B * NQ], U8, name="q_scales", align_bytes=64)
+        for b in range(B):
+            grouped = keep.tile([P, NQ * PACK], BF16, name=f"q_grouped{b}", align_bytes=64)
+            nc.scalar.activation(
+                grouped[:].rearrange("p (c i j) -> p c j i", i=4, j=PACK),
+                q_raw[b][:].rearrange("p j (c i) -> p c j i", i=4),
+                COPY,
+            )
+            span = slice(b * NQ, (b + 1) * NQ)
+            nc.vector.quantize_mx(out=q_codes[:, span].bitcast(FP8X4), scales=q_scales[:, span], in_=grouped[:])
+
+        p_tiles = []
+        for b in range(B):
+            grouped = keep.tile([P, N * PACK], BF16, name=f"k_grouped{b}", align_bytes=64)
+            nc.vector.tensor_copy(
+                grouped[:].bitcast(I32).rearrange("p (t s c) -> p s c t", t=PACK, c=2),
+                words[b][:].bitcast(I32).rearrange("p (c s t) -> p s c t", t=PACK, c=2),
+            )
+            k_codes = keep.tile([P, N], U32, name=f"k_codes{b}", align_bytes=64)
+            k_scales = keep.tile([P, N], U8, name=f"k_scales{b}", align_bytes=64)
+            nc.vector.quantize_mx(out=k_codes[:].bitcast(FP8X4), scales=k_scales[:], in_=grouped[:])
+            prob = keep.tile([P, PACK, NQ], F32, name=f"prob{b}")
+            span = slice(b * NQ, (b + 1) * NQ)
+            for half in range(2):
+                score = psum_s.tile([P, 2, NQ], F32, name="score")
+                for u in range(2):
+                    t = 2 * half + u
+                    cols_t = slice(t * P, (t + 1) * P)
+                    nc.tensor.matmul_mx(
+                        out=score[:, u, :],
+                        lhsT=k_codes[:, cols_t].bitcast(FP8X4),
+                        lhsT_scale=k_scales[:, cols_t],
+                        rhs=q_codes[:, span].bitcast(FP8X4),
+                        rhs_scale=q_scales[:, span],
+                        start=True,
+                        stop=True,
+                    )
+                for u in range(2):
+                    t = 2 * half + u
+                    nc.scalar.activation(prob[:, t, :], score[:, u, :], SIGMOID, bias=kb_col[:, b, t : t + 1])
+            p_tiles.append(prob)
+
+        w_codes, w_scales = [], []
+        for b in range(B):
+            grouped = keep.tile([P, NQ * PACK], BF16, name=f"w_grouped{b}", align_bytes=64)
+            nc.vector.tensor_tensor(
+                grouped[:].rearrange("p (c i t) -> p c t i", i=4, t=PACK),
+                p_tiles[b][:].rearrange("p t (c i) -> p c t i", i=4),
+                vs_col[:, b, :].unsqueeze(1).unsqueeze(3).to_broadcast([P, NQ // 4, PACK, 4]),
+                MULT,
+            )
+            codes = keep.tile([P, NQ], U32, name=f"w_codes{b}", align_bytes=64)
+            scales = keep.tile([P, NQ], U8, name=f"w_scales{b}", align_bytes=64)
+            nc.vector.quantize_mx(out=codes[:].bitcast(FP8X4), scales=scales[:], in_=grouped[:])
+            w_codes.append(codes)
+            w_scales.append(scales)
+
+        for e in range(2):
+            for b in range(B):
+                got = keep.tile([P, N], F32, name=f"v_got{e}{b}")
+                nc.vector.tensor_copy(got[:], v_win[e][:].indirect(lists[:, b * (N // 16) : (b + 1) * (N // 16)]))
+                turned = psum_t.tile([P, PACK, P], F32, name="turned")
+                for t in range(PACK):
+                    nc.tensor.transpose(turned[:, t, :], got[:, t :: PACK], ident[:])
+                grouped = keep.tile([P, P * PACK], BF16, name=f"v_grouped{e}{b}", align_bytes=64)
+                nc.scalar.activation(
+                    grouped[:].rearrange("p (e t) -> p e t", t=PACK), turned[:].rearrange("p t e -> p e t"), COPY
+                )
+                v_codes = keep.tile([P, P], U32, name=f"v_codes{e}{b}", align_bytes=64)
+                v_scales = keep.tile([P, P], U8, name=f"v_scales{e}{b}", align_bytes=64)
+                nc.vector.quantize_mx(out=v_codes[:].bitcast(FP8X4), scales=v_scales[:], in_=grouped[:])
+                y = psum_y.tile([P, 2, P], F32, name="y")
+                for h in range(2):
+                    rows = slice(h * P, (h + 1) * P)
+                    nc.tensor.matmul_mx(
+                        out=y[:, h, :],
+                        lhsT=w_codes[b][:, rows].bitcast(FP8X4),
+                        lhsT_scale=w_scales[b][:, rows],
+                        rhs=v_codes[:].bitcast(FP8X4),
+                        rhs_scale=v_scales[:],
+                        start=True,
+                        stop=True,
+                    )
+                result = keep.tile([P, 2, P], F32, name=f"result{e}{b}")
+                nc.scalar.activation(result[:], y[:], COPY, scale=1.0 / 16.0)
+                nc.sync.dma_start(
+                    out=out[b].rearrange("(h p) e -> p h e", p=P)[:, :, e * P : (e + 1) * P], in_=result[:]
+                )

@@ -6,6 +6,7 @@ from concourse.masks import make_identity
 B, NQ, D, DV, N, T = 2, 256, 512, 256, 512, 2048
 P = 128
 PACK = 4
+COLS = N // 16
 FLOPS = 2 * B * NQ * N * (D + DV)
 BYTES = 4 * (B * D * NQ + D * T + DV * T + 2 * T + B * NQ * DV) + 2 * P * (B * N // 16)
 
@@ -19,8 +20,7 @@ FP8X4 = mybir.dt.float8_e4m3fn_x4
 COPY = mybir.ActivationFunctionType.Copy
 SIGMOID = mybir.ActivationFunctionType.Sigmoid
 MULT = mybir.AluOpType.mult
-
-CHUNKS = (((0, 1024, 640), (1024, 1024, 640)), ((0, 1024, 640), (1024, 1024, 384)))
+ROW = P - 1
 
 
 def tile_attend_sigmoid_kernel(tc, qT, kT, vT, vs, kb, offs, out):
@@ -31,16 +31,21 @@ def tile_attend_sigmoid_kernel(tc, qT, kT, vT, vs, kb, offs, out):
         psum_t = ctx.enter_context(tc.psum_pool(name="psum_t", bufs=2))
         psum_y = ctx.enter_context(tc.psum_pool(name="psum_y", bufs=2))
 
-        lists = keep.tile([P, B * N // 16], U16, name="lists")
+        lists = keep.tile([P, B * COLS], U16, name="lists")
         nc.sync.dma_start(lists[:], offs)
+        part = [lists[:, b * COLS : (b + 1) * COLS] for b in range(B)]
 
-        k_rows = kT.rearrange("(p j) n -> p j n", j=PACK)
-        staged = {}
-        for c in range(2):
-            for h, (n0, width, _) in enumerate(CHUNKS[c]):
-                raw = keep.tile([P, 2, width], F32, name=f"k_raw{c}{h}")
-                nc.sync.dma_start(out=raw[:], in_=k_rows[:, 2 * c : 2 * c + 2, n0 : n0 + width])
-                staged[c, h] = raw
+        kb_win = keep.tile([P, T], F32, name="kb_win")
+        vs_win = keep.tile([P, T], F32, name="vs_win")
+        nc.scalar.dma_start(out=kb_win[ROW:P, :], in_=kb[0:1, :])
+        nc.scalar.dma_start(out=vs_win[ROW:P, :], in_=vs[0:1, :])
+
+        k_rows = kT.rearrange("(p j) n -> j p n", j=PACK)
+        k_win = []
+        for j in range(PACK):
+            win = keep.tile([P, T], F32, name=f"k_win{j}")
+            nc.sync.dma_start(out=win[:], in_=k_rows[j])
+            k_win.append(win)
         q_rows = qT.rearrange("b (p j) q -> b p j q", j=PACK)
         q_raw = []
         for b in range(B):
@@ -59,12 +64,8 @@ def tile_attend_sigmoid_kernel(tc, qT, kT, vT, vs, kb, offs, out):
         warmed = keep.tile([P, 1], F32, name="warmed")
         nc.scalar.activation(warmed[:], warm[:], SIGMOID)
 
-        kb_win = keep.tile([P, T], F32, name="kb_win")
-        vs_win = keep.tile([P, T], F32, name="vs_win")
-        nc.vector.memset(kb_win[:], 0.0)
-        nc.vector.memset(vs_win[:], 0.0)
-        nc.scalar.dma_start(out=kb_win[0:1, :], in_=kb[0:1, :])
-        nc.scalar.dma_start(out=vs_win[0:1, :], in_=vs[0:1, :])
+        nc.vector.memset(kb_win[:ROW, :], 0.0)
+        nc.vector.memset(vs_win[:ROW, :], 0.0)
         ident = keep.tile([P, P], F32, name="ident")
         make_identity(nc, ident[:])
 
@@ -74,34 +75,46 @@ def tile_attend_sigmoid_kernel(tc, qT, kT, vT, vs, kb, offs, out):
             nc.vector.tensor_copy(got[:], win[:].indirect(lists[:]))
             col = keep.tile([P, B, PACK], F32, name=f"{name}_col")
             for b in range(B):
-                turned = psum_t.tile([P, PACK, P], F32, name="turned")
+                turned = psum_s.tile([P, PACK, P], F32, name="score")
                 for t in range(PACK):
                     nc.tensor.transpose(turned[:, t, :], got[:, b * N + t : (b + 1) * N : PACK], ident[:])
-                nc.vector.tensor_copy(col[:, b, :], turned[:, :, 0])
+                nc.scalar.copy(col[:, b, :], turned[:, :, ROW])
             cols.append(col)
         kb_col, vs_col = cols
 
-        words = []
-        for b in range(B):
-            got = keep.tile([P, 2 * 2 * N], BF16, name=f"k_got{b}", align_bytes=64)
-            words.append(got)
-        for c in range(2):
-            pool_words = keep.tile([P, 2 * T], BF16, name=f"k_pool{c}", align_bytes=64)
-            for h, (n0, width, split) in enumerate(CHUNKS[c]):
-                raw = staged[c, h]
-                dst = pool_words[:, 2 * n0 : 2 * (n0 + width)].rearrange("p (c i e) -> p c e i", i=4, e=2)
-                src = raw[:].rearrange("p e (c i) -> p c e i", i=4)
-                g = split // 4
-                nc.scalar.activation(dst[:, :g], src[:, :g], COPY)
-                nc.vector.tensor_copy(dst[:, g:], src[:, g:])
-            for b in range(B):
-                nc.vector.tensor_copy(
-                    words[b][:].bitcast(U32)[:, c * N : (c + 1) * N],
-                    pool_words[:].bitcast(U32).indirect(lists[:, b * (N // 16) : (b + 1) * (N // 16)]),
-                )
+        both = keep.tile([P, 2 * B * N * 2], BF16, name="k_pairs", align_bytes=64)
+        words = both[:].bitcast(I32)
+        pairs = [both[:].rearrange("p (c i e) -> p c i e", c=2, e=2)[:, c] for c in range(2)]
+        for j in range(PACK - 1):
+            nc.vector.tensor_copy(pairs[j // 2][:, :, j % 2], k_win[j][:].indirect(lists[:]))
 
-        q_codes = keep.tile([P, B * NQ], U32, name="q_codes", align_bytes=64)
-        q_scales = keep.tile([P, B * NQ], U8, name="q_scales", align_bytes=64)
+        def interleave_keys(b):
+            nc.vector.tensor_copy(pairs[1][:, b * N : (b + 1) * N, 1], k_win[PACK - 1][:].indirect(part[b]))
+            grouped = keep.tile([P, N * PACK], BF16, name=f"k_grouped{b}", align_bytes=64)
+            nc.vector.tensor_copy(
+                grouped[:].bitcast(I32).rearrange("p (t s c) -> p s c t", t=PACK, c=2),
+                words.rearrange("p (c b s t) -> p b s c t", c=2, b=B, t=PACK)[:, b],
+            )
+            return grouped
+
+        def quantise(name, grouped, width):
+            codes = keep.tile([P, width], U32, name=f"{name}_codes", align_bytes=64)
+            scales = keep.tile([P, width], U8, name=f"{name}_scales", align_bytes=64)
+            nc.vector.quantize_mx(out=codes[:].bitcast(FP8X4), scales=scales[:], in_=grouped[:])
+            return codes, scales
+
+        def product(target, lhs, lhs_cols, rhs, rhs_cols):
+            nc.tensor.matmul_mx(
+                out=target,
+                lhsT=lhs[0][:, lhs_cols].bitcast(FP8X4),
+                lhsT_scale=lhs[1][:, lhs_cols],
+                rhs=rhs[0][:, rhs_cols].bitcast(FP8X4),
+                rhs_scale=rhs[1][:, rhs_cols],
+                start=True,
+                stop=True,
+            )
+
+        q_grouped = []
         for b in range(B):
             grouped = keep.tile([P, NQ * PACK], BF16, name=f"q_grouped{b}", align_bytes=64)
             nc.scalar.activation(
@@ -109,42 +122,25 @@ def tile_attend_sigmoid_kernel(tc, qT, kT, vT, vs, kb, offs, out):
                 q_raw[b][:].rearrange("p j (c i) -> p c j i", i=4),
                 COPY,
             )
-            span = slice(b * NQ, (b + 1) * NQ)
-            nc.vector.quantize_mx(out=q_codes[:, span].bitcast(FP8X4), scales=q_scales[:, span], in_=grouped[:])
+            q_grouped.append(grouped)
 
+        k_grouped = [interleave_keys(b) for b in range(B)]
         p_tiles = []
         for b in range(B):
-            grouped = keep.tile([P, N * PACK], BF16, name=f"k_grouped{b}", align_bytes=64)
-            nc.vector.tensor_copy(
-                grouped[:].bitcast(I32).rearrange("p (t s c) -> p s c t", t=PACK, c=2),
-                words[b][:].bitcast(I32).rearrange("p (c s t) -> p s c t", t=PACK, c=2),
-            )
-            k_codes = keep.tile([P, N], U32, name=f"k_codes{b}", align_bytes=64)
-            k_scales = keep.tile([P, N], U8, name=f"k_scales{b}", align_bytes=64)
-            nc.vector.quantize_mx(out=k_codes[:].bitcast(FP8X4), scales=k_scales[:], in_=grouped[:])
+            k_mx = quantise(f"k{b}", k_grouped[b], N)
+            q_mx = quantise(f"q{b}", q_grouped[b], NQ)
             prob = keep.tile([P, PACK, NQ], F32, name=f"prob{b}")
-            span = slice(b * NQ, (b + 1) * NQ)
             for half in range(2):
                 score = psum_s.tile([P, 2, NQ], F32, name="score")
                 for u in range(2):
                     t = 2 * half + u
-                    cols_t = slice(t * P, (t + 1) * P)
-                    nc.tensor.matmul_mx(
-                        out=score[:, u, :],
-                        lhsT=k_codes[:, cols_t].bitcast(FP8X4),
-                        lhsT_scale=k_scales[:, cols_t],
-                        rhs=q_codes[:, span].bitcast(FP8X4),
-                        rhs_scale=q_scales[:, span],
-                        start=True,
-                        stop=True,
-                    )
+                    product(score[:, u, :], k_mx, slice(t * P, (t + 1) * P), q_mx, slice(0, NQ))
                 for u in range(2):
                     t = 2 * half + u
                     nc.scalar.activation(prob[:, t, :], score[:, u, :], SIGMOID, bias=kb_col[:, b, t : t + 1])
             p_tiles.append(prob)
 
-        w_codes, w_scales = [], []
-        for b in range(B):
+        def weights(b):
             grouped = keep.tile([P, NQ * PACK], BF16, name=f"w_grouped{b}", align_bytes=64)
             nc.vector.tensor_tensor(
                 grouped[:].rearrange("p (c i t) -> p c t i", i=4, t=PACK),
@@ -152,40 +148,38 @@ def tile_attend_sigmoid_kernel(tc, qT, kT, vT, vs, kb, offs, out):
                 vs_col[:, b, :].unsqueeze(1).unsqueeze(3).to_broadcast([P, NQ // 4, PACK, 4]),
                 MULT,
             )
-            codes = keep.tile([P, NQ], U32, name=f"w_codes{b}", align_bytes=64)
-            scales = keep.tile([P, NQ], U8, name=f"w_scales{b}", align_bytes=64)
-            nc.vector.quantize_mx(out=codes[:].bitcast(FP8X4), scales=scales[:], in_=grouped[:])
-            w_codes.append(codes)
-            w_scales.append(scales)
+            return grouped
 
-        for e in range(2):
-            for b in range(B):
-                got = keep.tile([P, N], F32, name=f"v_got{e}{b}")
-                nc.vector.tensor_copy(got[:], v_win[e][:].indirect(lists[:, b * (N // 16) : (b + 1) * (N // 16)]))
-                turned = psum_t.tile([P, PACK, P], F32, name="turned")
-                for t in range(PACK):
-                    nc.tensor.transpose(turned[:, t, :], got[:, t :: PACK], ident[:])
-                grouped = keep.tile([P, P * PACK], BF16, name=f"v_grouped{e}{b}", align_bytes=64)
-                nc.scalar.activation(
-                    grouped[:].rearrange("p (e t) -> p e t", t=PACK), turned[:].rearrange("p t e -> p e t"), COPY
-                )
-                v_codes = keep.tile([P, P], U32, name=f"v_codes{e}{b}", align_bytes=64)
-                v_scales = keep.tile([P, P], U8, name=f"v_scales{e}{b}", align_bytes=64)
-                nc.vector.quantize_mx(out=v_codes[:].bitcast(FP8X4), scales=v_scales[:], in_=grouped[:])
-                y = psum_y.tile([P, 2, P], F32, name="y")
-                for h in range(2):
-                    rows = slice(h * P, (h + 1) * P)
-                    nc.tensor.matmul_mx(
-                        out=y[:, h, :],
-                        lhsT=w_codes[b][:, rows].bitcast(FP8X4),
-                        lhsT_scale=w_scales[b][:, rows],
-                        rhs=v_codes[:].bitcast(FP8X4),
-                        rhs_scale=v_scales[:],
-                        start=True,
-                        stop=True,
-                    )
-                result = keep.tile([P, 2, P], F32, name=f"result{e}{b}")
-                nc.scalar.activation(result[:], y[:], COPY, scale=1.0 / 16.0)
-                nc.sync.dma_start(
-                    out=out[b].rearrange("(h p) e -> p h e", p=P)[:, :, e * P : (e + 1) * P], in_=result[:]
-                )
+        def values(e, b):
+            got = keep.tile([P, N], BF16, name=f"v_got{e}{b}", align_bytes=64)
+            nc.vector.tensor_copy(got[:], v_win[e][:].indirect(part[b]))
+            turned = psum_t.tile([P, 2, P], F32, name="turned")
+            for u in range(2):
+                nc.tensor.transpose(turned[:, u, :], got[:].bitcast(F32)[:, u::2], ident[:])
+            grouped = keep.tile([P, P * PACK], BF16, name=f"v_grouped{e}{b}", align_bytes=64)
+            nc.scalar.copy(
+                grouped[:].bitcast(F32).rearrange("p (e u) -> p e u", u=2), turned[:].rearrange("p u e -> p e u")
+            )
+            return grouped
+
+        def finish(e, b, w_mx, v_grouped):
+            v_mx = quantise(f"v{e}{b}", v_grouped, P)
+            y = psum_y.tile([P, 2, P], F32, name="y")
+            for h in range(2):
+                product(y[:, h, :], w_mx, slice(h * P, (h + 1) * P), v_mx, slice(0, P))
+            result = keep.tile([P, 2, P], F32, name=f"result{e}{b}")
+            nc.scalar.activation(result[:], y[:], COPY, scale=1.0 / 16.0)
+            nc.sync.dma_start(out=out[b].rearrange("(h p) e -> p h e", p=P)[:, :, e * P : (e + 1) * P], in_=result[:])
+
+        w0 = weights(0)
+        v00 = values(0, 0)
+        w_mx0 = quantise("w0", w0, NQ)
+        v01 = values(0, 1)
+        w1 = weights(1)
+        finish(0, 0, w_mx0, v00)
+        w_mx1 = quantise("w1", w1, NQ)
+        v10 = values(1, 0)
+        finish(0, 1, w_mx1, v01)
+        v11 = values(1, 1)
+        finish(1, 0, w_mx0, v10)
+        finish(1, 1, w_mx1, v11)

@@ -55,7 +55,7 @@ def tile_attend_sigmoid_kernel(tc, qT, kT, vT, vs, kb, offs, out):
         v_rows = vT.rearrange("(e p) n -> e p n", p=P)
         v_win = []
         for e in range(2):
-            win = keep.tile([P, T], F32, name=f"v_win{e}")
+            win = keep.tile([P, T], F32, name=f"v_win{e}", align_bytes=64)
             nc.sync.dma_start(out=win[:], in_=v_rows[e])
             v_win.append(win)
 
@@ -88,8 +88,10 @@ def tile_attend_sigmoid_kernel(tc, qT, kT, vT, vs, kb, offs, out):
         for j in range(PACK - 1):
             nc.vector.tensor_copy(pairs[j // 2][:, :, j % 2], k_win[j][:].indirect(lists[:]))
 
-        def interleave_keys(b):
+        for b in range(B):
             nc.vector.tensor_copy(pairs[1][:, b * N : (b + 1) * N, 1], k_win[PACK - 1][:].indirect(part[b]))
+
+        def interleave_keys(b):
             grouped = keep.tile([P, N * PACK], BF16, name=f"k_grouped{b}", align_bytes=64)
             nc.vector.tensor_copy(
                 grouped[:].bitcast(I32).rearrange("p (t s c) -> p s c t", t=PACK, c=2),
@@ -100,7 +102,7 @@ def tile_attend_sigmoid_kernel(tc, qT, kT, vT, vs, kb, offs, out):
         def quantise(name, grouped, width):
             codes = keep.tile([P, width], U32, name=f"{name}_codes", align_bytes=64)
             scales = keep.tile([P, width], U8, name=f"{name}_scales", align_bytes=64)
-            nc.vector.quantize_mx(out=codes[:].bitcast(FP8X4), scales=scales[:], in_=grouped[:])
+            nc.vector.quantize_mx(out=codes[:].bitcast(FP8X4), scales=scales[:], in_=grouped)
             return codes, scales
 
         def product(target, lhs, lhs_cols, rhs, rhs_cols):
@@ -124,11 +126,11 @@ def tile_attend_sigmoid_kernel(tc, qT, kT, vT, vs, kb, offs, out):
             )
             q_grouped.append(grouped)
 
-        k_grouped = [interleave_keys(b) for b in range(B)]
         p_tiles = []
         for b in range(B):
-            k_mx = quantise(f"k{b}", k_grouped[b], N)
-            q_mx = quantise(f"q{b}", q_grouped[b], NQ)
+            k_grouped = interleave_keys(b)
+            q_mx = quantise(f"q{b}", q_grouped[b][:], NQ)
+            k_mx = quantise(f"k{b}", k_grouped[:], N)
             prob = keep.tile([P, PACK, NQ], F32, name=f"prob{b}")
             for half in range(2):
                 score = psum_s.tile([P, 2, NQ], F32, name="score")
@@ -140,46 +142,53 @@ def tile_attend_sigmoid_kernel(tc, qT, kT, vT, vs, kb, offs, out):
                     nc.scalar.activation(prob[:, t, :], score[:, u, :], SIGMOID, bias=kb_col[:, b, t : t + 1])
             p_tiles.append(prob)
 
-        def weights(b):
-            grouped = keep.tile([P, NQ * PACK], BF16, name=f"w_grouped{b}", align_bytes=64)
+        def weights(b, grouped, first, count):
             nc.vector.tensor_tensor(
-                grouped[:].rearrange("p (c i t) -> p c t i", i=4, t=PACK),
-                p_tiles[b][:].rearrange("p t (c i) -> p c t i", i=4),
-                vs_col[:, b, :].unsqueeze(1).unsqueeze(3).to_broadcast([P, NQ // 4, PACK, 4]),
+                grouped[:, first * PACK : (first + count) * PACK].rearrange("p (c i t) -> p c t i", i=4, t=PACK),
+                p_tiles[b][:, :, first : first + count].rearrange("p t (c i) -> p c t i", i=4),
+                vs_col[:, b, :].unsqueeze(1).unsqueeze(3).to_broadcast([P, count // 4, PACK, 4]),
                 MULT,
             )
-            return grouped
 
-        def values(e, b):
-            got = keep.tile([P, N], BF16, name=f"v_got{e}{b}", align_bytes=64)
-            nc.vector.tensor_copy(got[:], v_win[e][:].indirect(part[b]))
-            turned = psum_t.tile([P, 2, P], F32, name="turned")
-            for u in range(2):
-                nc.tensor.transpose(turned[:, u, :], got[:].bitcast(F32)[:, u::2], ident[:])
-            grouped = keep.tile([P, P * PACK], BF16, name=f"v_grouped{e}{b}", align_bytes=64)
+        def values(name, e, offsets, groups):
+            got = keep.tile([P, groups * N], BF16, name=f"v_got{name}", align_bytes=64)
+            nc.vector.tensor_copy(got[:], v_win[e][:].indirect(offsets))
+            turned = psum_t.tile([P, groups, 2, P], F32, name="turned")
+            for g in range(groups):
+                for u in range(2):
+                    nc.tensor.transpose(
+                        turned[:, g, u, :], got[:].bitcast(F32)[:, g * N // 2 + u : (g + 1) * N // 2 : 2], ident[:]
+                    )
+            grouped = keep.tile([P, groups * P * PACK], BF16, name=f"v_grouped{name}", align_bytes=64)
             nc.scalar.copy(
-                grouped[:].bitcast(F32).rearrange("p (e u) -> p e u", u=2), turned[:].rearrange("p u e -> p e u")
+                grouped[:].bitcast(F32).rearrange("p (g e u) -> p g e u", g=groups, u=2),
+                turned[:].rearrange("p g u e -> p g e u"),
             )
             return grouped
 
-        def finish(e, b, w_mx, v_grouped):
-            v_mx = quantise(f"v{e}{b}", v_grouped, P)
-            y = psum_y.tile([P, 2, P], F32, name="y")
-            for h in range(2):
-                product(y[:, h, :], w_mx, slice(h * P, (h + 1) * P), v_mx, slice(0, P))
-            result = keep.tile([P, 2, P], F32, name=f"result{e}{b}")
+        def finish(b, h, w_mx, w_cols, v_high):
+            y = psum_y.tile([P, DV], F32, name="y")
+            product(y[:, :P], w_mx, w_cols, v_low, slice(b * P, (b + 1) * P))
+            product(y[:, P:], w_mx, w_cols, v_high, slice(0, P))
+            result = keep.tile([P, DV], F32, name=f"result{b}{h}")
             nc.scalar.activation(result[:], y[:], COPY, scale=1.0 / 16.0)
-            nc.sync.dma_start(out=out[b].rearrange("(h p) e -> p h e", p=P)[:, :, e * P : (e + 1) * P], in_=result[:])
+            nc.sync.dma_start(out=out[b, h * P : (h + 1) * P, :], in_=result[:])
 
-        w0 = weights(0)
-        v00 = values(0, 0)
-        w_mx0 = quantise("w0", w0, NQ)
-        v01 = values(0, 1)
-        w1 = weights(1)
-        finish(0, 0, w_mx0, v00)
-        w_mx1 = quantise("w1", w1, NQ)
-        v10 = values(1, 0)
-        finish(0, 1, w_mx1, v01)
-        v11 = values(1, 1)
-        finish(1, 0, w_mx0, v10)
-        finish(1, 1, w_mx1, v11)
+        v0 = values("0", 0, lists[:], B)
+        w0 = keep.tile([P, NQ * PACK], BF16, name="v_win0", align_bytes=64)
+        weights(0, w0, 0, NQ)
+        v10 = values("10", 1, part[0], 1)
+        w_mx0 = quantise("w0", w0[:], NQ)
+        v11 = values("11", 1, part[1], 1)
+        v_low = quantise("v0", v0[:], B * P)
+        w1 = keep.tile([P, NQ * PACK], BF16, name="v_win1", align_bytes=64)
+        weights(1, w1, 0, P)
+        v_mx10 = quantise("v10", v10[:], P)
+        for h in range(2):
+            finish(0, h, w_mx0, slice(h * P, (h + 1) * P), v_mx10)
+        w_mx10 = quantise("w10", w1[:, : P * PACK], P)
+        weights(1, w1, P, P)
+        v_mx11 = quantise("v11", v11[:], P)
+        finish(1, 0, w_mx10, slice(0, P), v_mx11)
+        w_mx11 = quantise("w11", w1[:, P * PACK :], P)
+        finish(1, 1, w_mx11, slice(0, P), v_mx11)

@@ -92,7 +92,7 @@ def tile_attend_sigmoid_kernel(tc, qT, kT, vT, vs, kb, offs, out):
             nc.vector.tensor_copy(pairs[1][:, b * N : (b + 1) * N, 1], k_win[PACK - 1][:].indirect(part[b]))
 
         def interleave_keys(b):
-            grouped = keep.tile([P, N * PACK], BF16, name=f"k_grouped{b}", align_bytes=64)
+            grouped = keep.tile([P, N * PACK], BF16, name=("k_grouped0", "q_grouped0")[b], align_bytes=64)
             nc.vector.tensor_copy(
                 grouped[:].bitcast(I32).rearrange("p (t s c) -> p s c t", t=PACK, c=2),
                 words.rearrange("p (c b s t) -> p b s c t", c=2, b=B, t=PACK)[:, b],

@@ -27,9 +27,9 @@ def tile_attend_sigmoid_kernel(tc, qT, kT, vT, vs, kb, offs, out):
     nc = tc.nc
     with ExitStack() as ctx:
         keep = ctx.enter_context(tc.tile_pool(name="keep", bufs=1))
-        psum_s = ctx.enter_context(tc.psum_pool(name="psum_s", bufs=4))
+        psum_s = ctx.enter_context(tc.psum_pool(name="psum_s", bufs=3))
         psum_t = ctx.enter_context(tc.psum_pool(name="psum_t", bufs=2))
-        psum_y = ctx.enter_context(tc.psum_pool(name="psum_y", bufs=2))
+        psum_y = ctx.enter_context(tc.psum_pool(name="psum_y", bufs=3))
 
         lists = keep.tile([P, B * COLS], U16, name="lists")
         nc.sync.dma_start(lists[:], offs)
@@ -99,8 +99,8 @@ def tile_attend_sigmoid_kernel(tc, qT, kT, vT, vs, kb, offs, out):
             )
             return grouped
 
-        def quantise(name, grouped, width):
-            codes = keep.tile([P, width], U32, name=f"{name}_codes", align_bytes=64)
+        def quantise(name, grouped, width, slot=None):
+            codes = keep.tile([P, width], U32, name=slot or f"{name}_codes", align_bytes=64)
             scales = keep.tile([P, width], U8, name=f"{name}_scales", align_bytes=64)
             nc.vector.quantize_mx(out=codes[:].bitcast(FP8X4), scales=scales[:], in_=grouped)
             return codes, scales
@@ -142,13 +142,15 @@ def tile_attend_sigmoid_kernel(tc, qT, kT, vT, vs, kb, offs, out):
                     nc.scalar.activation(prob[:, t, :], score[:, u, :], SIGMOID, bias=kb_col[:, b, t : t + 1])
             p_tiles.append(prob)
 
-        def weights(b, grouped, first, count):
+        def weights(b, slot, first, count):
+            grouped = keep.tile([P, count * PACK], BF16, name=slot, align_bytes=64)
             nc.vector.tensor_tensor(
-                grouped[:, first * PACK : (first + count) * PACK].rearrange("p (c i t) -> p c t i", i=4, t=PACK),
+                grouped[:].rearrange("p (c i t) -> p c t i", i=4, t=PACK),
                 p_tiles[b][:, :, first : first + count].rearrange("p t (c i) -> p c t i", i=4),
                 vs_col[:, b, :].unsqueeze(1).unsqueeze(3).to_broadcast([P, count // 4, PACK, 4]),
                 MULT,
             )
+            return grouped
 
         def values(name, e, offsets, groups):
             got = keep.tile([P, groups * N], BF16, name=f"v_got{name}", align_bytes=64)
@@ -175,20 +177,18 @@ def tile_attend_sigmoid_kernel(tc, qT, kT, vT, vs, kb, offs, out):
             nc.sync.dma_start(out=out[b, h * P : (h + 1) * P, :], in_=result[:])
 
         v0 = values("0", 0, lists[:], B)
-        w0 = keep.tile([P, NQ * PACK], BF16, name="v_win0", align_bytes=64)
-        weights(0, w0, 0, NQ)
+        w0 = weights(0, "v_win0", 0, NQ)
         v10 = values("10", 1, part[0], 1)
-        w_mx0 = quantise("w0", w0[:], NQ)
         v11 = values("11", 1, part[1], 1)
+        w_mx0 = quantise("w0", w0[:], NQ, "v_win1")
         v_low = quantise("v0", v0[:], B * P)
-        w1 = keep.tile([P, NQ * PACK], BF16, name="v_win1", align_bytes=64)
-        weights(1, w1, 0, P)
         v_mx10 = quantise("v10", v10[:], P)
         for h in range(2):
             finish(0, h, w_mx0, slice(h * P, (h + 1) * P), v_mx10)
-        w_mx10 = quantise("w10", w1[:, : P * PACK], P)
-        weights(1, w1, P, P)
+        w10 = weights(1, "v_grouped10", 0, P)
         v_mx11 = quantise("v11", v11[:], P)
+        w_mx10 = quantise("w10", w10[:], P)
         finish(1, 0, w_mx10, slice(0, P), v_mx11)
-        w_mx11 = quantise("w11", w1[:, P * PACK :], P)
+        w11 = weights(1, "v_grouped11", P, P)
+        w_mx11 = quantise("w11", w11[:], P)
         finish(1, 1, w_mx11, slice(0, P), v_mx11)

@@ -49,7 +49,7 @@ def tile_attend_sigmoid_kernel(tc, qT, kT, vT, vs, kb, offs, out):
         q_rows = qT.rearrange("b (p j) q -> b p j q", j=PACK)
         q_raw = []
         for b in range(B):
-            raw = keep.tile([P, PACK, NQ], F32, name=f"q_raw{b}")
+            raw = keep.tile([P, PACK, NQ], F32, name=f"q_raw{b}", align_bytes=64)
             nc.sync.dma_start(out=raw[:], in_=q_rows[b])
             q_raw.append(raw)
         v_rows = vT.rearrange("(e p) n -> e p n", p=P)
@@ -130,7 +130,7 @@ def tile_attend_sigmoid_kernel(tc, qT, kT, vT, vs, kb, offs, out):
         for b in range(B):
             k_grouped = interleave_keys(b)
             q_mx = quantise(f"q{b}", q_grouped[b][:], NQ)
-            k_mx = quantise(f"k{b}", k_grouped[:], N)
+            k_mx = quantise(f"k{b}", k_grouped[:], N, f"q_raw{b}")
             prob = keep.tile([P, PACK, NQ], F32, name=f"prob{b}")
             for half in range(2):
                 score = psum_s.tile([P, 2, NQ], F32, name="score")
@@ -152,21 +152,15 @@ def tile_attend_sigmoid_kernel(tc, qT, kT, vT, vs, kb, offs, out):
             )
             return grouped
 
-        def values(name, e, offsets, groups):
-            got = keep.tile([P, groups * N], BF16, name=f"v_got{name}", align_bytes=64)
-            nc.vector.tensor_copy(got[:], v_win[e][:].indirect(offsets))
-            turned = psum_t.tile([P, groups, 2, P], F32, name="turned")
-            for g in range(groups):
-                for u in range(2):
-                    nc.tensor.transpose(
-                        turned[:, g, u, :], got[:].bitcast(F32)[:, g * N // 2 + u : (g + 1) * N // 2 : 2], ident[:]
-                    )
-            grouped = keep.tile([P, groups * P * PACK], BF16, name=f"v_grouped{name}", align_bytes=64)
+        def values(e, b, grouped):
+            got = keep.tile([P, N], BF16, name=f"v_got{e}{b}", align_bytes=64)
+            nc.vector.tensor_copy(got[:], v_win[e][:].indirect(part[b]))
+            turned = psum_t.tile([P, 2, P], F32, name="turned")
+            for u in range(2):
+                nc.tensor.transpose(turned[:, u, :], got[:].bitcast(F32)[:, u::2], ident[:])
             nc.scalar.copy(
-                grouped[:].bitcast(F32).rearrange("p (g e u) -> p g e u", g=groups, u=2),
-                turned[:].rearrange("p g u e -> p g e u"),
+                grouped.bitcast(F32).rearrange("p (e u) -> p e u", u=2), turned[:].rearrange("p u e -> p e u")
             )
-            return grouped
 
         def finish(b, h, w_mx, w_cols, v_high):
             y = psum_y.tile([P, DV], F32, name="y")
@@ -176,19 +170,23 @@ def tile_attend_sigmoid_kernel(tc, qT, kT, vT, vs, kb, offs, out):
             nc.scalar.activation(result[:], y[:], COPY, scale=1.0 / 16.0)
             nc.sync.dma_start(out=out[b, h * P : (h + 1) * P, :], in_=result[:])
 
-        v0 = values("0", 0, lists[:], B)
-        w0 = weights(0, "v_win0", 0, NQ)
-        v10 = values("10", 1, part[0], 1)
-        v11 = values("11", 1, part[1], 1)
-        w_mx0 = quantise("w0", w0[:], NQ, "v_win1")
+        v0 = keep.tile([P, B * P * PACK], BF16, name="v_grouped0", align_bytes=64)
+        v10 = keep.tile([P, P * PACK], BF16, name="v_grouped10", align_bytes=64)
+        v11 = keep.tile([P, P * PACK], BF16, name="v_grouped11", align_bytes=64)
+        for b in range(B):
+            values(0, b, v0[:, b * P * PACK : (b + 1) * P * PACK])
+        w0 = weights(0, "v_got00", 0, NQ)
         v_low = quantise("v0", v0[:], B * P)
+        w_mx0 = quantise("w0", w0[:], NQ)
+        values(1, 0, v10[:])
+        values(1, 1, v11[:])
+        w10 = weights(1, "v_got10", 0, P)
         v_mx10 = quantise("v10", v10[:], P)
         for h in range(2):
             finish(0, h, w_mx0, slice(h * P, (h + 1) * P), v_mx10)
-        w10 = weights(1, "v_grouped10", 0, P)
-        v_mx11 = quantise("v11", v11[:], P)
+        w11 = weights(1, "v_got11", P, P)
         w_mx10 = quantise("w10", w10[:], P)
+        v_mx11 = quantise("v11", v11[:], P)
         finish(1, 0, w_mx10, slice(0, P), v_mx11)
-        w11 = weights(1, "v_grouped11", P, P)
         w_mx11 = quantise("w11", w11[:], P)
         finish(1, 1, w_mx11, slice(0, P), v_mx11)

@@ -142,15 +142,13 @@ def tile_attend_sigmoid_kernel(tc, qT, kT, vT, vs, kb, offs, out):
                     nc.scalar.activation(prob[:, t, :], score[:, u, :], SIGMOID, bias=kb_col[:, b, t : t + 1])
             p_tiles.append(prob)
 
-        def weights(b, slot, first, count):
-            grouped = keep.tile([P, count * PACK], BF16, name=slot, align_bytes=64)
-            nc.vector.tensor_tensor(
-                grouped[:].rearrange("p (c i t) -> p c t i", i=4, t=PACK),
+        def weights(engine, b, grouped, first, count):
+            engine.tensor_tensor(
+                grouped.rearrange("p (c i t) -> p c t i", i=4, t=PACK),
                 p_tiles[b][:, :, first : first + count].rearrange("p t (c i) -> p c t i", i=4),
                 vs_col[:, b, :].unsqueeze(1).unsqueeze(3).to_broadcast([P, count // 4, PACK, 4]),
                 MULT,
             )
-            return grouped
 
         def values(e, b, grouped):
             got = keep.tile([P, N], BF16, name=f"v_got{e}{b}", align_bytes=64)
@@ -164,29 +162,29 @@ def tile_attend_sigmoid_kernel(tc, qT, kT, vT, vs, kb, offs, out):
 
         def finish(b, h, w_mx, w_cols, v_high):
             y = psum_y.tile([P, DV], F32, name="y")
-            product(y[:, :P], w_mx, w_cols, v_low, slice(b * P, (b + 1) * P))
+            product(y[:, :P], w_mx, w_cols, early_mx, slice(NQ + b * P, NQ + (b + 1) * P))
             product(y[:, P:], w_mx, w_cols, v_high, slice(0, P))
             result = keep.tile([P, DV], F32, name=f"result{b}{h}")
             nc.scalar.activation(result[:], y[:], COPY, scale=1.0 / 16.0)
             nc.sync.dma_start(out=out[b, h * P : (h + 1) * P, :], in_=result[:])
 
-        v0 = keep.tile([P, B * P * PACK], BF16, name="v_grouped0", align_bytes=64)
+        early = keep.tile([P, (NQ + B * P) * PACK], BF16, name="early", align_bytes=64)
         v10 = keep.tile([P, P * PACK], BF16, name="v_grouped10", align_bytes=64)
         v11 = keep.tile([P, P * PACK], BF16, name="v_grouped11", align_bytes=64)
+        weights(nc.gpsimd, 0, early[:, : NQ * PACK], 0, NQ)
         for b in range(B):
-            values(0, b, v0[:, b * P * PACK : (b + 1) * P * PACK])
-        w0 = weights(0, "v_got00", 0, NQ)
-        v_low = quantise("v0", v0[:], B * P)
-        w_mx0 = quantise("w0", w0[:], NQ)
+            values(0, b, early[:, (NQ + b * P) * PACK : (NQ + (b + 1) * P) * PACK])
         values(1, 0, v10[:])
         values(1, 1, v11[:])
-        w10 = weights(1, "v_got10", 0, P)
+        early_mx = quantise("early", early[:], NQ + B * P, "v_got10")
+        w1 = keep.tile([P, NQ * PACK], BF16, name="v_got11", align_bytes=64)
+        weights(nc.vector, 1, w1[:, : P * PACK], 0, P)
         v_mx10 = quantise("v10", v10[:], P)
         for h in range(2):
-            finish(0, h, w_mx0, slice(h * P, (h + 1) * P), v_mx10)
-        w11 = weights(1, "v_got11", P, P)
-        w_mx10 = quantise("w10", w10[:], P)
+            finish(0, h, early_mx, slice(h * P, (h + 1) * P), v_mx10)
+        weights(nc.vector, 1, w1[:, P * PACK :], P, P)
+        w_mx10 = quantise("w10", w1[:, : P * PACK], P)
         v_mx11 = quantise("v11", v11[:], P)
         finish(1, 0, w_mx10, slice(0, P), v_mx11)
-        w_mx11 = quantise("w11", w11[:], P)
+        w_mx11 = quantise("w11", w1[:, P * PACK :], P)
         finish(1, 1, w_mx11, slice(0, P), v_mx11)

@@ -27,9 +27,9 @@ def tile_attend_sigmoid_kernel(tc, qT, kT, vT, vs, kb, offs, out):
     nc = tc.nc
     with ExitStack() as ctx:
         keep = ctx.enter_context(tc.tile_pool(name="keep", bufs=1))
-        psum_s = ctx.enter_context(tc.psum_pool(name="psum_s", bufs=3))
+        psum_s = ctx.enter_context(tc.psum_pool(name="psum_s", bufs=4))
         psum_t = ctx.enter_context(tc.psum_pool(name="psum_t", bufs=2))
-        psum_y = ctx.enter_context(tc.psum_pool(name="psum_y", bufs=3))
+        psum_y = ctx.enter_context(tc.psum_pool(name="psum_y", bufs=2))
 
         lists = keep.tile([P, B * COLS], U16, name="lists")
         nc.sync.dma_start(lists[:], offs)
@@ -130,16 +130,23 @@ def tile_attend_sigmoid_kernel(tc, qT, kT, vT, vs, kb, offs, out):
         for b in range(B):
             k_grouped = interleave_keys(b)
             q_mx = quantise(f"q{b}", q_grouped[b][:], NQ)
-            k_mx = quantise(f"k{b}", k_grouped[:], N, f"q_raw{b}")
             prob = keep.tile([P, PACK, NQ], F32, name=f"prob{b}")
+            k_mx = (
+                keep.tile([P, N], U32, name=f"q_raw{b}", align_bytes=64),
+                keep.tile([P, N], U8, name=f"k_scales{b}", align_bytes=64),
+            )
             for half in range(2):
-                score = psum_s.tile([P, 2, NQ], F32, name="score")
+                cols = slice(half * N // 2, (half + 1) * N // 2)
+                nc.vector.quantize_mx(
+                    out=k_mx[0][:, cols].bitcast(FP8X4),
+                    scales=k_mx[1][:, cols],
+                    in_=k_grouped[:, half * 2 * N : (half + 1) * 2 * N],
+                )
                 for u in range(2):
                     t = 2 * half + u
-                    product(score[:, u, :], k_mx, slice(t * P, (t + 1) * P), q_mx, slice(0, NQ))
-                for u in range(2):
-                    t = 2 * half + u
-                    nc.scalar.activation(prob[:, t, :], score[:, u, :], SIGMOID, bias=kb_col[:, b, t : t + 1])
+                    score = psum_s.tile([P, NQ], F32, name="score")
+                    product(score[:], k_mx, slice(t * P, (t + 1) * P), q_mx, slice(0, NQ))
+                    nc.scalar.activation(prob[:, t, :], score[:], SIGMOID, bias=kb_col[:, b, t : t + 1])
             p_tiles.append(prob)
 
         def weights(engine, b, grouped, first, count):

@@ -28,8 +28,7 @@ def tile_attend_sigmoid_kernel(tc, qT, kT, vT, vs, kb, offs, out):
     with ExitStack() as ctx:
         keep = ctx.enter_context(tc.tile_pool(name="keep", bufs=1))
         psum_s = ctx.enter_context(tc.psum_pool(name="psum_s", bufs=4))
-        psum_t = ctx.enter_context(tc.psum_pool(name="psum_t", bufs=2))
-        psum_y = ctx.enter_context(tc.psum_pool(name="psum_y", bufs=2))
+        psum_t = ctx.enter_context(tc.psum_pool(name="psum_t", bufs=4))
 
         lists = keep.tile([P, B * COLS], U16, name="lists")
         nc.sync.dma_start(lists[:], offs)
@@ -168,14 +167,14 @@ def tile_attend_sigmoid_kernel(tc, qT, kT, vT, vs, kb, offs, out):
             )
 
         def finish(b, h, w_mx, w_cols, v_high):
-            y = psum_y.tile([P, DV], F32, name="y")
+            y = psum_s.tile([P, DV], F32, name="score")
             product(y[:, :P], w_mx, w_cols, early_mx, slice(NQ + b * P, NQ + (b + 1) * P))
             product(y[:, P:], w_mx, w_cols, v_high, slice(0, P))
             result = keep.tile([P, DV], F32, name=f"result{b}{h}")
             nc.scalar.activation(result[:], y[:], COPY, scale=1.0 / 16.0)
             nc.sync.dma_start(out=out[b, h * P : (h + 1) * P, :], in_=result[:])
 
-        early = keep.tile([P, (NQ + B * P) * PACK], BF16, name="early", align_bytes=64)
+        early = keep.tile([P, (NQ + B * P) * PACK], BF16, name="q_grouped0", align_bytes=64)
         v10 = keep.tile([P, P * PACK], BF16, name="v_grouped10", align_bytes=64)
         v11 = keep.tile([P, P * PACK], BF16, name="v_grouped11", align_bytes=64)
         weights(nc.gpsimd, 0, early[:, : NQ * PACK], 0, NQ)

@@ -166,31 +166,43 @@ def tile_attend_sigmoid_kernel(tc, qT, kT, vT, vs, kb, offs, out):
                 grouped.bitcast(F32).rearrange("p (e u) -> p e u", u=2), turned[:].rearrange("p u e -> p e u")
             )
 
-        def finish(b, h, w_mx, w_cols, v_high):
+        def finish(b, h, products):
             y = psum_s.tile([P, DV], F32, name="score")
-            product(y[:, :P], w_mx, w_cols, early_mx, slice(NQ + b * P, NQ + (b + 1) * P))
-            product(y[:, P:], w_mx, w_cols, v_high, slice(0, P))
+            for cols, lhs, lhs_cols, rhs, rhs_cols in products:
+                product(y[:, cols], lhs, lhs_cols, rhs, rhs_cols)
             result = keep.tile([P, DV], F32, name=f"result{b}{h}")
-            nc.scalar.activation(result[:], y[:], COPY, scale=1.0 / 16.0)
+            if b + h == 2:
+                nc.vector.tensor_scalar_mul(result[:], y[:], 1.0 / 16.0)
+            else:
+                nc.scalar.activation(result[:], y[:], COPY, scale=1.0 / 16.0)
             nc.sync.dma_start(out=out[b, h * P : (h + 1) * P, :], in_=result[:])
 
-        early = keep.tile([P, (NQ + B * P) * PACK], BF16, name="q_grouped0", align_bytes=64)
-        v10 = keep.tile([P, P * PACK], BF16, name="v_grouped10", align_bytes=64)
-        v11 = keep.tile([P, P * PACK], BF16, name="v_grouped11", align_bytes=64)
-        weights(nc.gpsimd, 0, early[:, : NQ * PACK], 0, NQ)
+        def quantise_into(mx, cols, grouped):
+            nc.vector.quantize_mx(out=mx[0][:, cols].bitcast(FP8X4), scales=mx[1][:, cols], in_=grouped)
+
+        W = P * PACK
+        early = keep.tile([P, 4 * W], BF16, name="q_grouped0", align_bytes=64)
+        v10 = keep.tile([P, W], BF16, name="v_grouped10", align_bytes=64)
+        v11 = keep.tile([P, W], BF16, name="v_grouped11", align_bytes=64)
+        weights(nc.gpsimd, 0, early[:, : 2 * W], 0, NQ)
         for b in range(B):
-            values(0, b, early[:, (NQ + b * P) * PACK : (NQ + (b + 1) * P) * PACK])
+            values(0, b, early[:, (2 + b) * W : (3 + b) * W])
         values(1, 0, v10[:])
         values(1, 1, v11[:])
-        early_mx = quantise("early", early[:], NQ + B * P, "v_got10")
+        mx = (
+            keep.tile([P, 5 * P], U32, name="v_got10", align_bytes=64),
+            keep.tile([P, 5 * P], U8, name="late_scales", align_bytes=64),
+        )
+        quantise_into(mx, slice(0, 4 * P), early[:])
         w1 = keep.tile([P, NQ * PACK], BF16, name="v_got11", align_bytes=64)
-        weights(nc.vector, 1, w1[:, : P * PACK], 0, P)
+        weights(nc.vector, 1, w1[:, :W], 0, P)
         v_mx10 = quantise("v10", v10[:], P)
         for h in range(2):
-            finish(0, h, early_mx, slice(h * P, (h + 1) * P), v_mx10)
-        weights(nc.vector, 1, w1[:, P * PACK :], P, P)
-        w_mx10 = quantise("w10", w1[:, : P * PACK], P)
-        v_mx11 = quantise("v11", v11[:], P)
-        finish(1, 0, w_mx10, slice(0, P), v_mx11)
-        w_mx11 = quantise("w11", w1[:, P * PACK :], P)
-        finish(1, 1, w_mx11, slice(0, P), v_mx11)
+            rows = slice(h * P, (h + 1) * P)
+            finish(0, h, [(slice(0, P), mx, rows, mx, slice(2 * P, 3 * P)), (slice(P, DV), mx, rows, v_mx10, slice(0, P))])
+        weights(nc.vector, 1, w1[:, W:], P, P)
+        w_mx10 = quantise("w10", w1[:, :W], P)
+        quantise_into(mx, slice(4 * P, 5 * P), v11[:])
+        finish(1, 0, [(slice(0, DV), w_mx10, slice(0, P), mx, slice(3 * P, 5 * P))])
+        w_mx11 = quantise("w11", w1[:, W:], P)
+        finish(1, 1, [(slice(0, DV), w_mx11, slice(0, P), mx, slice(3 * P, 5 * P))])

@@ -181,28 +181,21 @@ def tile_attend_sigmoid_kernel(tc, qT, kT, vT, vs, kb, offs, out):
             nc.vector.quantize_mx(out=mx[0][:, cols].bitcast(FP8X4), scales=mx[1][:, cols], in_=grouped)
 
         W = P * PACK
-        early = keep.tile([P, 4 * W], BF16, name="q_grouped0", align_bytes=64)
-        v10 = keep.tile([P, W], BF16, name="v_grouped10", align_bytes=64)
-        v11 = keep.tile([P, W], BF16, name="v_grouped11", align_bytes=64)
-        weights(nc.gpsimd, 0, early[:, : 2 * W], 0, NQ)
-        for b in range(B):
-            values(0, b, early[:, (2 + b) * W : (3 + b) * W])
-        values(1, 0, v10[:])
-        values(1, 1, v11[:])
-        mx = (
-            keep.tile([P, 5 * P], U32, name="v_got10", align_bytes=64),
-            keep.tile([P, 5 * P], U8, name="late_scales", align_bytes=64),
-        )
-        quantise_into(mx, slice(0, 4 * P), early[:])
-        w1 = keep.tile([P, NQ * PACK], BF16, name="v_got11", align_bytes=64)
-        weights(nc.vector, 1, w1[:, :W], 0, P)
-        v_mx10 = quantise("v10", v10[:], P)
+        first = keep.tile([P, 4 * W], BF16, name="q_grouped0", align_bytes=64)
+        second = keep.tile([P, 2 * W], BF16, name="second", align_bytes=64)
+        weights(nc.gpsimd, 0, first[:, : 2 * W], 0, NQ)
+        for e in range(2):
+            values(e, 0, first[:, (2 + e) * W : (3 + e) * W])
+            values(e, 1, second[:, e * W : (e + 1) * W])
+        w10 = keep.tile([P, W], BF16, name="v_got10", align_bytes=64)
+        weights(nc.vector, 1, w10[:], 0, P)
+        first_mx = quantise("first", first[:], 4 * P)
         for h in range(2):
-            rows = slice(h * P, (h + 1) * P)
-            finish(0, h, [(slice(0, P), mx, rows, mx, slice(2 * P, 3 * P)), (slice(P, DV), mx, rows, v_mx10, slice(0, P))])
-        weights(nc.vector, 1, w1[:, W:], P, P)
-        w_mx10 = quantise("w10", w1[:, :W], P)
-        quantise_into(mx, slice(4 * P, 5 * P), v11[:])
-        finish(1, 0, [(slice(0, DV), w_mx10, slice(0, P), mx, slice(3 * P, 5 * P))])
-        w_mx11 = quantise("w11", w1[:, W:], P)
-        finish(1, 1, [(slice(0, DV), w_mx11, slice(0, P), mx, slice(3 * P, 5 * P))])
+            finish(0, h, [(slice(0, DV), first_mx, slice(h * P, (h + 1) * P), first_mx, slice(2 * P, 4 * P))])
+        w11 = keep.tile([P, W], BF16, name="v_got11", align_bytes=64)
+        weights(nc.vector, 1, w11[:], P, P)
+        w_mx10 = quantise("w10", w10[:], P, "v_win1")
+        second_mx = quantise("second", second[:], 2 * P)
+        finish(1, 0, [(slice(0, DV), w_mx10, slice(0, P), second_mx, slice(0, 2 * P))])
+        w_mx11 = quantise("w11", w11[:], P)
+        finish(1, 1, [(slice(0, DV), w_mx11, slice(0, P), second_mx, slice(0, 2 * P))])

@@ -64,7 +64,7 @@ def tile_attend_sigmoid_kernel(tc, qT, kT, vT, vs, kb, offs, out):
         nc.scalar.activation(warmed[:], warm[:], SIGMOID)
 
         nc.vector.memset(kb_win[:ROW, :], 0.0)
-        nc.vector.memset(vs_win[:ROW, :], 0.0)
+        nc.gpsimd.memset(vs_win[:ROW, :], 0.0)
         ident = keep.tile([P, P], F32, name="ident")
         make_identity(nc, ident[:])
 

@@ -21,6 +21,7 @@ COPY = mybir.ActivationFunctionType.Copy
 SIGMOID = mybir.ActivationFunctionType.Sigmoid
 MULT = mybir.AluOpType.mult
 ROW = P - 1
+HEAD = 512
 
 
 def tile_attend_sigmoid_kernel(tc, qT, kT, vT, vs, kb, offs, out):
@@ -31,7 +32,6 @@ def tile_attend_sigmoid_kernel(tc, qT, kT, vT, vs, kb, offs, out):
         psum_t = ctx.enter_context(tc.psum_pool(name="psum_t", bufs=4))
 
         lists = keep.tile([P, B * COLS], U16, name="lists")
-        nc.sync.dma_start(lists[:], offs)
         part = [lists[:, b * COLS : (b + 1) * COLS] for b in range(B)]
 
         kb_win = keep.tile([P, T], F32, name="kb_win")
@@ -43,7 +43,12 @@ def tile_attend_sigmoid_kernel(tc, qT, kT, vT, vs, kb, offs, out):
         k_win = []
         for j in range(PACK):
             win = keep.tile([P, T], F32, name=f"k_win{j}")
-            nc.sync.dma_start(out=win[:], in_=k_rows[j])
+            if j == 0:
+                nc.sync.dma_start(out=win[:, :HEAD], in_=k_rows[j][:, :HEAD])
+                nc.sync.dma_start(lists[:], offs)
+                nc.sync.dma_start(out=win[:, HEAD:], in_=k_rows[j][:, HEAD:])
+            else:
+                nc.sync.dma_start(out=win[:], in_=k_rows[j])
             k_win.append(win)
         q_rows = qT.rearrange("b (p j) q -> b p j q", j=PACK)
         q_raw = []

@@ -29,7 +29,8 @@ def tile_attend_sigmoid_kernel(tc, qT, kT, vT, vs, kb, offs, out):
     with ExitStack() as ctx:
         keep = ctx.enter_context(tc.tile_pool(name="keep", bufs=1))
         psum_s = ctx.enter_context(tc.psum_pool(name="psum_s", bufs=4))
-        psum_t = ctx.enter_context(tc.psum_pool(name="psum_t", bufs=4))
+        psum_t = ctx.enter_context(tc.psum_pool(name="psum_t", bufs=3))
+        psum_v = ctx.enter_context(tc.psum_pool(name="psum_v", bufs=1))
 
         lists = keep.tile([P, B * COLS], U16, name="lists")
         part = [lists[:, b * COLS : (b + 1) * COLS] for b in range(B)]
@@ -79,12 +80,18 @@ def tile_attend_sigmoid_kernel(tc, qT, kT, vT, vs, kb, offs, out):
             nc.vector.tensor_copy(got[:], win[:].indirect(lists[:]))
             col = keep.tile([P, B, PACK], F32, name=f"{name}_col")
             for b in range(B):
-                turned = psum_s.tile([P, PACK, P], F32, name="score")
+                kept = name == "vs" and b == 1
+                if kept:
+                    turned = psum_v.tile([P, PACK, P], F32, name="vs_turned")
+                else:
+                    turned = psum_s.tile([P, PACK, P], F32, name="score")
                 for t in range(PACK):
                     nc.tensor.transpose(turned[:, t, :], got[:, b * N + t : (b + 1) * N : PACK], ident[:])
-                nc.scalar.copy(col[:, b, :], turned[:, :, ROW])
+                if not kept:
+                    nc.scalar.copy(col[:, b, :], turned[:, :, ROW])
             cols.append(col)
         kb_col, vs_col = cols
+        scale_cols = (vs_col[:, 0, :], turned[:, :, ROW])
 
         both = keep.tile([P, 2 * B * N * 2], BF16, name="k_pairs", align_bytes=64)
         words = both[:].bitcast(I32)
@@ -157,7 +164,7 @@ def tile_attend_sigmoid_kernel(tc, qT, kT, vT, vs, kb, offs, out):
             engine.tensor_tensor(
                 grouped.rearrange("p (c i t) -> p c t i", i=4, t=PACK),
                 p_tiles[b][:, :, first : first + count].rearrange("p t (c i) -> p c t i", i=4),
-                vs_col[:, b, :].unsqueeze(1).unsqueeze(3).to_broadcast([P, count // 4, PACK, 4]),
+                scale_cols[b].unsqueeze(1).unsqueeze(3).to_broadcast([P, count // 4, PACK, 4]),
                 MULT,
             )
 

@@ -170,10 +170,12 @@ def tile_attend_sigmoid_kernel(tc, qT, kT, vT, vs, kb, offs, out):
 
         def values(e, b, grouped):
             got = keep.tile([P, N], BF16, name=f"v_got{e}{b}", align_bytes=64)
-            nc.vector.tensor_copy(got[:], v_win[e][:].indirect(part[b]))
+            nc.vector.tensor_copy(
+                got[:].rearrange("p (u s i) -> p s u i", u=2, i=2), v_win[e][:].indirect(part[b])
+            )
             turned = psum_t.tile([P, 2, P], F32, name="turned")
             for u in range(2):
-                nc.tensor.transpose(turned[:, u, :], got[:].bitcast(F32)[:, u::2], ident[:])
+                nc.tensor.transpose(turned[:, u, :], got[:].bitcast(F32)[:, u * P : (u + 1) * P], ident[:])
             nc.scalar.copy(
                 grouped.bitcast(F32).rearrange("p (e u) -> p e u", u=2), turned[:].rearrange("p u e -> p e u")
             )

@@ -6,9 +6,13 @@ from concourse.masks import make_identity
 B, NQ, D, DV, N, T = 2, 256, 512, 256, 512, 2048
 P = 128
 PACK = 4
-COLS = N // 16
+LIST_COLS = N // 16
+GROUP = P * PACK
+ROW = P - 1
+HEAD = 512
+OUT_SCALE = 1.0 / 16.0
 FLOPS = 2 * B * NQ * N * (D + DV)
-BYTES = 4 * (B * D * NQ + D * T + DV * T + 2 * T + B * NQ * DV) + 2 * P * (B * N // 16)
+BYTES = 4 * (B * D * NQ + D * T + DV * T + 2 * T + B * NQ * DV) + 2 * P * B * LIST_COLS
 
 F32 = mybir.dt.float32
 BF16 = mybir.dt.bfloat16
@@ -20,20 +24,18 @@ FP8X4 = mybir.dt.float8_e4m3fn_x4
 COPY = mybir.ActivationFunctionType.Copy
 SIGMOID = mybir.ActivationFunctionType.Sigmoid
 MULT = mybir.AluOpType.mult
-ROW = P - 1
-HEAD = 512
 
 
 def tile_attend_sigmoid_kernel(tc, qT, kT, vT, vs, kb, offs, out):
     nc = tc.nc
     with ExitStack() as ctx:
         keep = ctx.enter_context(tc.tile_pool(name="keep", bufs=1))
-        psum_s = ctx.enter_context(tc.psum_pool(name="psum_s", bufs=4))
-        psum_t = ctx.enter_context(tc.psum_pool(name="psum_t", bufs=3))
-        psum_v = ctx.enter_context(tc.psum_pool(name="psum_v", bufs=1))
+        product_banks = ctx.enter_context(tc.psum_pool(name="product_banks", bufs=4))
+        value_banks = ctx.enter_context(tc.psum_pool(name="value_banks", bufs=3))
+        scale_bank = ctx.enter_context(tc.psum_pool(name="scale_bank", bufs=1))
 
-        lists = keep.tile([P, B * COLS], U16, name="lists")
-        part = [lists[:, b * COLS : (b + 1) * COLS] for b in range(B)]
+        lists = keep.tile([P, B * LIST_COLS], U16, name="lists")
+        own_list = [lists[:, b * LIST_COLS : (b + 1) * LIST_COLS] for b in range(B)]
 
         kb_win = keep.tile([P, T], F32, name="kb_win")
         vs_win = keep.tile([P, T], F32, name="vs_win")
@@ -41,82 +43,66 @@ def tile_attend_sigmoid_kernel(tc, qT, kT, vT, vs, kb, offs, out):
         nc.scalar.dma_start(out=vs_win[ROW:P, :], in_=vs[0:1, :])
 
         k_rows = kT.rearrange("(p j) n -> j p n", j=PACK)
-        k_win = []
-        for j in range(PACK):
-            win = keep.tile([P, T], F32, name=f"k_win{j}")
-            if j == 0:
-                nc.sync.dma_start(out=win[:, :HEAD], in_=k_rows[j][:, :HEAD])
-                nc.sync.dma_start(lists[:], offs)
-                nc.sync.dma_start(out=win[:, HEAD:], in_=k_rows[j][:, HEAD:])
-            else:
-                nc.sync.dma_start(out=win[:], in_=k_rows[j])
-            k_win.append(win)
+        k_win = [keep.tile([P, T], F32, name=f"k_win{j}") for j in range(PACK)]
+        nc.sync.dma_start(out=k_win[0][:, :HEAD], in_=k_rows[0][:, :HEAD])
+        nc.sync.dma_start(lists[:], offs)
+        nc.sync.dma_start(out=k_win[0][:, HEAD:], in_=k_rows[0][:, HEAD:])
+        for j in range(1, PACK):
+            nc.sync.dma_start(out=k_win[j][:], in_=k_rows[j])
         q_rows = qT.rearrange("b (p j) q -> b p j q", j=PACK)
-        q_raw = []
+        q_raw = [keep.tile([P, PACK, NQ], F32, name=f"q_raw{b}", align_bytes=64) for b in range(B)]
         for b in range(B):
-            raw = keep.tile([P, PACK, NQ], F32, name=f"q_raw{b}", align_bytes=64)
-            nc.sync.dma_start(out=raw[:], in_=q_rows[b])
-            q_raw.append(raw)
-        v_rows = vT.rearrange("(e p) n -> e p n", p=P)
-        v_win = []
-        for e in range(2):
-            win = keep.tile([P, T], F32, name=f"v_win{e}", align_bytes=64)
-            nc.sync.dma_start(out=win[:], in_=v_rows[e])
-            v_win.append(win)
+            nc.sync.dma_start(out=q_raw[b][:], in_=q_rows[b])
+        v_rows = vT.rearrange("(k p) n -> k p n", p=P)
+        v_win = [keep.tile([P, T], F32, name=f"v_win{k}", align_bytes=64) for k in range(DV // P)]
+        for k in range(DV // P):
+            nc.sync.dma_start(out=v_win[k][:], in_=v_rows[k])
 
-        warm = keep.tile([P, 1], F32, name="warm")
-        nc.vector.memset(warm[:], 0.0)
+        zero = keep.tile([P, 1], F32, name="zero")
+        nc.vector.memset(zero[:], 0.0)
         warmed = keep.tile([P, 1], F32, name="warmed")
-        nc.scalar.activation(warmed[:], warm[:], SIGMOID)
+        nc.scalar.activation(warmed[:], zero[:], SIGMOID)
 
         nc.vector.memset(kb_win[:ROW, :], 0.0)
         nc.gpsimd.memset(vs_win[:ROW, :], 0.0)
-        ident = keep.tile([P, P], F32, name="ident")
-        make_identity(nc, ident[:])
+        identity = keep.tile([P, P], F32, name="identity")
+        make_identity(nc, identity[:])
 
-        cols = []
-        for name, win in (("kb", kb_win), ("vs", vs_win)):
-            got = keep.tile([P, B * N], F32, name=f"{name}_got")
-            nc.vector.tensor_copy(got[:], win[:].indirect(lists[:]))
-            col = keep.tile([P, B, PACK], F32, name=f"{name}_col")
-            for b in range(B):
-                kept = name == "vs" and b == 1
-                if kept:
-                    turned = psum_v.tile([P, PACK, P], F32, name="vs_turned")
-                else:
-                    turned = psum_s.tile([P, PACK, P], F32, name="score")
-                for t in range(PACK):
-                    nc.tensor.transpose(turned[:, t, :], got[:, b * N + t : (b + 1) * N : PACK], ident[:])
-                if not kept:
-                    nc.scalar.copy(col[:, b, :], turned[:, :, ROW])
-            cols.append(col)
-        kb_col, vs_col = cols
-        scale_cols = (vs_col[:, 0, :], turned[:, :, ROW])
+        def turn_row(gathered, b, bank):
+            for t in range(PACK):
+                nc.tensor.transpose(bank[:, t, :], gathered[:, b * N + t : (b + 1) * N : PACK], identity[:])
+            return bank[:, :, ROW]
 
-        both = keep.tile([P, 2 * B * N * 2], BF16, name="k_pairs", align_bytes=64)
-        words = both[:].bitcast(I32)
-        pairs = [both[:].rearrange("p (c i e) -> p c i e", c=2, e=2)[:, c] for c in range(2)]
-        for j in range(PACK - 1):
-            nc.vector.tensor_copy(pairs[j // 2][:, :, j % 2], k_win[j][:].indirect(lists[:]))
-
+        kb_got = keep.tile([P, B * N], F32, name="kb_got")
+        nc.vector.tensor_copy(kb_got[:], kb_win[:].indirect(lists[:]))
+        kb_col = keep.tile([P, B, PACK], F32, name="kb_col")
         for b in range(B):
-            nc.vector.tensor_copy(pairs[1][:, b * N : (b + 1) * N, 1], k_win[PACK - 1][:].indirect(part[b]))
+            bank = product_banks.tile([P, PACK, P], F32, name="product")
+            nc.scalar.copy(kb_col[:, b, :], turn_row(kb_got, b, bank))
+        vs_got = keep.tile([P, B * N], F32, name="vs_got")
+        nc.vector.tensor_copy(vs_got[:], vs_win[:].indirect(lists[:]))
+        vs_col0 = keep.tile([P, PACK], F32, name="vs_col0")
+        bank = product_banks.tile([P, PACK, P], F32, name="product")
+        nc.scalar.copy(vs_col0[:], turn_row(vs_got, 0, bank))
+        bank = scale_bank.tile([P, PACK, P], F32, name="vs_turned")
+        vs_col = (vs_col0[:], turn_row(vs_got, 1, bank))
 
-        def interleave_keys(b):
-            grouped = keep.tile([P, N * PACK], BF16, name=("k_grouped0", "q_grouped0")[b], align_bytes=64)
-            nc.vector.tensor_copy(
-                grouped[:].bitcast(I32).rearrange("p (t s c) -> p s c t", t=PACK, c=2),
-                words.rearrange("p (c b s t) -> p b s c t", c=2, b=B, t=PACK)[:, b],
-            )
-            return grouped
+        k_pairs = keep.tile([P, 2 * B * N * 2], BF16, name="k_pairs", align_bytes=64)
+        pair_halves = k_pairs[:].rearrange("p (c i half) -> p c half i", c=2, half=2)
+        for j in range(PACK - 1):
+            nc.vector.tensor_copy(pair_halves[:, j // 2, j % 2], k_win[j][:].indirect(lists[:]))
+        for b in range(B):
+            nc.vector.tensor_copy(pair_halves[:, 1, 1, b * N : (b + 1) * N], k_win[PACK - 1][:].indirect(own_list[b]))
 
-        def quantise(name, grouped, width, slot=None):
-            codes = keep.tile([P, width], U32, name=slot or f"{name}_codes", align_bytes=64)
+        def mx_tiles(name, width, tag=None):
+            codes = keep.tile([P, width], U32, name=f"{name}_codes", tag=tag or f"{name}_codes", align_bytes=64)
             scales = keep.tile([P, width], U8, name=f"{name}_scales", align_bytes=64)
-            nc.vector.quantize_mx(out=codes[:].bitcast(FP8X4), scales=scales[:], in_=grouped)
             return codes, scales
 
-        def product(target, lhs, lhs_cols, rhs, rhs_cols):
+        def quantise(mx, cols, interleaved):
+            nc.vector.quantize_mx(out=mx[0][:, cols].bitcast(FP8X4), scales=mx[1][:, cols], in_=interleaved)
+
+        def multiply(target, lhs, lhs_cols, rhs, rhs_cols):
             nc.tensor.matmul_mx(
                 out=target,
                 lhsT=lhs[0][:, lhs_cols].bitcast(FP8X4),
@@ -127,89 +113,89 @@ def tile_attend_sigmoid_kernel(tc, qT, kT, vT, vs, kb, offs, out):
                 stop=True,
             )
 
-        q_grouped = []
+        def block(first, count=1):
+            return slice(first * P, (first + count) * P)
+
+        q_mixed = []
         for b in range(B):
-            grouped = keep.tile([P, NQ * PACK], BF16, name=f"q_grouped{b}", align_bytes=64)
+            mixed = keep.tile([P, NQ * PACK], BF16, name=f"q_mixed{b}", align_bytes=64)
             nc.scalar.activation(
-                grouped[:].rearrange("p (c i j) -> p c j i", i=4, j=PACK),
+                mixed[:].rearrange("p (c i j) -> p c j i", i=4, j=PACK),
                 q_raw[b][:].rearrange("p j (c i) -> p c j i", i=4),
                 COPY,
             )
-            q_grouped.append(grouped)
+            q_mixed.append(mixed)
 
-        p_tiles = []
+        prob = []
         for b in range(B):
-            k_grouped = interleave_keys(b)
-            q_mx = quantise(f"q{b}", q_grouped[b][:], NQ)
-            prob = keep.tile([P, PACK, NQ], F32, name=f"prob{b}")
-            k_mx = (
-                keep.tile([P, N], U32, name=f"q_raw{b}", align_bytes=64),
-                keep.tile([P, N], U8, name=f"k_scales{b}", align_bytes=64),
+            k_mixed = keep.tile(
+                [P, N * PACK], BF16, name=f"k_mixed{b}", tag=("k_mixed0", "q_mixed0")[b], align_bytes=64
             )
+            nc.vector.tensor_copy(
+                k_mixed[:].bitcast(I32).rearrange("p (t s c) -> p s c t", t=PACK, c=2),
+                k_pairs[:].bitcast(I32).rearrange("p (c b s t) -> p b s c t", c=2, b=B, t=PACK)[:, b],
+            )
+            q_mx = mx_tiles(f"q{b}", NQ)
+            quantise(q_mx, slice(0, NQ), q_mixed[b][:])
+            sigmoids = keep.tile([P, PACK, NQ], F32, name=f"prob{b}")
+            k_mx = mx_tiles(f"k{b}", N, tag=f"q_raw{b}")
             for half in range(2):
-                cols = slice(half * N // 2, (half + 1) * N // 2)
-                nc.vector.quantize_mx(
-                    out=k_mx[0][:, cols].bitcast(FP8X4),
-                    scales=k_mx[1][:, cols],
-                    in_=k_grouped[:, half * 2 * N : (half + 1) * 2 * N],
-                )
-                for u in range(2):
-                    t = 2 * half + u
-                    score = psum_s.tile([P, NQ], F32, name="score")
-                    product(score[:], k_mx, slice(t * P, (t + 1) * P), q_mx, slice(0, NQ))
-                    nc.scalar.activation(prob[:, t, :], score[:], SIGMOID, bias=kb_col[:, b, t : t + 1])
-            p_tiles.append(prob)
+                quantise(k_mx, block(2 * half, 2), k_mixed[:, 2 * half * GROUP : 2 * (half + 1) * GROUP])
+                for t in (2 * half, 2 * half + 1):
+                    score = product_banks.tile([P, NQ], F32, name="product")
+                    multiply(score[:], k_mx, block(t), q_mx, slice(0, NQ))
+                    nc.scalar.activation(sigmoids[:, t, :], score[:], SIGMOID, bias=kb_col[:, b, t : t + 1])
+            prob.append(sigmoids)
 
-        def weights(engine, b, grouped, first, count):
+        def weigh(engine, b, queries, interleaved):
+            count = queries.stop - queries.start
             engine.tensor_tensor(
-                grouped.rearrange("p (c i t) -> p c t i", i=4, t=PACK),
-                p_tiles[b][:, :, first : first + count].rearrange("p t (c i) -> p c t i", i=4),
-                scale_cols[b].unsqueeze(1).unsqueeze(3).to_broadcast([P, count // 4, PACK, 4]),
+                interleaved.rearrange("p (c i t) -> p c t i", i=4, t=PACK),
+                prob[b][:, :, queries].rearrange("p t (c i) -> p c t i", i=4),
+                vs_col[b].unsqueeze(1).unsqueeze(3).to_broadcast([P, count // 4, PACK, 4]),
                 MULT,
             )
 
-        def values(e, b, grouped):
-            got = keep.tile([P, N], BF16, name=f"v_got{e}{b}", align_bytes=64)
-            nc.vector.tensor_copy(
-                got[:].rearrange("p (u s i) -> p s u i", u=2, i=2), v_win[e][:].indirect(part[b])
-            )
-            turned = psum_t.tile([P, 2, P], F32, name="turned")
+        def bring_values(k, b, interleaved):
+            got = keep.tile([P, N], BF16, name=f"v_got{k}{b}", align_bytes=64)
+            nc.vector.tensor_copy(got[:].rearrange("p (u s i) -> p s u i", u=2, i=2), v_win[k][:].indirect(own_list[b]))
+            turned = value_banks.tile([P, 2, P], F32, name="turned")
             for u in range(2):
-                nc.tensor.transpose(turned[:, u, :], got[:].bitcast(F32)[:, u * P : (u + 1) * P], ident[:])
+                nc.tensor.transpose(turned[:, u, :], got[:].bitcast(F32)[:, block(u)], identity[:])
             nc.scalar.copy(
-                grouped.bitcast(F32).rearrange("p (e u) -> p e u", u=2), turned[:].rearrange("p u e -> p e u")
+                interleaved.bitcast(F32).rearrange("p (e u) -> p e u", u=2), turned[:].rearrange("p u e -> p e u")
             )
 
-        def finish(b, h, products):
-            y = psum_s.tile([P, DV], F32, name="score")
-            for cols, lhs, lhs_cols, rhs, rhs_cols in products:
-                product(y[:, cols], lhs, lhs_cols, rhs, rhs_cols)
+        def finish(b, h, w_mx, w_cols, v_mx, v_cols):
+            y = product_banks.tile([P, DV], F32, name="product")
+            multiply(y[:], w_mx, w_cols, v_mx, v_cols)
             result = keep.tile([P, DV], F32, name=f"result{b}{h}")
-            if b + h == 2:
-                nc.vector.tensor_scalar_mul(result[:], y[:], 1.0 / 16.0)
+            if (b, h) == (1, 1):
+                nc.vector.tensor_scalar_mul(result[:], y[:], OUT_SCALE)
             else:
-                nc.scalar.activation(result[:], y[:], COPY, scale=1.0 / 16.0)
-            nc.sync.dma_start(out=out[b, h * P : (h + 1) * P, :], in_=result[:])
+                nc.scalar.activation(result[:], y[:], COPY, scale=OUT_SCALE)
+            nc.sync.dma_start(out=out[b, block(h), :], in_=result[:])
 
-        def quantise_into(mx, cols, grouped):
-            nc.vector.quantize_mx(out=mx[0][:, cols].bitcast(FP8X4), scales=mx[1][:, cols], in_=grouped)
+        wv0 = keep.tile([P, 4 * GROUP], BF16, name="wv0", tag="q_mixed0", align_bytes=64)
+        v1 = keep.tile([P, 2 * GROUP], BF16, name="v1", align_bytes=64)
+        weigh(nc.gpsimd, 0, slice(0, NQ), wv0[:, : 2 * GROUP])
+        for k in range(DV // P):
+            bring_values(k, 0, wv0[:, (2 + k) * GROUP : (3 + k) * GROUP])
+            bring_values(k, 1, v1[:, k * GROUP : (k + 1) * GROUP])
 
-        W = P * PACK
-        first = keep.tile([P, 4 * W], BF16, name="q_grouped0", align_bytes=64)
-        second = keep.tile([P, 2 * W], BF16, name="second", align_bytes=64)
-        weights(nc.gpsimd, 0, first[:, : 2 * W], 0, NQ)
-        for e in range(2):
-            values(e, 0, first[:, (2 + e) * W : (3 + e) * W])
-            values(e, 1, second[:, e * W : (e + 1) * W])
-        w10 = keep.tile([P, W], BF16, name="v_got10", align_bytes=64)
-        weights(nc.vector, 1, w10[:], 0, P)
-        first_mx = quantise("first", first[:], 4 * P)
+        w10 = keep.tile([P, GROUP], BF16, name="w10", tag="v_got10", align_bytes=64)
+        weigh(nc.vector, 1, block(0), w10[:])
+        wv0_mx = mx_tiles("wv0", 4 * P)
+        quantise(wv0_mx, block(0, 4), wv0[:])
         for h in range(2):
-            finish(0, h, [(slice(0, DV), first_mx, slice(h * P, (h + 1) * P), first_mx, slice(2 * P, 4 * P))])
-        w11 = keep.tile([P, W], BF16, name="v_got11", align_bytes=64)
-        weights(nc.vector, 1, w11[:], P, P)
-        w_mx10 = quantise("w10", w10[:], P, "v_win1")
-        second_mx = quantise("second", second[:], 2 * P)
-        finish(1, 0, [(slice(0, DV), w_mx10, slice(0, P), second_mx, slice(0, 2 * P))])
-        w_mx11 = quantise("w11", w11[:], P)
-        finish(1, 1, [(slice(0, DV), w_mx11, slice(0, P), second_mx, slice(0, 2 * P))])
+            finish(0, h, wv0_mx, block(h), wv0_mx, block(2, 2))
+        w11 = keep.tile([P, GROUP], BF16, name="w11", tag="v_got11", align_bytes=64)
+        weigh(nc.vector, 1, block(1), w11[:])
+        w10_mx = mx_tiles("w10", P)
+        quantise(w10_mx, block(0), w10[:])
+        v1_mx = mx_tiles("v1", 2 * P)
+        quantise(v1_mx, block(0, 2), v1[:])
+        finish(1, 0, w10_mx, block(0), v1_mx, block(0, 2))
+        w11_mx = mx_tiles("w11", P)
+        quantise(w11_mx, block(0), w11[:])
+        finish(1, 1, w11_mx, block(0), v1_mx, block(0, 2))

@@ -170,10 +170,7 @@ def tile_attend_sigmoid_kernel(tc, qT, kT, vT, vs, kb, offs, out):
             y = product_banks.tile([P, DV], F32, name="product")
             multiply(y[:], w_mx, w_cols, v_mx, v_cols)
             result = keep.tile([P, DV], F32, name=f"result{b}{h}")
-            if (b, h) == (1, 1):
-                nc.vector.tensor_scalar_mul(result[:], y[:], OUT_SCALE)
-            else:
-                nc.scalar.activation(result[:], y[:], COPY, scale=OUT_SCALE)
+            nc.scalar.activation(result[:], y[:], COPY, scale=OUT_SCALE)
             nc.sync.dma_start(out=out[b, block(h), :], in_=result[:])
 
         wv0 = keep.tile([P, 4 * GROUP], BF16, name="wv0", tag="q_mixed0", align_bytes=64)
@@ -191,11 +188,24 @@ def tile_attend_sigmoid_kernel(tc, qT, kT, vT, vs, kb, offs, out):
             finish(0, h, wv0_mx, block(h), wv0_mx, block(2, 2))
         w11 = keep.tile([P, GROUP], BF16, name="w11", tag="v_got11", align_bytes=64)
         weigh(nc.vector, 1, block(1), w11[:])
-        w10_mx = mx_tiles("w10", P)
-        quantise(w10_mx, block(0), w10[:])
-        v1_mx = mx_tiles("v1", 2 * P)
-        quantise(v1_mx, block(0, 2), v1[:])
-        finish(1, 0, w10_mx, block(0), v1_mx, block(0, 2))
-        w11_mx = mx_tiles("w11", P)
-        quantise(w11_mx, block(0), w11[:])
-        finish(1, 1, w11_mx, block(0), v1_mx, block(0, 2))
+        w1_mx = mx_tiles("w1", 2 * P)
+        v1_mx = mx_tiles("v1", 2 * P, tag="q_mixed0")
+        results = [keep.tile([P, DV], F32, name=f"result1{h}") for h in range(2)]
+
+        def part(h, k, banks, name):
+            y = banks.tile([P, P], F32, name=name)
+            multiply(y[:], w1_mx, block(h), v1_mx, block(k))
+            if k == 0:
+                nc.vector.tensor_scalar_mul(results[h][:, block(k)], y[:], OUT_SCALE)
+            else:
+                nc.scalar.activation(results[h][:, block(k)], y[:], COPY, scale=OUT_SCALE)
+                nc.sync.dma_start(out=out[1, block(h), :], in_=results[h][:])
+
+        quantise(w1_mx, block(0), w10[:])
+        for k in range(2):
+            quantise(v1_mx, block(k), v1[:, k * GROUP : (k + 1) * GROUP])
+        quantise(w1_mx, block(1), w11[:])
+        for k in range(2):
+            part(0, k, product_banks, "product")
+        for k in range(2):
+            part(1, k, value_banks, "turned")

@@ -86,6 +86,8 @@ def tile_attend_sigmoid_kernel(tc, qT, kT, vT, vs, kb, offs, out):
         nc.scalar.copy(vs_col0[:], turn_row(vs_got, 0, bank))
         bank = scale_bank.tile([P, PACK, P], F32, name="vs_turned")
         vs_col = (vs_col0[:], turn_row(vs_got, 1, bank))
+        vs_col1 = keep.tile([P, PACK], F32, name="vs_col1")
+        nc.scalar.copy(vs_col1[:], vs_col[1])
 
         k_pairs = keep.tile([P, 2 * B * N * 2], BF16, name="k_pairs", align_bytes=64)
         pair_halves = k_pairs[:].rearrange("p (c i half) -> p c half i", c=2, half=2)
@@ -156,12 +158,15 @@ def tile_attend_sigmoid_kernel(tc, qT, kT, vT, vs, kb, offs, out):
                 MULT,
             )
 
-        def bring_values(k, b, interleaved):
+        def turn_values(k, b, unit):
             got = keep.tile([P, N], BF16, name=f"v_got{k}{b}", align_bytes=64)
             nc.vector.tensor_copy(got[:].rearrange("p (u s i) -> p s u i", u=2, i=2), v_win[k][:].indirect(own_list[b]))
             turned = value_banks.tile([P, 2, P], F32, name="turned")
             for u in range(2):
-                nc.tensor.transpose(turned[:, u, :], got[:].bitcast(F32)[:, block(u)], identity[:])
+                nc.tensor.transpose(turned[:, u, :], got[:].bitcast(F32)[:, block(u)], unit[:])
+            return turned
+
+        def unload(turned, interleaved):
             nc.scalar.copy(
                 interleaved.bitcast(F32).rearrange("p (e u) -> p e u", u=2), turned[:].rearrange("p u e -> p e u")
             )
@@ -174,38 +179,45 @@ def tile_attend_sigmoid_kernel(tc, qT, kT, vT, vs, kb, offs, out):
             nc.sync.dma_start(out=out[b, block(h), :], in_=result[:])
 
         wv0 = keep.tile([P, 4 * GROUP], BF16, name="wv0", tag="q_mixed0", align_bytes=64)
-        v1 = keep.tile([P, 2 * GROUP], BF16, name="v1", align_bytes=64)
         weigh(nc.gpsimd, 0, slice(0, NQ), wv0[:, : 2 * GROUP])
-        for k in range(DV // P):
-            bring_values(k, 0, wv0[:, (2 + k) * GROUP : (3 + k) * GROUP])
-            bring_values(k, 1, v1[:, k * GROUP : (k + 1) * GROUP])
-
-        w10 = keep.tile([P, GROUP], BF16, name="w10", tag="v_got10", align_bytes=64)
-        weigh(nc.vector, 1, block(0), w10[:])
+        SHARE = 64
+        planes = keep.tile([P, PACK, SHARE], BF16, name="planes")
+        for t in range(PACK):
+            nc.scalar.activation(planes[:, t, :], prob[1][:, t, NQ - SHARE :], COPY, scale=vs_col1[:, t : t + 1])
+        unload(turn_values(0, 0, identity), wv0[:, 2 * GROUP : 3 * GROUP])
+        turned01 = turn_values(0, 1, identity)
+        unload(turn_values(1, 0, identity), wv0[:, 3 * GROUP :])
+        wv10 = keep.tile([P, 2 * GROUP], BF16, name="wv10", tag="v_got10", align_bytes=64)
+        unload(turned01, wv10[:, GROUP:])
+        v11 = keep.tile([P, GROUP], BF16, name="v11", align_bytes=64)
+        unload(turn_values(1, 1, identity), v11[:])
+        weigh(nc.vector, 1, block(0), wv10[:, :GROUP])
         wv0_mx = mx_tiles("wv0", 4 * P)
         quantise(wv0_mx, block(0, 4), wv0[:])
         for h in range(2):
             finish(0, h, wv0_mx, block(h), wv0_mx, block(2, 2))
         w11 = keep.tile([P, GROUP], BF16, name="w11", tag="v_got11", align_bytes=64)
-        weigh(nc.vector, 1, block(1), w11[:])
-        w1_mx = mx_tiles("w1", 2 * P)
-        v1_mx = mx_tiles("v1", 2 * P, tag="q_mixed0")
+        weigh(nc.vector, 1, slice(P, NQ - SHARE), w11[:, : GROUP - PACK * SHARE])
+        nc.scalar.copy(
+            w11[:, GROUP - PACK * SHARE :].rearrange("p (c i t) -> p c t i", i=4, t=PACK),
+            planes[:].rearrange("p t (c i) -> p c t i", i=4),
+        )
+        mx1 = mx_tiles("mx1", 4 * P)
         results = [keep.tile([P, DV], F32, name=f"result1{h}") for h in range(2)]
 
-        def part(h, k, banks, name):
+        def part(h, k, banks, name, w_block, v_block):
             y = banks.tile([P, P], F32, name=name)
-            multiply(y[:], w1_mx, block(h), v1_mx, block(k))
+            multiply(y[:], mx1, block(w_block), mx1, block(v_block))
             if k == 0:
                 nc.vector.tensor_scalar_mul(results[h][:, block(k)], y[:], OUT_SCALE)
             else:
                 nc.scalar.activation(results[h][:, block(k)], y[:], COPY, scale=OUT_SCALE)
                 nc.sync.dma_start(out=out[1, block(h), :], in_=results[h][:])
 
-        quantise(w1_mx, block(0), w10[:])
+        quantise(mx1, block(0, 2), wv10[:])
+        quantise(mx1, block(2), v11[:])
+        quantise(mx1, block(3), w11[:])
         for k in range(2):
-            quantise(v1_mx, block(k), v1[:, k * GROUP : (k + 1) * GROUP])
-        quantise(w1_mx, block(1), w11[:])
+            part(0, k, product_banks, "product", 0, 1 + k)
         for k in range(2):
-            part(0, k, product_banks, "product")
-        for k in range(2):
-            part(1, k, value_banks, "turned")
+            part(1, k, value_banks, "turned", 3, 1 + k)

@@ -9,6 +9,7 @@ PACK = 4
 LIST_COLS = N // 16
 GROUP = P * PACK
 ROW = P - 1
+SHARE = 128
 HEAD = 512
 OUT_SCALE = 1.0 / 16.0
 FLOPS = 2 * B * NQ * N * (D + DV)
@@ -30,6 +31,7 @@ def tile_attend_sigmoid_kernel(tc, qT, kT, vT, vs, kb, offs, out):
     nc = tc.nc
     with ExitStack() as ctx:
         keep = ctx.enter_context(tc.tile_pool(name="keep", bufs=1))
+        shared = ctx.enter_context(tc.tile_pool(name="shared", bufs=1))
         product_banks = ctx.enter_context(tc.psum_pool(name="product_banks", bufs=4))
         value_banks = ctx.enter_context(tc.psum_pool(name="value_banks", bufs=3))
         scale_bank = ctx.enter_context(tc.psum_pool(name="scale_bank", bufs=1))
@@ -129,16 +131,25 @@ def tile_attend_sigmoid_kernel(tc, qT, kT, vT, vs, kb, offs, out):
             q_mixed.append(mixed)
 
         prob = []
+        k_mixed_all = [
+            keep.tile([P, N * PACK], BF16, name=f"k_mixed{b}", tag=("k_mixed0", "q_mixed0")[b], align_bytes=64)
+            for b in range(B)
+        ]
+
+        def deal_views(mixed, b, tiles, word):
+            return (
+                mixed[:].bitcast(word).rearrange("p (t s c) -> p s c t", t=PACK, c=2)[:, :, :, tiles],
+                k_pairs[:].bitcast(word).rearrange("p (c b s t) -> p b s c t", c=2, b=B, t=PACK)[:, b, :, :, tiles],
+            )
+
         for b in range(B):
-            k_mixed = keep.tile(
-                [P, N * PACK], BF16, name=f"k_mixed{b}", tag=("k_mixed0", "q_mixed0")[b], align_bytes=64
-            )
-            nc.vector.tensor_copy(
-                k_mixed[:].bitcast(I32).rearrange("p (t s c) -> p s c t", t=PACK, c=2),
-                k_pairs[:].bitcast(I32).rearrange("p (c b s t) -> p b s c t", c=2, b=B, t=PACK)[:, b],
-            )
+            k_mixed = k_mixed_all[b]
+            tiles = slice(0, PACK if b == 0 else 2)
+            nc.vector.tensor_copy(*deal_views(k_mixed, b, tiles, I32))
             q_mx = mx_tiles(f"q{b}", NQ)
             quantise(q_mx, slice(0, NQ), q_mixed[b][:])
+            if b == 0:
+                nc.scalar.copy(*deal_views(k_mixed_all[1], 1, slice(2, PACK), U32))
             sigmoids = keep.tile([P, PACK, NQ], F32, name=f"prob{b}")
             k_mx = mx_tiles(f"k{b}", N, tag=f"q_raw{b}")
             for half in range(2):
@@ -158,12 +169,15 @@ def tile_attend_sigmoid_kernel(tc, qT, kT, vT, vs, kb, offs, out):
                 MULT,
             )
 
-        def turn_values(k, b, unit):
-            got = keep.tile([P, N], BF16, name=f"v_got{k}{b}", align_bytes=64)
+        def turn_values(k, b):
+            if (k, b) == (1, 0):
+                got = shared.tile([P, N], BF16, name="v_got10", offset=3 * GROUP, align_bytes=64)
+            else:
+                got = keep.tile([P, N], BF16, name=f"v_got{k}{b}", align_bytes=64)
             nc.vector.tensor_copy(got[:].rearrange("p (u s i) -> p s u i", u=2, i=2), v_win[k][:].indirect(own_list[b]))
             turned = value_banks.tile([P, 2, P], F32, name="turned")
             for u in range(2):
-                nc.tensor.transpose(turned[:, u, :], got[:].bitcast(F32)[:, block(u)], unit[:])
+                nc.tensor.transpose(turned[:, u, :], got[:].bitcast(F32)[:, block(u)], identity[:])
             return turned
 
         def unload(turned, interleaved):
@@ -171,53 +185,55 @@ def tile_attend_sigmoid_kernel(tc, qT, kT, vT, vs, kb, offs, out):
                 interleaved.bitcast(F32).rearrange("p (e u) -> p e u", u=2), turned[:].rearrange("p u e -> p e u")
             )
 
-        def finish(b, h, w_mx, w_cols, v_mx, v_cols):
-            y = product_banks.tile([P, DV], F32, name="product")
-            multiply(y[:], w_mx, w_cols, v_mx, v_cols)
-            result = keep.tile([P, DV], F32, name=f"result{b}{h}")
-            nc.scalar.activation(result[:], y[:], COPY, scale=OUT_SCALE)
-            nc.sync.dma_start(out=out[b, block(h), :], in_=result[:])
+        def group(first, count=1):
+            return slice(first * GROUP, (first + count) * GROUP)
 
-        wv0 = keep.tile([P, 4 * GROUP], BF16, name="wv0", tag="q_mixed0", align_bytes=64)
-        weigh(nc.gpsimd, 0, slice(0, NQ), wv0[:, : 2 * GROUP])
-        SHARE = 64
+        first = keep.tile([P, 4 * GROUP], BF16, name="first", tag="q_mixed0", align_bytes=64)
+        weigh(nc.gpsimd, 0, slice(0, NQ), first[:, group(1, 2)])
         planes = keep.tile([P, PACK, SHARE], BF16, name="planes")
         for t in range(PACK):
             nc.scalar.activation(planes[:, t, :], prob[1][:, t, NQ - SHARE :], COPY, scale=vs_col1[:, t : t + 1])
-        unload(turn_values(0, 0, identity), wv0[:, 2 * GROUP : 3 * GROUP])
-        turned01 = turn_values(0, 1, identity)
-        unload(turn_values(1, 0, identity), wv0[:, 3 * GROUP :])
-        wv10 = keep.tile([P, 2 * GROUP], BF16, name="wv10", tag="v_got10", align_bytes=64)
-        unload(turned01, wv10[:, GROUP:])
-        v11 = keep.tile([P, GROUP], BF16, name="v11", align_bytes=64)
-        unload(turn_values(1, 1, identity), v11[:])
-        weigh(nc.vector, 1, block(0), wv10[:, :GROUP])
-        wv0_mx = mx_tiles("wv0", 4 * P)
-        quantise(wv0_mx, block(0, 4), wv0[:])
-        for h in range(2):
-            finish(0, h, wv0_mx, block(h), wv0_mx, block(2, 2))
-        w11 = keep.tile([P, GROUP], BF16, name="w11", tag="v_got11", align_bytes=64)
-        weigh(nc.vector, 1, slice(P, NQ - SHARE), w11[:, : GROUP - PACK * SHARE])
+        unload(turn_values(0, 0), first[:, group(0)])
+        turned01 = turn_values(0, 1)
+        w11 = keep.tile([P, GROUP], BF16, name="w11", align_bytes=64)
         nc.scalar.copy(
             w11[:, GROUP - PACK * SHARE :].rearrange("p (c i t) -> p c t i", i=4, t=PACK),
             planes[:].rearrange("p t (c i) -> p c t i", i=4),
         )
-        mx1 = mx_tiles("mx1", 4 * P)
-        results = [keep.tile([P, DV], F32, name=f"result1{h}") for h in range(2)]
+        unload(turn_values(1, 0), first[:, group(3)])
+        wv10 = shared.tile([P, 2 * GROUP], BF16, name="wv10", offset=0, align_bytes=64)
+        unload(turned01, wv10[:, GROUP:])
+        v11 = keep.tile([P, GROUP], BF16, name="v11", align_bytes=64)
+        unload(turn_values(1, 1), v11[:])
+        weigh(nc.vector, 1, block(0), wv10[:, :GROUP])
+        mx = (
+            keep.tile([P, 8 * P], U32, name="mx_codes", align_bytes=64),
+            shared.tile([P, 8 * P], U8, name="mx_scales", offset=4 * GROUP, align_bytes=64),
+        )
+        results = [[keep.tile([P, DV], F32, name=f"result{b}{h}") for h in range(2)] for b in range(B)]
 
-        def part(h, k, banks, name, w_block, v_block):
+        def part(b, h, k, banks, name, eng):
             y = banks.tile([P, P], F32, name=name)
-            multiply(y[:], mx1, block(w_block), mx1, block(v_block))
-            if k == 0:
-                nc.vector.tensor_scalar_mul(results[h][:, block(k)], y[:], OUT_SCALE)
+            if b == 0:
+                multiply(y[:], mx, block(1 + h), mx, block(3 * k))
             else:
-                nc.scalar.activation(results[h][:, block(k)], y[:], COPY, scale=OUT_SCALE)
-                nc.sync.dma_start(out=out[1, block(h), :], in_=results[h][:])
+                multiply(y[:], mx, block(4 + 3 * h), mx, block(5 + k))
+            if eng == "V":
+                nc.vector.tensor_scalar_mul(results[b][h][:, block(k)], y[:], OUT_SCALE)
+            else:
+                nc.scalar.activation(results[b][h][:, block(k)], y[:], COPY, scale=OUT_SCALE)
+            if k == 1:
+                nc.sync.dma_start(out=out[b, block(h), :], in_=results[b][h][:])
 
-        quantise(mx1, block(0, 2), wv10[:])
-        quantise(mx1, block(2), v11[:])
-        quantise(mx1, block(3), w11[:])
-        for k in range(2):
-            part(0, k, product_banks, "product", 0, 1 + k)
-        for k in range(2):
-            part(1, k, value_banks, "turned", 3, 1 + k)
+        quantise(mx, block(0, 2), first[:, group(0, 2)])
+        quantise(mx, block(2, 2), first[:, group(2, 2)])
+        quantise(mx, block(4, 2), wv10[:])
+        quantise(mx, block(6), v11[:])
+        quantise(mx, block(7), w11[:])
+        for h in range(2):
+            for k in range(2):
+                part(0, h, k, product_banks, "product", "S")
+        part(1, 0, 0, value_banks, "turned", "S")
+        part(1, 0, 1, value_banks, "turned", "V")
+        part(1, 1, 0, value_banks, "turned", "V")
+        part(1, 1, 1, product_banks, "product", "S")

@@ -10,6 +10,8 @@ LIST_COLS = N // 16
 GROUP = P * PACK
 ROW = P - 1
 SHARE = 128
+EARLY = 80
+HALF = 64
 HEAD = 512
 OUT_SCALE = 1.0 / 16.0
 FLOPS = 2 * B * NQ * N * (D + DV)
@@ -83,13 +85,13 @@ def tile_attend_sigmoid_kernel(tc, qT, kT, vT, vs, kb, offs, out):
             nc.scalar.copy(kb_col[:, b, :], turn_row(kb_got, b, bank))
         vs_got = keep.tile([P, B * N], F32, name="vs_got")
         nc.vector.tensor_copy(vs_got[:], vs_win[:].indirect(lists[:]))
-        vs_col0 = keep.tile([P, PACK], F32, name="vs_col0")
-        bank = product_banks.tile([P, PACK, P], F32, name="product")
-        nc.scalar.copy(vs_col0[:], turn_row(vs_got, 0, bank))
-        bank = scale_bank.tile([P, PACK, P], F32, name="vs_turned")
-        vs_col = (vs_col0[:], turn_row(vs_got, 1, bank))
-        vs_col1 = keep.tile([P, PACK], F32, name="vs_col1")
-        nc.scalar.copy(vs_col1[:], vs_col[1])
+        bank = scale_bank.tile([P, P + 2 * B * PACK], F32, name="vs_turned")
+        for n in reversed(range(B * PACK)):
+            b, t = divmod(n, PACK)
+            nc.tensor.transpose(bank[:, 2 * n : 2 * n + P], vs_got[:, b * N + t : (b + 1) * N : PACK], identity[:])
+        vs_psum = bank[:, ROW : ROW + 2 * B * PACK : 2].rearrange("p (b t) -> p b t", b=B)
+        vs_sbuf = keep.tile([P, B, PACK], F32, name="vs_sbuf")
+        nc.scalar.copy(vs_sbuf[:], vs_psum)
 
         k_pairs = keep.tile([P, 2 * B * N * 2], BF16, name="k_pairs", align_bytes=64)
         pair_halves = k_pairs[:].rearrange("p (c i half) -> p c half i", c=2, half=2)
@@ -165,13 +167,13 @@ def tile_attend_sigmoid_kernel(tc, qT, kT, vT, vs, kb, offs, out):
             engine.tensor_tensor(
                 interleaved.rearrange("p (c i t) -> p c t i", i=4, t=PACK),
                 prob[b][:, :, queries].rearrange("p t (c i) -> p c t i", i=4),
-                vs_col[b].unsqueeze(1).unsqueeze(3).to_broadcast([P, count // 4, PACK, 4]),
+                (vs_psum if engine is nc.vector else vs_sbuf)[:, b, :].unsqueeze(1).unsqueeze(3).to_broadcast([P, count // 4, PACK, 4]),
                 MULT,
             )
 
         def turn_values(k, b):
             if (k, b) == (1, 0):
-                got = shared.tile([P, N], BF16, name="v_got10", offset=3 * GROUP, align_bytes=64)
+                got = shared.tile([P, 3 * N], BF16, name="v_got10", offset=GROUP, align_bytes=64)[:, :N]
             else:
                 got = keep.tile([P, N], BF16, name=f"v_got{k}{b}", align_bytes=64)
             nc.vector.tensor_copy(got[:].rearrange("p (u s i) -> p s u i", u=2, i=2), v_win[k][:].indirect(own_list[b]))
@@ -189,23 +191,26 @@ def tile_attend_sigmoid_kernel(tc, qT, kT, vT, vs, kb, offs, out):
             return slice(first * GROUP, (first + count) * GROUP)
 
         first = keep.tile([P, 4 * GROUP], BF16, name="first", tag="q_mixed0", align_bytes=64)
-        weigh(nc.gpsimd, 0, slice(0, NQ), first[:, group(1, 2)])
+        weigh(nc.gpsimd, 0, slice(0, NQ - EARLY), first[:, GROUP : 3 * GROUP - PACK * EARLY])
         planes = keep.tile([P, PACK, SHARE], BF16, name="planes")
         for t in range(PACK):
-            nc.scalar.activation(planes[:, t, :], prob[1][:, t, NQ - SHARE :], COPY, scale=vs_col1[:, t : t + 1])
+            nc.scalar.activation(planes[:, t, :], prob[1][:, t, NQ - SHARE :], COPY, scale=vs_sbuf[:, 1, t : t + 1])
         unload(turn_values(0, 0), first[:, group(0)])
-        turned01 = turn_values(0, 1)
-        w11 = keep.tile([P, GROUP], BF16, name="w11", align_bytes=64)
+        v01 = keep.tile([P, GROUP], BF16, name="v01", align_bytes=64)
+        unload(turn_values(0, 1), v01[:])
+        weigh(nc.vector, 0, slice(NQ - EARLY, NQ), first[:, 3 * GROUP - PACK * EARLY : 3 * GROUP])
+        w10_head = keep.tile([P, PACK * HALF], BF16, name="w10_head", align_bytes=64)
+        weigh(nc.gpsimd, 1, slice(0, HALF), w10_head[:])
+        unload(turn_values(1, 0), first[:, group(3)])
+        w11 = shared.tile([P, GROUP], BF16, name="w11", offset=2 * GROUP, align_bytes=64)
         nc.scalar.copy(
-            w11[:, GROUP - PACK * SHARE :].rearrange("p (c i t) -> p c t i", i=4, t=PACK),
+            w11[:].rearrange("p (c i t) -> p c t i", i=4, t=PACK),
             planes[:].rearrange("p t (c i) -> p c t i", i=4),
         )
-        unload(turn_values(1, 0), first[:, group(3)])
-        wv10 = shared.tile([P, 2 * GROUP], BF16, name="wv10", offset=0, align_bytes=64)
-        unload(turned01, wv10[:, GROUP:])
         v11 = keep.tile([P, GROUP], BF16, name="v11", align_bytes=64)
         unload(turn_values(1, 1), v11[:])
-        weigh(nc.vector, 1, block(0), wv10[:, :GROUP])
+        w10_rest = shared.tile([P, PACK * (P - HALF)], BF16, name="w10_rest", offset=GROUP, align_bytes=64)
+        weigh(nc.vector, 1, slice(HALF, P), w10_rest[:])
         mx = (
             keep.tile([P, 8 * P], U32, name="mx_codes", align_bytes=64),
             shared.tile([P, 8 * P], U8, name="mx_scales", offset=4 * GROUP, align_bytes=64),
@@ -227,7 +232,9 @@ def tile_attend_sigmoid_kernel(tc, qT, kT, vT, vs, kb, offs, out):
 
         quantise(mx, block(0, 2), first[:, group(0, 2)])
         quantise(mx, block(2, 2), first[:, group(2, 2)])
-        quantise(mx, block(4, 2), wv10[:])
+        quantise(mx, block(5), v01[:])
+        quantise(mx, slice(4 * P, 4 * P + HALF), w10_head[:])
+        quantise(mx, slice(4 * P + HALF, 5 * P), w10_rest[:])
         quantise(mx, block(6), v11[:])
         quantise(mx, block(7), w11[:])
         for h in range(2):

@@ -235,12 +235,12 @@ def tile_attend_sigmoid_kernel(tc, qT, kT, vT, vs, kb, offs, out):
         quantise(mx, block(5), v01[:])
         quantise(mx, slice(4 * P, 4 * P + HALF), w10_head[:])
         quantise(mx, slice(4 * P + HALF, 5 * P), w10_rest[:])
-        quantise(mx, block(6), v11[:])
         quantise(mx, block(7), w11[:])
+        quantise(mx, block(6), v11[:])
         for h in range(2):
             for k in range(2):
                 part(0, h, k, product_banks, "product", "S")
-        part(1, 0, 0, value_banks, "turned", "S")
+        part(1, 0, 0, value_banks, "turned", "V")
+        part(1, 1, 0, value_banks, "turned", "S")
         part(1, 0, 1, value_banks, "turned", "V")
-        part(1, 1, 0, value_banks, "turned", "V")
         part(1, 1, 1, product_banks, "product", "S")

@@ -162,6 +162,10 @@ def tile_attend_sigmoid_kernel(tc, qT, kT, vT, vs, kb, offs, out):
                     nc.scalar.activation(sigmoids[:, t, :], score[:], SIGMOID, bias=kb_col[:, b, t : t + 1])
             prob.append(sigmoids)
 
+        spare = product_banks.tile([P, N], F32, name="product")
+        multiply(spare[:], q_mx, block(0), k_mx, slice(0, N))
+        multiply(spare[:, :NQ], q_mx, block(1), k_mx, slice(0, NQ))
+
         def weigh(engine, b, queries, interleaved):
             count = queries.stop - queries.start
             engine.tensor_tensor(

@@ -11,7 +11,7 @@ GROUP = P * PACK
 ROW = P - 1
 SHARE = 128
 EARLY = 80
-HALF = 64
+REST = 64
 HEAD = 512
 OUT_SCALE = 1.0 / 16.0
 FLOPS = 2 * B * NQ * N * (D + DV)
@@ -33,7 +33,6 @@ def tile_attend_sigmoid_kernel(tc, qT, kT, vT, vs, kb, offs, out):
     nc = tc.nc
     with ExitStack() as ctx:
         keep = ctx.enter_context(tc.tile_pool(name="keep", bufs=1))
-        shared = ctx.enter_context(tc.tile_pool(name="shared", bufs=1))
         product_banks = ctx.enter_context(tc.psum_pool(name="product_banks", bufs=4))
         value_banks = ctx.enter_context(tc.psum_pool(name="value_banks", bufs=3))
         scale_bank = ctx.enter_context(tc.psum_pool(name="scale_bank", bufs=1))
@@ -71,6 +70,8 @@ def tile_attend_sigmoid_kernel(tc, qT, kT, vT, vs, kb, offs, out):
         nc.gpsimd.memset(vs_win[:ROW, :], 0.0)
         identity = keep.tile([P, P], F32, name="identity")
         make_identity(nc, identity[:])
+        identity_late = keep.tile([P, P], F32, name="identity_late", align_bytes=64)
+        nc.scalar.copy(identity_late[:], identity[:])
 
         def turn_row(gathered, b, bank):
             for t in range(PACK):
@@ -175,15 +176,18 @@ def tile_attend_sigmoid_kernel(tc, qT, kT, vT, vs, kb, offs, out):
                 MULT,
             )
 
+        second = keep.tile([P, 3 * GROUP], BF16, name="second", align_bytes=64)
+        w1 = second[:, GROUP:]
+
         def turn_values(k, b):
             if (k, b) == (1, 0):
-                got = shared.tile([P, 3 * N], BF16, name="v_got10", offset=GROUP, align_bytes=64)[:, :N]
+                got = w1[:, GROUP - P : 2 * GROUP - P]
             else:
-                got = keep.tile([P, N], BF16, name=f"v_got{k}{b}", align_bytes=64)
-            nc.vector.tensor_copy(got[:].rearrange("p (u s i) -> p s u i", u=2, i=2), v_win[k][:].indirect(own_list[b]))
+                got = keep.tile([P, N], BF16, name=f"v_got{k}{b}", align_bytes=64)[:]
+            nc.vector.tensor_copy(got.rearrange("p (u s i) -> p s u i", u=2, i=2), v_win[k][:].indirect(own_list[b]))
             turned = value_banks.tile([P, 2, P], F32, name="turned")
-            for u in range(2):
-                nc.tensor.transpose(turned[:, u, :], got[:].bitcast(F32)[:, block(u)], identity[:])
+            for u in ((1, 0) if (k, b) == (1, 0) else (0, 1)):
+                nc.tensor.transpose(turned[:, u, :], got.bitcast(F32)[:, block(u)], (identity_late if (k, b, u) == (1, 0, 0) else identity)[:])
             return turned
 
         def unload(turned, interleaved):
@@ -200,24 +204,20 @@ def tile_attend_sigmoid_kernel(tc, qT, kT, vT, vs, kb, offs, out):
         for t in range(PACK):
             nc.scalar.activation(planes[:, t, :], prob[1][:, t, NQ - SHARE :], COPY, scale=vs_sbuf[:, 1, t : t + 1])
         unload(turn_values(0, 0), first[:, group(0)])
-        v01 = keep.tile([P, GROUP], BF16, name="v01", align_bytes=64)
-        unload(turn_values(0, 1), v01[:])
+        unload(turn_values(0, 1), second[:, group(0)])
         weigh(nc.vector, 0, slice(NQ - EARLY, NQ), first[:, 3 * GROUP - PACK * EARLY : 3 * GROUP])
-        w10_head = keep.tile([P, PACK * HALF], BF16, name="w10_head", align_bytes=64)
-        weigh(nc.gpsimd, 1, slice(0, HALF), w10_head[:])
+        weigh(nc.gpsimd, 1, slice(0, P - REST), w1[:, : GROUP - PACK * REST])
         unload(turn_values(1, 0), first[:, group(3)])
-        w11 = shared.tile([P, GROUP], BF16, name="w11", offset=2 * GROUP, align_bytes=64)
         nc.scalar.copy(
-            w11[:].rearrange("p (c i t) -> p c t i", i=4, t=PACK),
+            w1[:, GROUP:].rearrange("p (c i t) -> p c t i", i=4, t=PACK),
             planes[:].rearrange("p t (c i) -> p c t i", i=4),
         )
         v11 = keep.tile([P, GROUP], BF16, name="v11", align_bytes=64)
         unload(turn_values(1, 1), v11[:])
-        w10_rest = shared.tile([P, PACK * (P - HALF)], BF16, name="w10_rest", offset=GROUP, align_bytes=64)
-        weigh(nc.vector, 1, slice(HALF, P), w10_rest[:])
+        weigh(nc.vector, 1, slice(P - REST, P), w1[:, GROUP - PACK * REST : GROUP])
         mx = (
             keep.tile([P, 8 * P], U32, name="mx_codes", align_bytes=64),
-            shared.tile([P, 8 * P], U8, name="mx_scales", offset=4 * GROUP, align_bytes=64),
+            keep.tile([P, 8 * P], U8, name="mx_scales", tag="identity_late", align_bytes=64),
         )
         results = [[keep.tile([P, DV], F32, name=f"result{b}{h}") for h in range(2)] for b in range(B)]
 
@@ -226,7 +226,7 @@ def tile_attend_sigmoid_kernel(tc, qT, kT, vT, vs, kb, offs, out):
             if b == 0:
                 multiply(y[:], mx, block(1 + h), mx, block(3 * k))
             else:
-                multiply(y[:], mx, block(4 + 3 * h), mx, block(5 + k))
+                multiply(y[:], mx, block(5 + 2 * h), mx, block(4 + 2 * k))
             if eng == "V":
                 nc.vector.tensor_scalar_mul(results[b][h][:, block(k)], y[:], OUT_SCALE)
             else:
@@ -236,10 +236,8 @@ def tile_attend_sigmoid_kernel(tc, qT, kT, vT, vs, kb, offs, out):
 
         quantise(mx, block(0, 2), first[:, group(0, 2)])
         quantise(mx, block(2, 2), first[:, group(2, 2)])
-        quantise(mx, block(5), v01[:])
-        quantise(mx, slice(4 * P, 4 * P + HALF), w10_head[:])
-        quantise(mx, slice(4 * P + HALF, 5 * P), w10_rest[:])
-        quantise(mx, block(7), w11[:])
+        quantise(mx, block(4, 2), second[:, group(0, 2)])
+        quantise(mx, block(7), second[:, group(2)])
         quantise(mx, block(6), v11[:])
         for h in range(2):
             for k in range(2):

@@ -9,10 +9,9 @@ PACK = 4
 LIST_COLS = N // 16
 GROUP = P * PACK
 ROW = P - 1
-SHARE = 128
-EARLY = 80
-REST = 64
 HEAD = 512
+EARLY = 80
+SECOND = 64
 OUT_SCALE = 1.0 / 16.0
 FLOPS = 2 * B * NQ * N * (D + DV)
 BYTES = 4 * (B * D * NQ + D * T + DV * T + 2 * T + B * NQ * DV) + 2 * P * B * LIST_COLS
@@ -27,6 +26,14 @@ FP8X4 = mybir.dt.float8_e4m3fn_x4
 COPY = mybir.ActivationFunctionType.Copy
 SIGMOID = mybir.ActivationFunctionType.Sigmoid
 MULT = mybir.AluOpType.mult
+
+
+def block(first, count=1):
+    return slice(first * P, (first + count) * P)
+
+
+def group(first, count=1):
+    return slice(first * GROUP, (first + count) * GROUP)
 
 
 def tile_attend_sigmoid_kernel(tc, qT, kT, vT, vs, kb, offs, out):
@@ -73,17 +80,14 @@ def tile_attend_sigmoid_kernel(tc, qT, kT, vT, vs, kb, offs, out):
         identity_late = keep.tile([P, P], F32, name="identity_late", align_bytes=64)
         nc.scalar.copy(identity_late[:], identity[:])
 
-        def turn_row(gathered, b, bank):
-            for t in range(PACK):
-                nc.tensor.transpose(bank[:, t, :], gathered[:, b * N + t : (b + 1) * N : PACK], identity[:])
-            return bank[:, :, ROW]
-
         kb_got = keep.tile([P, B * N], F32, name="kb_got")
         nc.vector.tensor_copy(kb_got[:], kb_win[:].indirect(lists[:]))
         kb_col = keep.tile([P, B, PACK], F32, name="kb_col")
         for b in range(B):
             bank = product_banks.tile([P, PACK, P], F32, name="product")
-            nc.scalar.copy(kb_col[:, b, :], turn_row(kb_got, b, bank))
+            for t in range(PACK):
+                nc.tensor.transpose(bank[:, t, :], kb_got[:, b * N + t : (b + 1) * N : PACK], identity[:])
+            nc.scalar.copy(kb_col[:, b, :], bank[:, :, ROW])
         vs_got = keep.tile([P, B * N], F32, name="vs_got")
         nc.vector.tensor_copy(vs_got[:], vs_win[:].indirect(lists[:]))
         bank = scale_bank.tile([P, P + 2 * B * PACK], F32, name="vs_turned")
@@ -101,9 +105,9 @@ def tile_attend_sigmoid_kernel(tc, qT, kT, vT, vs, kb, offs, out):
         for b in range(B):
             nc.vector.tensor_copy(pair_halves[:, 1, 1, b * N : (b + 1) * N], k_win[PACK - 1][:].indirect(own_list[b]))
 
-        def mx_tiles(name, width, tag=None):
-            codes = keep.tile([P, width], U32, name=f"{name}_codes", tag=tag or f"{name}_codes", align_bytes=64)
-            scales = keep.tile([P, width], U8, name=f"{name}_scales", align_bytes=64)
+        def mx_tiles(name, width, codes_tag=None, scales_tag=None):
+            codes = keep.tile([P, width], U32, name=f"{name}_codes", tag=codes_tag or f"{name}_codes", align_bytes=64)
+            scales = keep.tile([P, width], U8, name=f"{name}_scales", tag=scales_tag or f"{name}_scales", align_bytes=64)
             return codes, scales
 
         def quantise(mx, cols, interleaved):
@@ -120,9 +124,6 @@ def tile_attend_sigmoid_kernel(tc, qT, kT, vT, vs, kb, offs, out):
                 stop=True,
             )
 
-        def block(first, count=1):
-            return slice(first * P, (first + count) * P)
-
         q_mixed = []
         for b in range(B):
             mixed = keep.tile([P, NQ * PACK], BF16, name=f"q_mixed{b}", align_bytes=64)
@@ -133,116 +134,105 @@ def tile_attend_sigmoid_kernel(tc, qT, kT, vT, vs, kb, offs, out):
             )
             q_mixed.append(mixed)
 
-        prob = []
-        k_mixed_all = [
+        k_mixed = [
             keep.tile([P, N * PACK], BF16, name=f"k_mixed{b}", tag=("k_mixed0", "q_mixed0")[b], align_bytes=64)
             for b in range(B)
         ]
 
-        def deal_views(mixed, b, tiles, word):
+        def deal_views(b, tiles, word):
             return (
-                mixed[:].bitcast(word).rearrange("p (t s c) -> p s c t", t=PACK, c=2)[:, :, :, tiles],
+                k_mixed[b][:].bitcast(word).rearrange("p (t s c) -> p s c t", t=PACK, c=2)[:, :, :, tiles],
                 k_pairs[:].bitcast(word).rearrange("p (c b s t) -> p b s c t", c=2, b=B, t=PACK)[:, b, :, :, tiles],
             )
 
+        prob = []
         for b in range(B):
-            k_mixed = k_mixed_all[b]
-            tiles = slice(0, PACK if b == 0 else 2)
-            nc.vector.tensor_copy(*deal_views(k_mixed, b, tiles, I32))
+            nc.vector.tensor_copy(*deal_views(b, slice(0, (PACK, 2)[b]), I32))
             q_mx = mx_tiles(f"q{b}", NQ)
             quantise(q_mx, slice(0, NQ), q_mixed[b][:])
             if b == 0:
-                nc.scalar.copy(*deal_views(k_mixed_all[1], 1, slice(2, PACK), U32))
+                nc.scalar.copy(*deal_views(1, slice(2, PACK), U32))
             sigmoids = keep.tile([P, PACK, NQ], F32, name=f"prob{b}")
-            k_mx = mx_tiles(f"k{b}", N, tag=f"q_raw{b}")
+            k_mx = mx_tiles(f"k{b}", N, codes_tag=f"q_raw{b}")
             for half in range(2):
-                quantise(k_mx, block(2 * half, 2), k_mixed[:, 2 * half * GROUP : 2 * (half + 1) * GROUP])
+                quantise(k_mx, block(2 * half, 2), k_mixed[b][:, group(2 * half, 2)])
                 for t in (2 * half, 2 * half + 1):
                     score = product_banks.tile([P, NQ], F32, name="product")
                     multiply(score[:], k_mx, block(t), q_mx, slice(0, NQ))
                     nc.scalar.activation(sigmoids[:, t, :], score[:], SIGMOID, bias=kb_col[:, b, t : t + 1])
             prob.append(sigmoids)
 
-        spare = product_banks.tile([P, N], F32, name="product")
-        multiply(spare[:], q_mx, block(0), k_mx, slice(0, N))
-        multiply(spare[:, :NQ], q_mx, block(1), k_mx, slice(0, NQ))
+        second = keep.tile([P, 3 * GROUP], BF16, name="second", align_bytes=64)
+        w1 = second[:, group(1, 2)]
 
-        def weigh(engine, b, queries, interleaved):
-            count = queries.stop - queries.start
+        def weigh(engine, scales, b, first_query, count, weights):
             engine.tensor_tensor(
-                interleaved.rearrange("p (c i t) -> p c t i", i=4, t=PACK),
-                prob[b][:, :, queries].rearrange("p t (c i) -> p c t i", i=4),
-                (vs_psum if engine is nc.vector else vs_sbuf)[:, b, :].unsqueeze(1).unsqueeze(3).to_broadcast([P, count // 4, PACK, 4]),
+                weights[:, PACK * first_query : PACK * (first_query + count)].rearrange(
+                    "p (c i t) -> p c t i", i=4, t=PACK
+                ),
+                prob[b][:, :, first_query : first_query + count].rearrange("p t (c i) -> p c t i", i=4),
+                scales[:, b, :].unsqueeze(1).unsqueeze(3).to_broadcast([P, count // 4, PACK, 4]),
                 MULT,
             )
 
-        second = keep.tile([P, 3 * GROUP], BF16, name="second", align_bytes=64)
-        w1 = second[:, GROUP:]
-
-        def turn_values(k, b):
-            if (k, b) == (1, 0):
-                got = w1[:, GROUP - P : 2 * GROUP - P]
-            else:
-                got = keep.tile([P, N], BF16, name=f"v_got{k}{b}", align_bytes=64)[:]
+        def values(k, b, got, interleaved, turns):
             nc.vector.tensor_copy(got.rearrange("p (u s i) -> p s u i", u=2, i=2), v_win[k][:].indirect(own_list[b]))
             turned = value_banks.tile([P, 2, P], F32, name="turned")
-            for u in ((1, 0) if (k, b) == (1, 0) else (0, 1)):
-                nc.tensor.transpose(turned[:, u, :], got.bitcast(F32)[:, block(u)], (identity_late if (k, b, u) == (1, 0, 0) else identity)[:])
-            return turned
-
-        def unload(turned, interleaved):
+            for u, unit in turns:
+                nc.tensor.transpose(turned[:, u, :], got.bitcast(F32)[:, block(u)], unit[:])
             nc.scalar.copy(
                 interleaved.bitcast(F32).rearrange("p (e u) -> p e u", u=2), turned[:].rearrange("p u e -> p e u")
             )
 
-        def group(first, count=1):
-            return slice(first * GROUP, (first + count) * GROUP)
+        def own_tile(name):
+            return keep.tile([P, N], BF16, name=name, align_bytes=64)[:]
 
+        plain_turns = ((0, identity), (1, identity))
         first = keep.tile([P, 4 * GROUP], BF16, name="first", tag="q_mixed0", align_bytes=64)
-        weigh(nc.gpsimd, 0, slice(0, NQ - EARLY), first[:, GROUP : 3 * GROUP - PACK * EARLY])
-        planes = keep.tile([P, PACK, SHARE], BF16, name="planes")
+        w0 = first[:, group(1, 2)]
+        weigh(nc.gpsimd, vs_sbuf, 0, 0, NQ - EARLY, w0)
+        planes = keep.tile([P, PACK, P], BF16, name="planes")
         for t in range(PACK):
-            nc.scalar.activation(planes[:, t, :], prob[1][:, t, NQ - SHARE :], COPY, scale=vs_sbuf[:, 1, t : t + 1])
-        unload(turn_values(0, 0), first[:, group(0)])
-        unload(turn_values(0, 1), second[:, group(0)])
-        weigh(nc.vector, 0, slice(NQ - EARLY, NQ), first[:, 3 * GROUP - PACK * EARLY : 3 * GROUP])
-        weigh(nc.gpsimd, 1, slice(0, P - REST), w1[:, : GROUP - PACK * REST])
-        unload(turn_values(1, 0), first[:, group(3)])
+            nc.scalar.activation(planes[:, t, :], prob[1][:, t, P:], COPY, scale=vs_sbuf[:, 1, t : t + 1])
+        values(0, 0, own_tile("v_got00"), first[:, group(0)], plain_turns)
+        values(0, 1, own_tile("v_got01"), second[:, group(0)], plain_turns)
+        weigh(nc.vector, vs_psum, 0, NQ - EARLY, EARLY, w0)
+        weigh(nc.gpsimd, vs_sbuf, 1, 0, SECOND, w1)
+        values(1, 0, w1[:, GROUP - P : 2 * GROUP - P], first[:, group(3)], ((1, identity), (0, identity_late)))
         nc.scalar.copy(
-            w1[:, GROUP:].rearrange("p (c i t) -> p c t i", i=4, t=PACK),
+            w1[:, group(1)].rearrange("p (c i t) -> p c t i", i=4, t=PACK),
             planes[:].rearrange("p t (c i) -> p c t i", i=4),
         )
         v11 = keep.tile([P, GROUP], BF16, name="v11", align_bytes=64)
-        unload(turn_values(1, 1), v11[:])
-        weigh(nc.vector, 1, slice(P - REST, P), w1[:, GROUP - PACK * REST : GROUP])
-        mx = (
-            keep.tile([P, 8 * P], U32, name="mx_codes", align_bytes=64),
-            keep.tile([P, 8 * P], U8, name="mx_scales", tag="identity_late", align_bytes=64),
-        )
-        results = [[keep.tile([P, DV], F32, name=f"result{b}{h}") for h in range(2)] for b in range(B)]
+        values(1, 1, own_tile("v_got11"), v11[:], plain_turns)
+        weigh(nc.vector, vs_psum, 1, SECOND, P - SECOND, w1)
 
-        def part(b, h, k, banks, name, eng):
-            y = banks.tile([P, P], F32, name=name)
-            if b == 0:
-                multiply(y[:], mx, block(1 + h), mx, block(3 * k))
-            else:
-                multiply(y[:], mx, block(5 + 2 * h), mx, block(4 + 2 * k))
-            if eng == "V":
-                nc.vector.tensor_scalar_mul(results[b][h][:, block(k)], y[:], OUT_SCALE)
-            else:
-                nc.scalar.activation(results[b][h][:, block(k)], y[:], COPY, scale=OUT_SCALE)
-            if k == 1:
-                nc.sync.dma_start(out=out[b, block(h), :], in_=results[b][h][:])
-
+        mx = mx_tiles("mx", 8 * P, scales_tag="identity_late")
         quantise(mx, block(0, 2), first[:, group(0, 2)])
         quantise(mx, block(2, 2), first[:, group(2, 2)])
         quantise(mx, block(4, 2), second[:, group(0, 2)])
         quantise(mx, block(7), second[:, group(2)])
         quantise(mx, block(6), v11[:])
+        w_block = ((1, 2), (5, 7))
+        v_block = ((0, 3), (4, 6))
+        results = [[keep.tile([P, DV], F32, name=f"result{b}{h}") for h in range(2)] for b in range(B)]
+
+        def finish(b, h, k, bank, scale_out):
+            multiply(bank[:], mx, block(w_block[b][h]), mx, block(v_block[b][k]))
+            scale_out(results[b][h][:, block(k)], bank[:])
+            if k == 1:
+                nc.sync.dma_start(out=out[b, block(h), :], in_=results[b][h][:])
+
+        def by_scalar(target, bank):
+            nc.scalar.activation(target, bank, COPY, scale=OUT_SCALE)
+
+        def by_vector(target, bank):
+            nc.vector.tensor_scalar_mul(target, bank, OUT_SCALE)
+
         for h in range(2):
             for k in range(2):
-                part(0, h, k, product_banks, "product", "S")
-        part(1, 0, 0, value_banks, "turned", "V")
-        part(1, 1, 0, value_banks, "turned", "S")
-        part(1, 0, 1, value_banks, "turned", "V")
-        part(1, 1, 1, product_banks, "product", "S")
+                finish(0, h, k, product_banks.tile([P, P], F32, name="product"), by_scalar)
+        finish(1, 0, 0, value_banks.tile([P, P], F32, name="turned"), by_vector)
+        finish(1, 1, 0, value_banks.tile([P, P], F32, name="turned"), by_scalar)
+        finish(1, 0, 1, value_banks.tile([P, P], F32, name="turned"), by_vector)
+        finish(1, 1, 1, product_banks.tile([P, P], F32, name="product"), by_scalar)

@@ -11,7 +11,7 @@ GROUP = P * PACK
 ROW = P - 1
 HEAD = 512
 EARLY = 80
-SECOND = 64
+SECOND = 80
 OUT_SCALE = 1.0 / 16.0
 FLOPS = 2 * B * NQ * N * (D + DV)
 BYTES = 4 * (B * D * NQ + D * T + DV * T + 2 * T + B * NQ * DV) + 2 * P * B * LIST_COLS
@@ -209,7 +209,8 @@ def tile_attend_sigmoid_kernel(tc, qT, kT, vT, vs, kb, offs, out):
 
         mx = mx_tiles("mx", 8 * P, scales_tag="identity_late")
         quantise(mx, block(0, 2), first[:, group(0, 2)])
-        quantise(mx, block(2, 2), first[:, group(2, 2)])
+        quantise(mx, block(3), first[:, group(3)])
+        quantise(mx, block(2), first[:, group(2)])
         quantise(mx, block(4, 2), second[:, group(0, 2)])
         quantise(mx, block(7), second[:, group(2)])
         quantise(mx, block(6), v11[:])

@@ -12,6 +12,7 @@ ROW = P - 1
 HEAD = 512
 EARLY = 80
 SECOND = 80
+MIXED = 128
 OUT_SCALE = 1.0 / 16.0
 FLOPS = 2 * B * NQ * N * (D + DV)
 BYTES = 4 * (B * D * NQ + D * T + DV * T + 2 * T + B * NQ * DV) + 2 * P * B * LIST_COLS
@@ -102,8 +103,11 @@ def tile_attend_sigmoid_kernel(tc, qT, kT, vT, vs, kb, offs, out):
         pair_halves = k_pairs[:].rearrange("p (c i half) -> p c half i", c=2, half=2)
         for j in range(PACK - 1):
             nc.vector.tensor_copy(pair_halves[:, j // 2, j % 2], k_win[j][:].indirect(lists[:]))
-        for b in range(B):
-            nc.vector.tensor_copy(pair_halves[:, 1, 1, b * N : (b + 1) * N], k_win[PACK - 1][:].indirect(own_list[b]))
+        for first, count in ((0, N // 2), (N // 2, N // 2), (N, N)):
+            nc.vector.tensor_copy(
+                pair_halves[:, 1, 1, first : first + count],
+                k_win[PACK - 1][:].indirect(lists[:, first // 16 : (first + count) // 16]),
+            )
 
         def mx_tiles(name, width, codes_tag=None, scales_tag=None):
             codes = keep.tile([P, width], U32, name=f"{name}_codes", tag=codes_tag or f"{name}_codes", align_bytes=64)
@@ -124,41 +128,51 @@ def tile_attend_sigmoid_kernel(tc, qT, kT, vT, vs, kb, offs, out):
                 stop=True,
             )
 
-        q_mixed = []
-        for b in range(B):
-            mixed = keep.tile([P, NQ * PACK], BF16, name=f"q_mixed{b}", align_bytes=64)
-            nc.scalar.activation(
-                mixed[:].rearrange("p (c i j) -> p c j i", i=4, j=PACK),
-                q_raw[b][:].rearrange("p j (c i) -> p c j i", i=4),
-                COPY,
+        q_mixed = [keep.tile([P, NQ * PACK], BF16, name=f"q_mixed{b}", align_bytes=64) for b in range(B)]
+
+        def mix_views(b, first, count):
+            return (
+                q_mixed[b][:, PACK * first : PACK * (first + count)].rearrange("p (c i j) -> p c j i", i=4, j=PACK),
+                q_raw[b][:, :, first : first + count].rearrange("p j (c i) -> p c j i", i=4),
             )
-            q_mixed.append(mixed)
 
         k_mixed = [
             keep.tile([P, N * PACK], BF16, name=f"k_mixed{b}", tag=("k_mixed0", "q_mixed0")[b], align_bytes=64)
             for b in range(B)
         ]
 
-        def deal_views(b, tiles, word):
+        def deal_views(b, rows, word):
             return (
-                k_mixed[b][:].bitcast(word).rearrange("p (t s c) -> p s c t", t=PACK, c=2)[:, :, :, tiles],
-                k_pairs[:].bitcast(word).rearrange("p (c b s t) -> p b s c t", c=2, b=B, t=PACK)[:, b, :, :, tiles],
+                k_mixed[b][:].bitcast(word).rearrange("p (t s c) -> p s c t", t=PACK, c=2)[:, rows],
+                k_pairs[:].bitcast(word).rearrange("p (c b s t) -> p b s c t", c=2, b=B, t=PACK)[:, b, rows],
             )
+
+        for half in range(2):
+            nc.scalar.copy(*deal_views(0, slice(half * P // 2, (half + 1) * P // 2), U32))
+        nc.vector.tensor_copy(*mix_views(0, 0, MIXED))
+        nc.scalar.activation(*mix_views(0, MIXED, NQ - MIXED), COPY)
+        nc.scalar.activation(*mix_views(1, 0, NQ), COPY)
 
         prob = []
         for b in range(B):
-            nc.vector.tensor_copy(*deal_views(b, slice(0, (PACK, 2)[b]), I32))
+            if b == 1:
+                nc.vector.tensor_copy(*deal_views(b, slice(0, P), I32))
             q_mx = mx_tiles(f"q{b}", NQ)
-            quantise(q_mx, slice(0, NQ), q_mixed[b][:])
-            if b == 0:
-                nc.scalar.copy(*deal_views(1, slice(2, PACK), U32))
             sigmoids = keep.tile([P, PACK, NQ], F32, name=f"prob{b}")
-            k_mx = mx_tiles(f"k{b}", N, codes_tag=f"q_raw{b}")
+            if b == 0:
+                k_mx = [mx_tiles("k0a", 2 * P), mx_tiles("k0b", 2 * P, codes_tag="q_raw0")]
+                k_cols = [0, 0]
+                quantise(k_mx[0], block(0, 2), k_mixed[0][:, group(0, 2)])
+            else:
+                k_mx = [mx_tiles("k1", N, codes_tag="q_raw1")] * 2
+                k_cols = [0, 2]
+            quantise(q_mx, slice(0, NQ), q_mixed[b][:])
             for half in range(2):
-                quantise(k_mx, block(2 * half, 2), k_mixed[b][:, group(2 * half, 2)])
+                if (b, half) != (0, 0):
+                    quantise(k_mx[half], block(k_cols[half], 2), k_mixed[b][:, group(2 * half, 2)])
                 for t in (2 * half, 2 * half + 1):
                     score = product_banks.tile([P, NQ], F32, name="product")
-                    multiply(score[:], k_mx, block(t), q_mx, slice(0, NQ))
+                    multiply(score[:], k_mx[half], block(k_cols[half] + t % 2), q_mx, slice(0, NQ))
                     nc.scalar.activation(sigmoids[:, t, :], score[:], SIGMOID, bias=kb_col[:, b, t : t + 1])
             prob.append(sigmoids)
 

@@ -10,9 +10,6 @@ LIST_COLS = N // 16
 GROUP = P * PACK
 ROW = P - 1
 HEAD = 512
-EARLY = 80
-SECOND = 80
-MIXED = 128
 OUT_SCALE = 1.0 / 16.0
 FLOPS = 2 * B * NQ * N * (D + DV)
 BYTES = 4 * (B * D * NQ + D * T + DV * T + 2 * T + B * NQ * DV) + 2 * P * B * LIST_COLS
@@ -84,11 +81,14 @@ def tile_attend_sigmoid_kernel(tc, qT, kT, vT, vs, kb, offs, out):
         kb_got = keep.tile([P, B * N], F32, name="kb_got")
         nc.vector.tensor_copy(kb_got[:], kb_win[:].indirect(lists[:]))
         kb_col = keep.tile([P, B, PACK], F32, name="kb_col")
+        kb_mark = keep.tile([P, 1], F32, name="kb_mark", tag="middle", align_bytes=64)
         for b in range(B):
             bank = product_banks.tile([P, PACK, P], F32, name="product")
             for t in range(PACK):
                 nc.tensor.transpose(bank[:, t, :], kb_got[:, b * N + t : (b + 1) * N : PACK], identity[:])
             nc.scalar.copy(kb_col[:, b, :], bank[:, :, ROW])
+            if b == 1:
+                nc.scalar.copy(kb_mark[:], bank[:, 0, ROW : ROW + 1])
         vs_got = keep.tile([P, B * N], F32, name="vs_got")
         nc.vector.tensor_copy(vs_got[:], vs_win[:].indirect(lists[:]))
         bank = scale_bank.tile([P, P + 2 * B * PACK], F32, name="vs_turned")
@@ -129,6 +129,12 @@ def tile_attend_sigmoid_kernel(tc, qT, kT, vT, vs, kb, offs, out):
             )
 
         q_mixed = [keep.tile([P, NQ * PACK], BF16, name=f"q_mixed{b}", align_bytes=64) for b in range(B)]
+        k_mixed0 = keep.tile([P, N * PACK], BF16, name="k_mixed0", align_bytes=64)
+        k_mixed1 = [
+            keep.tile([P, 2 * GROUP], BF16, name=f"k_mixed1{half}", tag=("k_mixed10", "q_mixed0")[half], align_bytes=64)
+            for half in range(2)
+        ]
+        k_halves = [[k_mixed0[:, group(2 * half, 2)] for half in range(2)], [tile[:] for tile in k_mixed1]]
 
         def mix_views(b, first, count):
             return (
@@ -136,64 +142,75 @@ def tile_attend_sigmoid_kernel(tc, qT, kT, vT, vs, kb, offs, out):
                 q_raw[b][:, :, first : first + count].rearrange("p j (c i) -> p c j i", i=4),
             )
 
-        k_mixed = [
-            keep.tile([P, N * PACK], BF16, name=f"k_mixed{b}", tag=("k_mixed0", "q_mixed0")[b], align_bytes=64)
-            for b in range(B)
-        ]
+        def k_words(word):
+            return k_pairs[:].bitcast(word).rearrange("p (c b s t) -> p b s c t", c=2, b=B, t=PACK)
 
-        def deal_views(b, rows, word):
-            return (
-                k_mixed[b][:].bitcast(word).rearrange("p (t s c) -> p s c t", t=PACK, c=2)[:, rows],
-                k_pairs[:].bitcast(word).rearrange("p (c b s t) -> p b s c t", c=2, b=B, t=PACK)[:, b, rows],
+        for rows in (slice(0, P // 2), slice(P // 2, P)):
+            nc.scalar.copy(
+                k_mixed0[:].bitcast(U32).rearrange("p (t s c) -> p s c t", t=PACK, c=2)[:, rows], k_words(U32)[:, 0, rows]
             )
 
-        for half in range(2):
-            nc.scalar.copy(*deal_views(0, slice(half * P // 2, (half + 1) * P // 2), U32))
-        nc.vector.tensor_copy(*mix_views(0, 0, MIXED))
-        nc.scalar.activation(*mix_views(0, MIXED, NQ - MIXED), COPY)
-        nc.scalar.activation(*mix_views(1, 0, NQ), COPY)
+        def deal_views(half, word):
+            return (
+                k_mixed1[half][:].bitcast(word).rearrange("p (t s c) -> p s c t", t=2, c=2),
+                k_words(word)[:, 1, :, :, 2 * half : 2 * half + 2],
+            )
 
-        prob = []
-        for b in range(B):
-            if b == 1:
-                nc.vector.tensor_copy(*deal_views(b, slice(0, P), I32))
-            q_mx = mx_tiles(f"q{b}", NQ)
-            sigmoids = keep.tile([P, PACK, NQ], F32, name=f"prob{b}")
-            if b == 0:
-                k_mx = [mx_tiles("k0a", 2 * P), mx_tiles("k0b", 2 * P, codes_tag="q_raw0")]
-                k_cols = [0, 0]
-                quantise(k_mx[0], block(0, 2), k_mixed[0][:, group(0, 2)])
-            else:
-                k_mx = [mx_tiles("k1", N, codes_tag="q_raw1")] * 2
-                k_cols = [0, 2]
-            quantise(q_mx, slice(0, NQ), q_mixed[b][:])
-            for half in range(2):
-                if (b, half) != (0, 0):
-                    quantise(k_mx[half], block(k_cols[half], 2), k_mixed[b][:, group(2 * half, 2)])
-                for t in (2 * half, 2 * half + 1):
-                    score = product_banks.tile([P, NQ], F32, name="product")
-                    multiply(score[:], k_mx[half], block(k_cols[half] + t % 2), q_mx, slice(0, NQ))
-                    nc.scalar.activation(sigmoids[:, t, :], score[:], SIGMOID, bias=kb_col[:, b, t : t + 1])
-            prob.append(sigmoids)
+        nc.scalar.copy(*deal_views(0, U32))
+        nc.vector.tensor_copy(*mix_views(0, 0, 256))
+        nc.scalar.activation(*mix_views(1, 0, NQ - 0), COPY)
 
-        second = keep.tile([P, 3 * GROUP], BF16, name="second", align_bytes=64)
-        w1 = second[:, group(1, 2)]
+        q_mx = [mx_tiles(f"q{b}", NQ) for b in range(B)]
+        k_mx = [
+            [mx_tiles(f"k{b}{half}", 2 * P, codes_tag="q_raw1" if (b, half) == (1, 1) else None) for half in range(2)]
+            for b in range(B)
+        ]
+        prob = [keep.tile([P, PACK, NQ], F32, name=f"prob{b}") for b in range(B)]
 
-        def weigh(engine, scales, b, first_query, count, weights):
+        def quantise_keys(b, half):
+            quantise(k_mx[b][half], block(0, 2), k_halves[b][half])
+
+        def scores(b, half):
+            for t in (2 * half, 2 * half + 1):
+                score = product_banks.tile([P, NQ], F32, name="product")
+                multiply(score[:], k_mx[b][half], block(t % 2), q_mx[b], slice(0, NQ))
+                bias = kb_mark[:] if (b, t) == (1, 0) else kb_col[:, b, t : t + 1]
+                nc.scalar.activation(prob[b][:, t, :], score[:], SIGMOID, bias=bias)
+
+        quantise_keys(0, 0)
+        quantise(q_mx[0], slice(0, NQ), q_mixed[0][:])
+        scores(0, 0)
+        quantise_keys(0, 1)
+        scores(0, 1)
+        nc.vector.tensor_copy(*deal_views(1, I32))
+        quantise_keys(1, 0)
+        quantise(q_mx[1], slice(0, NQ), q_mixed[1][:])
+        scores(1, 0)
+        quantise_keys(1, 1)
+        scores(1, 1)
+
+        first = keep.tile([P, 2 * GROUP], BF16, name="first", align_bytes=64)
+        middle = keep.tile([P, 2 * GROUP], BF16, name="middle", align_bytes=64)
+        last = keep.tile([P, 2 * GROUP], BF16, name="last", align_bytes=64)
+        v10 = keep.tile([P, GROUP], BF16, name="v10", align_bytes=64)
+        v11 = keep.tile([P, GROUP], BF16, name="v11", align_bytes=64)
+
+        def weigh(engine, scales, b, h, weights):
             engine.tensor_tensor(
-                weights[:, PACK * first_query : PACK * (first_query + count)].rearrange(
-                    "p (c i t) -> p c t i", i=4, t=PACK
-                ),
-                prob[b][:, :, first_query : first_query + count].rearrange("p t (c i) -> p c t i", i=4),
-                scales[:, b, :].unsqueeze(1).unsqueeze(3).to_broadcast([P, count // 4, PACK, 4]),
+                weights.rearrange("p (c i t) -> p c t i", i=4, t=PACK),
+                prob[b][:, :, block(h)].rearrange("p t (c i) -> p c t i", i=4),
+                scales[:, b, :].unsqueeze(1).unsqueeze(3).to_broadcast([P, P // 4, PACK, 4]),
                 MULT,
             )
 
-        def values(k, b, got, interleaved, turns):
+        def turn(k, b, got, turns):
             nc.vector.tensor_copy(got.rearrange("p (u s i) -> p s u i", u=2, i=2), v_win[k][:].indirect(own_list[b]))
             turned = value_banks.tile([P, 2, P], F32, name="turned")
             for u, unit in turns:
                 nc.tensor.transpose(turned[:, u, :], got.bitcast(F32)[:, block(u)], unit[:])
+            return turned
+
+        def lay(interleaved, turned):
             nc.scalar.copy(
                 interleaved.bitcast(F32).rearrange("p (e u) -> p e u", u=2), turned[:].rearrange("p u e -> p e u")
             )
@@ -202,38 +219,35 @@ def tile_attend_sigmoid_kernel(tc, qT, kT, vT, vs, kb, offs, out):
             return keep.tile([P, N], BF16, name=name, align_bytes=64)[:]
 
         plain_turns = ((0, identity), (1, identity))
-        first = keep.tile([P, 4 * GROUP], BF16, name="first", tag="q_mixed0", align_bytes=64)
-        w0 = first[:, group(1, 2)]
-        weigh(nc.gpsimd, vs_sbuf, 0, 0, NQ - EARLY, w0)
+        weigh(nc.gpsimd, vs_sbuf, 0, 0, first[:, group(1)])
+        turned00 = turn(0, 0, own_tile("v_got00"), plain_turns)
+        turned01 = turn(0, 1, own_tile("v_got01"), plain_turns)
+        weigh(nc.vector, vs_psum, 0, 1, middle[:, group(0)])
+        weigh(nc.gpsimd, vs_sbuf, 1, 0, middle[:, group(1)])
         planes = keep.tile([P, PACK, P], BF16, name="planes")
         for t in range(PACK):
             nc.scalar.activation(planes[:, t, :], prob[1][:, t, P:], COPY, scale=vs_sbuf[:, 1, t : t + 1])
-        values(0, 0, own_tile("v_got00"), first[:, group(0)], plain_turns)
-        values(0, 1, own_tile("v_got01"), second[:, group(0)], plain_turns)
-        weigh(nc.vector, vs_psum, 0, NQ - EARLY, EARLY, w0)
-        weigh(nc.gpsimd, vs_sbuf, 1, 0, SECOND, w1)
-        values(1, 0, w1[:, GROUP - P : 2 * GROUP - P], first[:, group(3)], ((1, identity), (0, identity_late)))
+        lay(first[:, group(0)], turned00)
         nc.scalar.copy(
-            w1[:, group(1)].rearrange("p (c i t) -> p c t i", i=4, t=PACK),
+            last[:, group(1)].rearrange("p (c i t) -> p c t i", i=4, t=PACK),
             planes[:].rearrange("p t (c i) -> p c t i", i=4),
         )
-        v11 = keep.tile([P, GROUP], BF16, name="v11", align_bytes=64)
-        values(1, 1, own_tile("v_got11"), v11[:], plain_turns)
-        weigh(nc.vector, vs_psum, 1, SECOND, P - SECOND, w1)
+        lay(v10[:], turn(1, 0, last[:, group(0)], ((0, identity_late), (1, identity))))
+        lay(last[:, group(0)], turned01)
+        lay(v11[:], turn(1, 1, own_tile("v_got11"), plain_turns))
 
         mx = mx_tiles("mx", 8 * P, scales_tag="identity_late")
-        quantise(mx, block(0, 2), first[:, group(0, 2)])
-        quantise(mx, block(3), first[:, group(3)])
-        quantise(mx, block(2), first[:, group(2)])
-        quantise(mx, block(4, 2), second[:, group(0, 2)])
-        quantise(mx, block(7), second[:, group(2)])
-        quantise(mx, block(6), v11[:])
-        w_block = ((1, 2), (5, 7))
-        v_block = ((0, 3), (4, 6))
+        quantise(mx, block(0, 2), first[:])
+        quantise(mx, block(2, 2), middle[:])
+        quantise(mx, block(4), v10[:])
+        quantise(mx, block(5, 2), last[:])
+        quantise(mx, block(7), v11[:])
+        w_block = ((1, 2), (3, 6))
+        v_block = ((0, 5), (4, 7))
         results = [[keep.tile([P, DV], F32, name=f"result{b}{h}") for h in range(2)] for b in range(B)]
 
         def finish(b, h, k, bank, scale_out):
-            multiply(bank[:], mx, block(w_block[b][h]), mx, block(v_block[b][k]))
+            multiply(bank[:], mx, block(w_block[b][h]), mx, block(v_block[k][b]))
             scale_out(results[b][h][:, block(k)], bank[:])
             if k == 1:
                 nc.sync.dma_start(out=out[b, block(h), :], in_=results[b][h][:])
@@ -244,9 +258,10 @@ def tile_attend_sigmoid_kernel(tc, qT, kT, vT, vs, kb, offs, out):
         def by_vector(target, bank):
             nc.vector.tensor_scalar_mul(target, bank, OUT_SCALE)
 
-        for h in range(2):
-            for k in range(2):
-                finish(0, h, k, product_banks.tile([P, P], F32, name="product"), by_scalar)
+        finish(0, 0, 0, product_banks.tile([P, P], F32, name="product"), by_scalar)
+        finish(0, 1, 0, product_banks.tile([P, P], F32, name="product"), by_scalar)
+        finish(0, 0, 1, product_banks.tile([P, P], F32, name="product"), by_scalar)
+        finish(0, 1, 1, product_banks.tile([P, P], F32, name="product"), by_vector)
         finish(1, 0, 0, value_banks.tile([P, P], F32, name="turned"), by_vector)
         finish(1, 1, 0, value_banks.tile([P, P], F32, name="turned"), by_scalar)
         finish(1, 0, 1, value_banks.tile([P, P], F32, name="turned"), by_vector)

@@ -101,8 +101,12 @@ def tile_attend_sigmoid_kernel(tc, qT, kT, vT, vs, kb, offs, out):
 
         k_pairs = keep.tile([P, 2 * B * N * 2], BF16, name="k_pairs", align_bytes=64)
         pair_halves = k_pairs[:].rearrange("p (c i half) -> p c half i", c=2, half=2)
-        for j in range(PACK - 1):
-            nc.vector.tensor_copy(pair_halves[:, j // 2, j % 2], k_win[j][:].indirect(lists[:]))
+        for j in range(2):
+            nc.vector.tensor_copy(pair_halves[:, 0, j, :N], k_win[j][:].indirect(own_list[0]))
+            rounded = keep.tile([P, T], BF16, name=f"k_rounded{j}")
+            nc.scalar.activation(rounded[:], k_win[j][:], COPY)
+            nc.scalar.activation(pair_halves[:, 0, j, N:], rounded[:].indirect(own_list[1]), COPY)
+        nc.vector.tensor_copy(pair_halves[:, 1, 0], k_win[2][:].indirect(lists[:]))
         for first, count in ((0, N // 2), (N // 2, N // 2), (N, N)):
             nc.vector.tensor_copy(
                 pair_halves[:, 1, 1, first : first + count],
@@ -261,7 +265,7 @@ def tile_attend_sigmoid_kernel(tc, qT, kT, vT, vs, kb, offs, out):
         finish(0, 0, 0, product_banks.tile([P, P], F32, name="product"), by_scalar)
         finish(0, 1, 0, product_banks.tile([P, P], F32, name="product"), by_scalar)
         finish(0, 0, 1, product_banks.tile([P, P], F32, name="product"), by_scalar)
-        finish(0, 1, 1, product_banks.tile([P, P], F32, name="product"), by_vector)
+        finish(0, 1, 1, product_banks.tile([P, P], F32, name="product"), by_scalar)
         finish(1, 0, 0, value_banks.tile([P, P], F32, name="turned"), by_vector)
         finish(1, 1, 0, value_banks.tile([P, P], F32, name="turned"), by_scalar)
         finish(1, 0, 1, value_banks.tile([P, P], F32, name="turned"), by_vector)

@@ -228,6 +228,10 @@ def tile_attend_sigmoid_kernel(tc, qT, kT, vT, vs, kb, offs, out):
         turned01 = turn(0, 1, own_tile("v_got01"), plain_turns)
         weigh(nc.vector, vs_psum, 0, 1, middle[:, group(0)])
         weigh(nc.gpsimd, vs_sbuf, 1, 0, middle[:, group(1)])
+        idle = scale_bank.tile([P, 2 * NQ], F32, name="vs_turned")
+        for n in range(3):
+            multiply(idle[:, (n % 2) * NQ : (n % 2 + 1) * NQ], k_mx[1][1], block(0), q_mx[1], slice(0, NQ))
+
         planes = keep.tile([P, PACK, P], BF16, name="planes")
         for t in range(PACK):
             nc.scalar.activation(planes[:, t, :], prob[1][:, t, P:], COPY, scale=vs_sbuf[:, 1, t : t + 1])

@@ -80,37 +80,52 @@ def tile_attend_sigmoid_kernel(tc, qT, kT, vT, vs, kb, offs, out):
 
         kb_got = keep.tile([P, B * N], F32, name="kb_got")
         nc.vector.tensor_copy(kb_got[:], kb_win[:].indirect(lists[:]))
+
+        def by_place(name, got):
+            dealt = keep.tile([P, B, PACK, P], F32, name=name)
+            for b in range(B):
+                nc.gpsimd.tensor_copy(
+                    dealt[:, b].rearrange("p t (m r) -> p m t r", r=4),
+                    got[:, b * N : (b + 1) * N].rearrange("p (m t r) -> p m t r", t=PACK, r=4),
+                )
+            return dealt
+
+        kb_dealt = by_place("kb_dealt", kb_got)
         kb_col = keep.tile([P, B, PACK], F32, name="kb_col")
         kb_mark = keep.tile([P, 1], F32, name="kb_mark", tag="middle", align_bytes=64)
         for b in range(B):
             bank = product_banks.tile([P, PACK, P], F32, name="product")
             for t in range(PACK):
-                nc.tensor.transpose(bank[:, t, :], kb_got[:, b * N + t : (b + 1) * N : PACK], identity[:])
+                nc.tensor.transpose(bank[:, t, :], kb_dealt[:, b, t, :], identity[:])
             nc.scalar.copy(kb_col[:, b, :], bank[:, :, ROW])
             if b == 1:
                 nc.scalar.copy(kb_mark[:], bank[:, 0, ROW : ROW + 1])
         vs_got = keep.tile([P, B * N], F32, name="vs_got")
         nc.vector.tensor_copy(vs_got[:], vs_win[:].indirect(lists[:]))
+        vs_dealt = by_place("vs_dealt", vs_got)
         bank = scale_bank.tile([P, P + 2 * B * PACK], F32, name="vs_turned")
         for n in reversed(range(B * PACK)):
             b, t = divmod(n, PACK)
-            nc.tensor.transpose(bank[:, 2 * n : 2 * n + P], vs_got[:, b * N + t : (b + 1) * N : PACK], identity[:])
+            nc.tensor.transpose(bank[:, 2 * n : 2 * n + P], vs_dealt[:, b, t, :], identity[:])
         vs_psum = bank[:, ROW : ROW + 2 * B * PACK : 2].rearrange("p (b t) -> p b t", b=B)
         vs_sbuf = keep.tile([P, B, PACK], F32, name="vs_sbuf")
         nc.scalar.copy(vs_sbuf[:], vs_psum)
 
         k_pairs = keep.tile([P, 2 * B * N * 2], BF16, name="k_pairs", align_bytes=64)
-        pair_halves = k_pairs[:].rearrange("p (c i half) -> p c half i", c=2, half=2)
+        pair_halves = k_pairs[:].rearrange("p (c t m r half) -> p c half m t r", c=2, t=PACK, r=4, half=2)
+
+        def places(j, first, count):
+            return pair_halves[:, j // 2, j % 2, first // 16 : (first + count) // 16]
+
         for j in range(2):
-            nc.vector.tensor_copy(pair_halves[:, 0, j, :N], k_win[j][:].indirect(own_list[0]))
+            nc.vector.tensor_copy(places(j, 0, N), k_win[j][:].indirect(own_list[0]))
             rounded = keep.tile([P, T], BF16, name=f"k_rounded{j}")
             nc.scalar.activation(rounded[:], k_win[j][:], COPY)
-            nc.scalar.activation(pair_halves[:, 0, j, N:], rounded[:].indirect(own_list[1]), COPY)
-        nc.vector.tensor_copy(pair_halves[:, 1, 0], k_win[2][:].indirect(lists[:]))
+            nc.scalar.activation(places(j, N, N), rounded[:].indirect(own_list[1]), COPY)
+        nc.vector.tensor_copy(places(2, 0, B * N), k_win[2][:].indirect(lists[:]))
         for first, count in ((0, N // 2), (N // 2, N // 2), (N, N)):
             nc.vector.tensor_copy(
-                pair_halves[:, 1, 1, first : first + count],
-                k_win[PACK - 1][:].indirect(lists[:, first // 16 : (first + count) // 16]),
+                places(3, first, count), k_win[3][:].indirect(lists[:, first // 16 : (first + count) // 16])
             )
 
         def mx_tiles(name, width, codes_tag=None, scales_tag=None):
@@ -133,12 +148,11 @@ def tile_attend_sigmoid_kernel(tc, qT, kT, vT, vs, kb, offs, out):
             )
 
         q_mixed = [keep.tile([P, NQ * PACK], BF16, name=f"q_mixed{b}", align_bytes=64) for b in range(B)]
-        k_mixed0 = keep.tile([P, N * PACK], BF16, name="k_mixed0", align_bytes=64)
-        k_mixed1 = [
-            keep.tile([P, 2 * GROUP], BF16, name=f"k_mixed1{half}", tag=("k_mixed10", "q_mixed0")[half], align_bytes=64)
-            for half in range(2)
+        k_mixed = [
+            keep.tile([P, N * PACK], BF16, name=f"k_mixed{b}", tag=("k_mixed0", "q_raw0")[b], align_bytes=64)
+            for b in range(B)
         ]
-        k_halves = [[k_mixed0[:, group(2 * half, 2)] for half in range(2)], [tile[:] for tile in k_mixed1]]
+        k_halves = [[k_mixed[b][:, group(2 * half, 2)] for half in range(2)] for b in range(B)]
 
         def mix_views(b, first, count):
             return (
@@ -146,23 +160,16 @@ def tile_attend_sigmoid_kernel(tc, qT, kT, vT, vs, kb, offs, out):
                 q_raw[b][:, :, first : first + count].rearrange("p j (c i) -> p c j i", i=4),
             )
 
-        def k_words(word):
-            return k_pairs[:].bitcast(word).rearrange("p (c b s t) -> p b s c t", c=2, b=B, t=PACK)
-
-        for rows in (slice(0, P // 2), slice(P // 2, P)):
-            nc.scalar.copy(
-                k_mixed0[:].bitcast(U32).rearrange("p (t s c) -> p s c t", t=PACK, c=2)[:, rows], k_words(U32)[:, 0, rows]
-            )
-
-        def deal_views(half, word):
+        def weave_views(b, tiles, rows, word):
             return (
-                k_mixed1[half][:].bitcast(word).rearrange("p (t s c) -> p s c t", t=2, c=2),
-                k_words(word)[:, 1, :, :, 2 * half : 2 * half + 2],
+                k_mixed[b][:].bitcast(word).rearrange("p (t m r c) -> p t m c r", t=PACK, r=4, c=2)[:, tiles, rows],
+                k_pairs[:].bitcast(word).rearrange("p (c t b m r) -> p b t m c r", c=2, t=PACK, b=B, r=4)[:, b, tiles, rows],
             )
 
-        nc.scalar.copy(*deal_views(0, U32))
-        nc.vector.tensor_copy(*mix_views(0, 0, 256))
-        nc.scalar.activation(*mix_views(1, 0, NQ - 0), COPY)
+        nc.scalar.copy(*weave_views(0, slice(0, PACK), slice(0, 16), U32))
+        nc.gpsimd.tensor_copy(*weave_views(0, slice(0, PACK), slice(16, 32), U32))
+        for b in range(B):
+            nc.scalar.activation(*mix_views(b, 0, NQ), COPY)
 
         q_mx = [mx_tiles(f"q{b}", NQ) for b in range(B)]
         k_mx = [
@@ -182,11 +189,12 @@ def tile_attend_sigmoid_kernel(tc, qT, kT, vT, vs, kb, offs, out):
                 nc.scalar.activation(prob[b][:, t, :], score[:], SIGMOID, bias=bias)
 
         quantise_keys(0, 0)
+        quantise_keys(0, 1)
         quantise(q_mx[0], slice(0, NQ), q_mixed[0][:])
         scores(0, 0)
-        quantise_keys(0, 1)
         scores(0, 1)
-        nc.vector.tensor_copy(*deal_views(1, I32))
+        for half in range(2):
+            nc.vector.tensor_copy(*weave_views(1, slice(2 * half, 2 * half + 2), slice(0, 32), I32))
         quantise_keys(1, 0)
         quantise(q_mx[1], slice(0, NQ), q_mixed[1][:])
         scores(1, 0)
@@ -208,7 +216,7 @@ def tile_attend_sigmoid_kernel(tc, qT, kT, vT, vs, kb, offs, out):
             )
 
         def turn(k, b, got, turns):
-            nc.vector.tensor_copy(got.rearrange("p (u s i) -> p s u i", u=2, i=2), v_win[k][:].indirect(own_list[b]))
+            nc.vector.tensor_copy(got.rearrange("p (u m r i) -> p m u i r", u=2, r=4, i=2), v_win[k][:].indirect(own_list[b]))
             turned = value_banks.tile([P, 2, P], F32, name="turned")
             for u, unit in turns:
                 nc.tensor.transpose(turned[:, u, :], got.bitcast(F32)[:, block(u)], unit[:])

@@ -9,7 +9,6 @@ PACK = 4
 LIST_COLS = N // 16
 GROUP = P * PACK
 ROW = P - 1
-HEAD = 512
 OUT_SCALE = 1.0 / 16.0
 FLOPS = 2 * B * NQ * N * (D + DV)
 BYTES = 4 * (B * D * NQ + D * T + DV * T + 2 * T + B * NQ * DV) + 2 * P * B * LIST_COLS
@@ -52,9 +51,8 @@ def tile_attend_sigmoid_kernel(tc, qT, kT, vT, vs, kb, offs, out):
 
         k_rows = kT.rearrange("(p j) n -> j p n", j=PACK)
         k_win = [keep.tile([P, T], F32, name=f"k_win{j}") for j in range(PACK)]
-        nc.sync.dma_start(out=k_win[0][:, :HEAD], in_=k_rows[0][:, :HEAD])
+        nc.sync.dma_start(out=k_win[0][:], in_=k_rows[0])
         nc.sync.dma_start(lists[:], offs)
-        nc.sync.dma_start(out=k_win[0][:, HEAD:], in_=k_rows[0][:, HEAD:])
         for j in range(1, PACK):
             nc.sync.dma_start(out=k_win[j][:], in_=k_rows[j])
         q_rows = qT.rearrange("b (p j) q -> b p j q", j=PACK)

@@ -89,15 +89,12 @@ def tile_attend_sigmoid_kernel(tc, qT, kT, vT, vs, kb, offs, out):
             return dealt
 
         kb_dealt = by_place("kb_dealt", kb_got)
-        kb_col = keep.tile([P, B, PACK], F32, name="kb_col")
-        kb_mark = keep.tile([P, 1], F32, name="kb_mark", tag="middle", align_bytes=64)
+        kb_banks = []
         for b in range(B):
             bank = product_banks.tile([P, PACK, P], F32, name="product")
             for t in range(PACK):
                 nc.tensor.transpose(bank[:, t, :], kb_dealt[:, b, t, :], identity[:])
-            nc.scalar.copy(kb_col[:, b, :], bank[:, :, ROW])
-            if b == 1:
-                nc.scalar.copy(kb_mark[:], bank[:, 0, ROW : ROW + 1])
+            kb_banks.append(bank)
         vs_got = keep.tile([P, B * N], F32, name="vs_got")
         nc.vector.tensor_copy(vs_got[:], vs_win[:].indirect(lists[:]))
         vs_dealt = by_place("vs_dealt", vs_got)
@@ -106,8 +103,6 @@ def tile_attend_sigmoid_kernel(tc, qT, kT, vT, vs, kb, offs, out):
             b, t = divmod(n, PACK)
             nc.tensor.transpose(bank[:, 2 * n : 2 * n + P], vs_dealt[:, b, t, :], identity[:])
         vs_psum = bank[:, ROW : ROW + 2 * B * PACK : 2].rearrange("p (b t) -> p b t", b=B)
-        vs_sbuf = keep.tile([P, B, PACK], F32, name="vs_sbuf")
-        nc.scalar.copy(vs_sbuf[:], vs_psum)
 
         k_pairs = keep.tile([P, 2 * B * N * 2], BF16, name="k_pairs", align_bytes=64)
         pair_halves = k_pairs[:].rearrange("p (c t m r half) -> p c half m t r", c=2, t=PACK, r=4, half=2)
@@ -125,6 +120,14 @@ def tile_attend_sigmoid_kernel(tc, qT, kT, vT, vs, kb, offs, out):
             nc.vector.tensor_copy(
                 places(3, first, count), k_win[3][:].indirect(lists[:, first // 16 : (first + count) // 16])
             )
+
+        columns = keep.tile([P, 2, B, PACK], F32, name="columns", tag="k_rounded1")
+        kb_col, vs_sbuf = columns[:, 0], columns[:, 1]
+        kb_mark = keep.tile([P, 1], F32, name="kb_mark", tag="middle", align_bytes=64)
+        for b in range(B):
+            nc.scalar.copy(kb_col[:, b, :], kb_banks[b][:, :, ROW])
+        nc.scalar.copy(vs_sbuf, vs_psum)
+        nc.scalar.copy(kb_mark[:], kb_col[:, 1, 0:1])
 
         def mx_tiles(name, width, codes_tag=None, scales_tag=None):
             codes = keep.tile([P, width], U32, name=f"{name}_codes", tag=codes_tag or f"{name}_codes", align_bytes=64)

@@ -276,9 +276,12 @@ def tile_attend_sigmoid_kernel(tc, qT, kT, vT, vs, kb, offs, out):
             nc.vector.tensor_scalar_mul(target, bank, OUT_SCALE)
 
         finish(0, 0, 0, product_banks.tile([P, P], F32, name="product"), by_scalar)
-        finish(0, 1, 0, product_banks.tile([P, P], F32, name="product"), by_scalar)
+        both = product_banks.tile([P, DV], F32, name="product")
+        multiply(both[:, block(0)], mx, block(w_block[0][1]), mx, block(v_block[0][0]))
         finish(0, 0, 1, product_banks.tile([P, P], F32, name="product"), by_scalar)
-        finish(0, 1, 1, product_banks.tile([P, P], F32, name="product"), by_scalar)
+        multiply(both[:, block(1)], mx, block(w_block[0][1]), mx, block(v_block[1][0]))
+        by_scalar(results[0][1][:], both[:])
+        nc.sync.dma_start(out=out[0, block(1), :], in_=results[0][1][:])
         finish(1, 0, 0, value_banks.tile([P, P], F32, name="turned"), by_vector)
         finish(1, 1, 0, value_banks.tile([P, P], F32, name="turned"), by_scalar)
         finish(1, 0, 1, value_banks.tile([P, P], F32, name="turned"), by_vector)

@@ -9,6 +9,7 @@ PACK = 4
 LIST_COLS = N // 16
 GROUP = P * PACK
 ROW = P - 1
+EARLY = 176
 OUT_SCALE = 1.0 / 16.0
 FLOPS = 2 * B * NQ * N * (D + DV)
 BYTES = 4 * (B * D * NQ + D * T + DV * T + 2 * T + B * NQ * DV) + 2 * P * B * LIST_COLS
@@ -123,11 +124,12 @@ def tile_attend_sigmoid_kernel(tc, qT, kT, vT, vs, kb, offs, out):
 
         columns = keep.tile([P, 2, B, PACK], F32, name="columns", tag="k_rounded1")
         kb_col, vs_sbuf = columns[:, 0], columns[:, 1]
-        kb_mark = keep.tile([P, 1], F32, name="kb_mark", tag="middle", align_bytes=64)
+        early = keep.tile([P, 4 * GROUP], BF16, name="early", align_bytes=64)
+        kb_mark = early[:, 3 * GROUP - 2 : 3 * GROUP].bitcast(F32)
         for b in range(B):
             nc.scalar.copy(kb_col[:, b, :], kb_banks[b][:, :, ROW])
         nc.scalar.copy(vs_sbuf, vs_psum)
-        nc.scalar.copy(kb_mark[:], kb_col[:, 1, 0:1])
+        nc.scalar.copy(kb_mark, kb_col[:, 1, 0:1])
 
         def mx_tiles(name, width, codes_tag=None, scales_tag=None):
             codes = keep.tile([P, width], U32, name=f"{name}_codes", tag=codes_tag or f"{name}_codes", align_bytes=64)
@@ -186,7 +188,7 @@ def tile_attend_sigmoid_kernel(tc, qT, kT, vT, vs, kb, offs, out):
             for t in (2 * half, 2 * half + 1):
                 score = product_banks.tile([P, NQ], F32, name="product")
                 multiply(score[:], k_mx[b][half], block(t % 2), q_mx[b], slice(0, NQ))
-                bias = kb_mark[:] if (b, t) == (1, 0) else kb_col[:, b, t : t + 1]
+                bias = kb_mark if (b, t) == (1, 0) else kb_col[:, b, t : t + 1]
                 nc.scalar.activation(prob[b][:, t, :], score[:], SIGMOID, bias=bias)
 
         quantise_keys(0, 0)
@@ -202,17 +204,16 @@ def tile_attend_sigmoid_kernel(tc, qT, kT, vT, vs, kb, offs, out):
         quantise_keys(1, 1)
         scores(1, 1)
 
-        first = keep.tile([P, 2 * GROUP], BF16, name="first", align_bytes=64)
-        middle = keep.tile([P, 2 * GROUP], BF16, name="middle", align_bytes=64)
         last = keep.tile([P, 2 * GROUP], BF16, name="last", align_bytes=64)
         v10 = keep.tile([P, GROUP], BF16, name="v10", align_bytes=64)
         v11 = keep.tile([P, GROUP], BF16, name="v11", align_bytes=64)
 
-        def weigh(engine, scales, b, h, weights):
+        def weigh(engine, scales, b, first, count):
+            start = GROUP + PACK * (b * NQ + first)
             engine.tensor_tensor(
-                weights.rearrange("p (c i t) -> p c t i", i=4, t=PACK),
-                prob[b][:, :, block(h)].rearrange("p t (c i) -> p c t i", i=4),
-                scales[:, b, :].unsqueeze(1).unsqueeze(3).to_broadcast([P, P // 4, PACK, 4]),
+                early[:, start : start + PACK * count].rearrange("p (c i t) -> p c t i", i=4, t=PACK),
+                prob[b][:, :, first : first + count].rearrange("p t (c i) -> p c t i", i=4),
+                scales[:, b, :].unsqueeze(1).unsqueeze(3).to_broadcast([P, count // 4, PACK, 4]),
                 MULT,
             )
 
@@ -232,11 +233,11 @@ def tile_attend_sigmoid_kernel(tc, qT, kT, vT, vs, kb, offs, out):
             return keep.tile([P, N], BF16, name=name, align_bytes=64)[:]
 
         plain_turns = ((0, identity), (1, identity))
-        weigh(nc.gpsimd, vs_sbuf, 0, 0, first[:, group(1)])
+        weigh(nc.gpsimd, vs_sbuf, 0, 0, NQ - EARLY)
         turned00 = turn(0, 0, own_tile("v_got00"), plain_turns)
         turned01 = turn(0, 1, own_tile("v_got01"), plain_turns)
-        weigh(nc.vector, vs_psum, 0, 1, middle[:, group(0)])
-        weigh(nc.gpsimd, vs_sbuf, 1, 0, middle[:, group(1)])
+        weigh(nc.vector, vs_psum, 0, NQ - EARLY, EARLY)
+        weigh(nc.gpsimd, vs_sbuf, 1, 0, P)
         idle = scale_bank.tile([P, 2 * NQ], F32, name="vs_turned")
         for n in range(3):
             multiply(idle[:, (n % 2) * NQ : (n % 2 + 1) * NQ], k_mx[1][1], block(0), q_mx[1], slice(0, NQ))
@@ -244,7 +245,7 @@ def tile_attend_sigmoid_kernel(tc, qT, kT, vT, vs, kb, offs, out):
         planes = keep.tile([P, PACK, P], BF16, name="planes")
         for t in range(PACK):
             nc.scalar.activation(planes[:, t, :], prob[1][:, t, P:], COPY, scale=vs_sbuf[:, 1, t : t + 1])
-        lay(first[:, group(0)], turned00)
+        lay(early[:, group(0)], turned00)
         nc.scalar.copy(
             last[:, group(1)].rearrange("p (c i t) -> p c t i", i=4, t=PACK),
             planes[:].rearrange("p t (c i) -> p c t i", i=4),
@@ -254,8 +255,8 @@ def tile_attend_sigmoid_kernel(tc, qT, kT, vT, vs, kb, offs, out):
         lay(v11[:], turn(1, 1, own_tile("v_got11"), plain_turns))
 
         mx = mx_tiles("mx", 8 * P, scales_tag="identity_late")
-        quantise(mx, block(0, 2), first[:])
-        quantise(mx, block(2, 2), middle[:])
+        quantise(mx, block(0, 2), early[:, group(0, 2)])
+        quantise(mx, block(2, 2), early[:, group(2, 2)])
         quantise(mx, block(4), v10[:])
         quantise(mx, block(5, 2), last[:])
         quantise(mx, block(7), v11[:])

@@ -38,8 +38,11 @@ def tile_attend_sigmoid_kernel(tc, qT, kT, vT, vs, kb, offs, out):
     nc = tc.nc
     with ExitStack() as ctx:
         keep = ctx.enter_context(tc.tile_pool(name="keep", bufs=1))
-        product_banks = ctx.enter_context(tc.psum_pool(name="product_banks", bufs=4))
-        value_banks = ctx.enter_context(tc.psum_pool(name="value_banks", bufs=3))
+        banks = ctx.enter_context(tc.psum_pool(name="banks", bufs=1))
+
+        def in_bank(n, shape):
+            return banks.tile(shape, F32, name=f"bank{n}")
+
         scale_bank = ctx.enter_context(tc.psum_pool(name="scale_bank", bufs=1))
 
         lists = keep.tile([P, B * LIST_COLS], U16, name="lists")
@@ -92,7 +95,7 @@ def tile_attend_sigmoid_kernel(tc, qT, kT, vT, vs, kb, offs, out):
         kb_dealt = by_place("kb_dealt", kb_got)
         kb_banks = []
         for b in range(B):
-            bank = product_banks.tile([P, PACK, P], F32, name="product")
+            bank = in_bank(b, [P, PACK, P])
             for t in range(PACK):
                 nc.tensor.transpose(bank[:, t, :], kb_dealt[:, b, t, :], identity[:])
             kb_banks.append(bank)
@@ -186,7 +189,7 @@ def tile_attend_sigmoid_kernel(tc, qT, kT, vT, vs, kb, offs, out):
 
         def scores(b, half):
             for t in (2 * half, 2 * half + 1):
-                score = product_banks.tile([P, NQ], F32, name="product")
+                score = in_bank(t, [P, NQ])
                 multiply(score[:], k_mx[b][half], block(t % 2), q_mx[b], slice(0, NQ))
                 bias = kb_mark if (b, t) == (1, 0) else kb_col[:, b, t : t + 1]
                 nc.scalar.activation(prob[b][:, t, :], score[:], SIGMOID, bias=bias)
@@ -219,7 +222,7 @@ def tile_attend_sigmoid_kernel(tc, qT, kT, vT, vs, kb, offs, out):
 
         def turn(k, b, got, turns):
             nc.vector.tensor_copy(got.rearrange("p (u m r i) -> p m u i r", u=2, r=4, i=2), v_win[k][:].indirect(own_list[b]))
-            turned = value_banks.tile([P, 2, P], F32, name="turned")
+            turned = in_bank(((4, 5), (6, 4))[k][b], [P, 2, P])
             for u, unit in turns:
                 nc.tensor.transpose(turned[:, u, :], got.bitcast(F32)[:, block(u)], unit[:])
             return turned
@@ -235,7 +238,15 @@ def tile_attend_sigmoid_kernel(tc, qT, kT, vT, vs, kb, offs, out):
         plain_turns = ((0, identity), (1, identity))
         weigh(nc.gpsimd, vs_sbuf, 0, 0, NQ - EARLY)
         turned00 = turn(0, 0, own_tile("v_got00"), plain_turns)
-        turned01 = turn(0, 1, own_tile("v_got01"), plain_turns)
+        got01 = own_tile("v_got01")
+        turned01 = turn(0, 1, got01, plain_turns)
+        resting = in_bank(0, [P, P])
+
+        def spare_turns(count, source):
+            for n in range(count):
+                nc.tensor.transpose(resting[:], source.bitcast(F32)[:, block(0)], identity[:])
+
+        spare_turns(3, got01)
         weigh(nc.vector, vs_psum, 0, NQ - EARLY, EARLY)
         weigh(nc.gpsimd, vs_sbuf, 1, 0, P)
         idle = scale_bank.tile([P, 2 * NQ], F32, name="vs_turned")
@@ -251,6 +262,7 @@ def tile_attend_sigmoid_kernel(tc, qT, kT, vT, vs, kb, offs, out):
             planes[:].rearrange("p t (c i) -> p c t i", i=4),
         )
         lay(v10[:], turn(1, 0, last[:, group(0)], ((0, identity_late), (1, identity))))
+        spare_turns(2, last[:, group(0)])
         lay(last[:, group(0)], turned01)
         lay(v11[:], turn(1, 1, own_tile("v_got11"), plain_turns))
 
@@ -276,14 +288,14 @@ def tile_attend_sigmoid_kernel(tc, qT, kT, vT, vs, kb, offs, out):
         def by_vector(target, bank):
             nc.vector.tensor_scalar_mul(target, bank, OUT_SCALE)
 
-        finish(0, 0, 0, product_banks.tile([P, P], F32, name="product"), by_scalar)
-        both = product_banks.tile([P, DV], F32, name="product")
+        finish(0, 0, 0, in_bank(0, [P, P]), by_scalar)
+        both = in_bank(1, [P, DV])
         multiply(both[:, block(0)], mx, block(w_block[0][1]), mx, block(v_block[0][0]))
-        finish(0, 0, 1, product_banks.tile([P, P], F32, name="product"), by_scalar)
+        finish(0, 0, 1, in_bank(2, [P, P]), by_scalar)
         multiply(both[:, block(1)], mx, block(w_block[0][1]), mx, block(v_block[1][0]))
         by_scalar(results[0][1][:], both[:])
         nc.sync.dma_start(out=out[0, block(1), :], in_=results[0][1][:])
-        finish(1, 0, 0, value_banks.tile([P, P], F32, name="turned"), by_vector)
-        finish(1, 1, 0, value_banks.tile([P, P], F32, name="turned"), by_scalar)
-        finish(1, 0, 1, value_banks.tile([P, P], F32, name="turned"), by_vector)
-        finish(1, 1, 1, product_banks.tile([P, P], F32, name="product"), by_scalar)
+        finish(1, 0, 0, in_bank(3, [P, P]), by_vector)
+        finish(1, 1, 0, in_bank(6, [P, P]), by_scalar)
+        finish(1, 0, 1, in_bank(4, [P, P]), by_vector)
+        finish(1, 1, 1, in_bank(5, [P, P]), by_scalar)

@@ -246,7 +246,7 @@ def tile_attend_sigmoid_kernel(tc, qT, kT, vT, vs, kb, offs, out):
             for n in range(count):
                 nc.tensor.transpose(resting[:], source.bitcast(F32)[:, block(0)], identity[:])
 
-        spare_turns(3, got01)
+        spare_turns(5, got01)
         weigh(nc.vector, vs_psum, 0, NQ - EARLY, EARLY)
         weigh(nc.gpsimd, vs_sbuf, 1, 0, P)
         idle = scale_bank.tile([P, 2 * NQ], F32, name="vs_turned")
@@ -262,7 +262,7 @@ def tile_attend_sigmoid_kernel(tc, qT, kT, vT, vs, kb, offs, out):
             planes[:].rearrange("p t (c i) -> p c t i", i=4),
         )
         lay(v10[:], turn(1, 0, last[:, group(0)], ((0, identity_late), (1, identity))))
-        spare_turns(2, last[:, group(0)])
+        spare_turns(3, last[:, group(0)])
         lay(last[:, group(0)], turned01)
         lay(v11[:], turn(1, 1, own_tile("v_got11"), plain_turns))
 

@@ -279,7 +279,9 @@ def tile_attend_sigmoid_kernel(tc, qT, kT, vT, vs, kb, offs, out):
         def finish(b, h, k, bank, scale_out):
             multiply(bank[:], mx, block(w_block[b][h]), mx, block(v_block[k][b]))
             scale_out(results[b][h][:, block(k)], bank[:])
-            if k == 1:
+            if b == 0:
+                nc.sync.dma_start(out=out[b, block(h), block(k)], in_=results[b][h][:, block(k)])
+            elif k == 1:
                 nc.sync.dma_start(out=out[b, block(h), :], in_=results[b][h][:])
 
         def by_scalar(target, bank):

@@ -268,7 +268,8 @@ def tile_attend_sigmoid_kernel(tc, qT, kT, vT, vs, kb, offs, out):
 
         mx = mx_tiles("mx", 8 * P, scales_tag="identity_late")
         quantise(mx, block(0, 2), early[:, group(0, 2)])
-        quantise(mx, block(2, 2), early[:, group(2, 2)])
+        quantise(mx, block(2), early[:, group(2)])
+        quantise(mx, block(3), early[:, group(3)])
         quantise(mx, block(4), v10[:])
         quantise(mx, block(5, 2), last[:])
         quantise(mx, block(7), v11[:])
@@ -291,13 +292,10 @@ def tile_attend_sigmoid_kernel(tc, qT, kT, vT, vs, kb, offs, out):
             nc.vector.tensor_scalar_mul(target, bank, OUT_SCALE)
 
         finish(0, 0, 0, in_bank(0, [P, P]), by_scalar)
-        both = in_bank(1, [P, DV])
-        multiply(both[:, block(0)], mx, block(w_block[0][1]), mx, block(v_block[0][0]))
+        finish(0, 1, 0, in_bank(1, [P, P]), by_scalar)
         finish(0, 0, 1, in_bank(2, [P, P]), by_scalar)
-        multiply(both[:, block(1)], mx, block(w_block[0][1]), mx, block(v_block[1][0]))
-        by_scalar(results[0][1][:], both[:])
-        nc.sync.dma_start(out=out[0, block(1), :], in_=results[0][1][:])
-        finish(1, 0, 0, in_bank(3, [P, P]), by_vector)
-        finish(1, 1, 0, in_bank(6, [P, P]), by_scalar)
+        finish(0, 1, 1, in_bank(3, [P, P]), by_scalar)
+        finish(1, 0, 0, in_bank(6, [P, P]), by_vector)
+        finish(1, 1, 0, in_bank(5, [P, P]), by_scalar)
         finish(1, 0, 1, in_bank(4, [P, P]), by_vector)
-        finish(1, 1, 1, in_bank(5, [P, P]), by_scalar)
+        finish(1, 1, 1, in_bank(0, [P, P]), by_scalar)

@@ -269,8 +269,9 @@ def tile_attend_sigmoid_kernel(tc, qT, kT, vT, vs, kb, offs, out):
         mx = mx_tiles("mx", 8 * P, scales_tag="identity_late")
         quantise(mx, block(0, 2), early[:, group(0, 2)])
         quantise(mx, block(2), early[:, group(2)])
-        quantise(mx, block(3), early[:, group(3)])
         quantise(mx, block(4), v10[:])
+        w10_mx = mx_tiles("w10", P, codes_tag="v_got11")
+        quantise(w10_mx, block(0), early[:, group(3)])
         quantise(mx, block(5, 2), last[:])
         quantise(mx, block(7), v11[:])
         w_block = ((1, 2), (3, 6))
@@ -278,9 +279,12 @@ def tile_attend_sigmoid_kernel(tc, qT, kT, vT, vs, kb, offs, out):
         results = [[keep.tile([P, DV], F32, name=f"result{b}{h}") for h in range(2)] for b in range(B)]
 
         def finish(b, h, k, bank, scale_out):
-            multiply(bank[:], mx, block(w_block[b][h]), mx, block(v_block[k][b]))
+            if (b, h) == (1, 0):
+                multiply(bank[:], w10_mx, block(0), mx, block(v_block[k][b]))
+            else:
+                multiply(bank[:], mx, block(w_block[b][h]), mx, block(v_block[k][b]))
             scale_out(results[b][h][:, block(k)], bank[:])
-            if b == 0:
+            if (b, h) == (0, 0):
                 nc.sync.dma_start(out=out[b, block(h), block(k)], in_=results[b][h][:, block(k)])
             elif k == 1:
                 nc.sync.dma_start(out=out[b, block(h), :], in_=results[b][h][:])

@@ -79,6 +79,8 @@ def tile_attend_sigmoid_kernel(tc, qT, kT, vT, vs, kb, offs, out):
         make_identity(nc, identity[:])
         identity_late = keep.tile([P, P], F32, name="identity_late", align_bytes=64)
         nc.scalar.copy(identity_late[:], identity[:])
+        identity_last = keep.tile([P, P], F32, name="identity_last", align_bytes=64)
+        nc.scalar.copy(identity_last[:], identity[:])
 
         kb_got = keep.tile([P, B * N], F32, name="kb_got")
         nc.vector.tensor_copy(kb_got[:], kb_win[:].indirect(lists[:]))
@@ -264,13 +266,13 @@ def tile_attend_sigmoid_kernel(tc, qT, kT, vT, vs, kb, offs, out):
         lay(v10[:], turn(1, 0, last[:, group(0)], ((0, identity_late), (1, identity))))
         spare_turns(3, last[:, group(0)])
         lay(last[:, group(0)], turned01)
-        lay(v11[:], turn(1, 1, own_tile("v_got11"), plain_turns))
+        lay(v11[:], turn(1, 1, own_tile("v_got11"), ((0, identity_last), (1, identity))))
 
         mx = mx_tiles("mx", 8 * P, scales_tag="identity_late")
         quantise(mx, block(0, 2), early[:, group(0, 2)])
         quantise(mx, block(2), early[:, group(2)])
         quantise(mx, block(4), v10[:])
-        w10_mx = mx_tiles("w10", P, codes_tag="v_got11")
+        w10_mx = mx_tiles("w10", P, scales_tag="identity_last")
         quantise(w10_mx, block(0), early[:, group(3)])
         quantise(mx, block(5, 2), last[:])
         quantise(mx, block(7), v11[:])

@@ -6,10 +6,14 @@ from concourse.masks import make_identity
 B, NQ, D, DV, N, T = 2, 256, 512, 256, 512, 2048
 P = 128
 PACK = 4
-LIST_COLS = N // 16
+RUN = 4
+SPAN = PACK * RUN
+LIST_COLS = N // SPAN
 GROUP = P * PACK
 ROW = P - 1
 EARLY = 176
+SPARE_PASSES = 3
+SPARE_TURNS = (5, 3)
 OUT_SCALE = 1.0 / 16.0
 FLOPS = 2 * B * NQ * N * (D + DV)
 BYTES = 4 * (B * D * NQ + D * T + DV * T + 2 * T + B * NQ * DV) + 2 * P * B * LIST_COLS
@@ -77,64 +81,62 @@ def tile_attend_sigmoid_kernel(tc, qT, kT, vT, vs, kb, offs, out):
         nc.gpsimd.memset(vs_win[:ROW, :], 0.0)
         identity = keep.tile([P, P], F32, name="identity")
         make_identity(nc, identity[:])
-        identity_late = keep.tile([P, P], F32, name="identity_late", align_bytes=64)
-        nc.scalar.copy(identity_late[:], identity[:])
-        identity_last = keep.tile([P, P], F32, name="identity_last", align_bytes=64)
-        nc.scalar.copy(identity_last[:], identity[:])
-
-        kb_got = keep.tile([P, B * N], F32, name="kb_got")
-        nc.vector.tensor_copy(kb_got[:], kb_win[:].indirect(lists[:]))
+        late_identity = [keep.tile([P, P], F32, name=f"late_identity{b}", align_bytes=64) for b in range(B)]
+        for b in range(B):
+            nc.scalar.copy(late_identity[b][:], identity[:])
 
         def by_place(name, got):
             dealt = keep.tile([P, B, PACK, P], F32, name=name)
             for b in range(B):
                 nc.gpsimd.tensor_copy(
-                    dealt[:, b].rearrange("p t (m r) -> p m t r", r=4),
-                    got[:, b * N : (b + 1) * N].rearrange("p (m t r) -> p m t r", t=PACK, r=4),
+                    dealt[:, b].rearrange("p t (m r) -> p m t r", r=RUN),
+                    got[:, b * N : (b + 1) * N].rearrange("p (m t r) -> p m t r", t=PACK, r=RUN),
                 )
             return dealt
 
+        kb_got = keep.tile([P, B * N], F32, name="kb_got")
+        nc.vector.tensor_copy(kb_got[:], kb_win[:].indirect(lists[:]))
         kb_dealt = by_place("kb_dealt", kb_got)
-        kb_banks = []
+        kb_turned = []
         for b in range(B):
-            bank = in_bank(b, [P, PACK, P])
+            turned = in_bank(b, [P, PACK, P])
             for t in range(PACK):
-                nc.tensor.transpose(bank[:, t, :], kb_dealt[:, b, t, :], identity[:])
-            kb_banks.append(bank)
+                nc.tensor.transpose(turned[:, t, :], kb_dealt[:, b, t, :], identity[:])
+            kb_turned.append(turned)
         vs_got = keep.tile([P, B * N], F32, name="vs_got")
         nc.vector.tensor_copy(vs_got[:], vs_win[:].indirect(lists[:]))
         vs_dealt = by_place("vs_dealt", vs_got)
-        bank = scale_bank.tile([P, P + 2 * B * PACK], F32, name="vs_turned")
+        vs_turned = scale_bank.tile([P, P + 2 * B * PACK], F32, name="scale_bank")
         for n in reversed(range(B * PACK)):
             b, t = divmod(n, PACK)
-            nc.tensor.transpose(bank[:, 2 * n : 2 * n + P], vs_dealt[:, b, t, :], identity[:])
-        vs_psum = bank[:, ROW : ROW + 2 * B * PACK : 2].rearrange("p (b t) -> p b t", b=B)
+            nc.tensor.transpose(vs_turned[:, 2 * n : 2 * n + P], vs_dealt[:, b, t, :], identity[:])
+        vs_psum = vs_turned[:, ROW : ROW + 2 * B * PACK : 2].rearrange("p (b t) -> p b t", b=B)
 
         k_pairs = keep.tile([P, 2 * B * N * 2], BF16, name="k_pairs", align_bytes=64)
-        pair_halves = k_pairs[:].rearrange("p (c t m r half) -> p c half m t r", c=2, t=PACK, r=4, half=2)
+        pair_halves = k_pairs[:].rearrange("p (c t m r half) -> p c half m t r", c=2, t=PACK, r=RUN, half=2)
 
-        def places(j, first, count):
-            return pair_halves[:, j // 2, j % 2, first // 16 : (first + count) // 16]
+        def halves(j, first, count):
+            return pair_halves[:, j // 2, j % 2, first // SPAN : (first + count) // SPAN]
 
         for j in range(2):
-            nc.vector.tensor_copy(places(j, 0, N), k_win[j][:].indirect(own_list[0]))
+            nc.vector.tensor_copy(halves(j, 0, N), k_win[j][:].indirect(own_list[0]))
             rounded = keep.tile([P, T], BF16, name=f"k_rounded{j}")
             nc.scalar.activation(rounded[:], k_win[j][:], COPY)
-            nc.scalar.activation(places(j, N, N), rounded[:].indirect(own_list[1]), COPY)
-        nc.vector.tensor_copy(places(2, 0, B * N), k_win[2][:].indirect(lists[:]))
+            nc.scalar.activation(halves(j, N, N), rounded[:].indirect(own_list[1]), COPY)
+        nc.vector.tensor_copy(halves(2, 0, B * N), k_win[2][:].indirect(lists[:]))
         for first, count in ((0, N // 2), (N // 2, N // 2), (N, N)):
             nc.vector.tensor_copy(
-                places(3, first, count), k_win[3][:].indirect(lists[:, first // 16 : (first + count) // 16])
+                halves(3, first, count), k_win[3][:].indirect(lists[:, first // SPAN : (first + count) // SPAN])
             )
 
         columns = keep.tile([P, 2, B, PACK], F32, name="columns", tag="k_rounded1")
         kb_col, vs_sbuf = columns[:, 0], columns[:, 1]
         early = keep.tile([P, 4 * GROUP], BF16, name="early", align_bytes=64)
-        kb_mark = early[:, 3 * GROUP - 2 : 3 * GROUP].bitcast(F32)
+        first_bias = early[:, 3 * GROUP - 2 : 3 * GROUP].bitcast(F32)
         for b in range(B):
-            nc.scalar.copy(kb_col[:, b, :], kb_banks[b][:, :, ROW])
+            nc.scalar.copy(kb_col[:, b, :], kb_turned[b][:, :, ROW])
         nc.scalar.copy(vs_sbuf, vs_psum)
-        nc.scalar.copy(kb_mark, kb_col[:, 1, 0:1])
+        nc.scalar.copy(first_bias, kb_col[:, 1, 0:1])
 
         def mx_tiles(name, width, codes_tag=None, scales_tag=None):
             codes = keep.tile([P, width], U32, name=f"{name}_codes", tag=codes_tag or f"{name}_codes", align_bytes=64)
@@ -160,24 +162,23 @@ def tile_attend_sigmoid_kernel(tc, qT, kT, vT, vs, kb, offs, out):
             keep.tile([P, N * PACK], BF16, name=f"k_mixed{b}", tag=("k_mixed0", "q_raw0")[b], align_bytes=64)
             for b in range(B)
         ]
-        k_halves = [[k_mixed[b][:, group(2 * half, 2)] for half in range(2)] for b in range(B)]
 
-        def mix_views(b, first, count):
+        def weave_views(b, tiles, spans, pair):
             return (
-                q_mixed[b][:, PACK * first : PACK * (first + count)].rearrange("p (c i j) -> p c j i", i=4, j=PACK),
-                q_raw[b][:, :, first : first + count].rearrange("p j (c i) -> p c j i", i=4),
+                k_mixed[b][:].bitcast(pair).rearrange("p (t m r c) -> p t m c r", t=PACK, r=RUN, c=2)[:, tiles, spans],
+                k_pairs[:].bitcast(pair).rearrange("p (c t b m r) -> p b t m c r", c=2, t=PACK, b=B, r=RUN)[
+                    :, b, tiles, spans
+                ],
             )
 
-        def weave_views(b, tiles, rows, word):
-            return (
-                k_mixed[b][:].bitcast(word).rearrange("p (t m r c) -> p t m c r", t=PACK, r=4, c=2)[:, tiles, rows],
-                k_pairs[:].bitcast(word).rearrange("p (c t b m r) -> p b t m c r", c=2, t=PACK, b=B, r=4)[:, b, tiles, rows],
-            )
-
-        nc.scalar.copy(*weave_views(0, slice(0, PACK), slice(0, 16), U32))
-        nc.gpsimd.tensor_copy(*weave_views(0, slice(0, PACK), slice(16, 32), U32))
+        nc.scalar.copy(*weave_views(0, slice(0, PACK), slice(0, LIST_COLS // 2), U32))
+        nc.gpsimd.tensor_copy(*weave_views(0, slice(0, PACK), slice(LIST_COLS // 2, LIST_COLS), U32))
         for b in range(B):
-            nc.scalar.activation(*mix_views(b, 0, NQ), COPY)
+            nc.scalar.activation(
+                q_mixed[b][:].rearrange("p (c i j) -> p c j i", i=4, j=PACK),
+                q_raw[b][:].rearrange("p j (c i) -> p c j i", i=4),
+                COPY,
+            )
 
         q_mx = [mx_tiles(f"q{b}", NQ) for b in range(B)]
         k_mx = [
@@ -187,13 +188,13 @@ def tile_attend_sigmoid_kernel(tc, qT, kT, vT, vs, kb, offs, out):
         prob = [keep.tile([P, PACK, NQ], F32, name=f"prob{b}") for b in range(B)]
 
         def quantise_keys(b, half):
-            quantise(k_mx[b][half], block(0, 2), k_halves[b][half])
+            quantise(k_mx[b][half], block(0, 2), k_mixed[b][:, group(2 * half, 2)])
 
         def scores(b, half):
             for t in (2 * half, 2 * half + 1):
                 score = in_bank(t, [P, NQ])
                 multiply(score[:], k_mx[b][half], block(t % 2), q_mx[b], slice(0, NQ))
-                bias = kb_mark if (b, t) == (1, 0) else kb_col[:, b, t : t + 1]
+                bias = first_bias if (b, t) == (1, 0) else kb_col[:, b, t : t + 1]
                 nc.scalar.activation(prob[b][:, t, :], score[:], SIGMOID, bias=bias)
 
         quantise_keys(0, 0)
@@ -202,14 +203,14 @@ def tile_attend_sigmoid_kernel(tc, qT, kT, vT, vs, kb, offs, out):
         scores(0, 0)
         scores(0, 1)
         for half in range(2):
-            nc.vector.tensor_copy(*weave_views(1, slice(2 * half, 2 * half + 2), slice(0, 32), I32))
+            nc.vector.tensor_copy(*weave_views(1, slice(2 * half, 2 * half + 2), slice(0, LIST_COLS), I32))
         quantise_keys(1, 0)
         quantise(q_mx[1], slice(0, NQ), q_mixed[1][:])
         scores(1, 0)
         quantise_keys(1, 1)
         scores(1, 1)
 
-        last = keep.tile([P, 2 * GROUP], BF16, name="last", align_bytes=64)
+        late = keep.tile([P, 2 * GROUP], BF16, name="late", align_bytes=64)
         v10 = keep.tile([P, GROUP], BF16, name="v10", align_bytes=64)
         v11 = keep.tile([P, GROUP], BF16, name="v11", align_bytes=64)
 
@@ -222,10 +223,12 @@ def tile_attend_sigmoid_kernel(tc, qT, kT, vT, vs, kb, offs, out):
                 MULT,
             )
 
-        def turn(k, b, got, turns):
-            nc.vector.tensor_copy(got.rearrange("p (u m r i) -> p m u i r", u=2, r=4, i=2), v_win[k][:].indirect(own_list[b]))
+        def turn(k, b, got, first_identity):
+            nc.vector.tensor_copy(
+                got.rearrange("p (u m r i) -> p m u i r", u=2, r=RUN, i=2), v_win[k][:].indirect(own_list[b])
+            )
             turned = in_bank(((4, 5), (6, 4))[k][b], [P, 2, P])
-            for u, unit in turns:
+            for u, unit in enumerate((first_identity, identity)):
                 nc.tensor.transpose(turned[:, u, :], got.bitcast(F32)[:, block(u)], unit[:])
             return turned
 
@@ -234,74 +237,69 @@ def tile_attend_sigmoid_kernel(tc, qT, kT, vT, vs, kb, offs, out):
                 interleaved.bitcast(F32).rearrange("p (e u) -> p e u", u=2), turned[:].rearrange("p u e -> p e u")
             )
 
-        def own_tile(name):
+        def got_tile(name):
             return keep.tile([P, N], BF16, name=name, align_bytes=64)[:]
 
-        plain_turns = ((0, identity), (1, identity))
         weigh(nc.gpsimd, vs_sbuf, 0, 0, NQ - EARLY)
-        turned00 = turn(0, 0, own_tile("v_got00"), plain_turns)
-        got01 = own_tile("v_got01")
-        turned01 = turn(0, 1, got01, plain_turns)
-        resting = in_bank(0, [P, P])
+        turned00 = turn(0, 0, got_tile("v_got00"), identity)
+        got01 = got_tile("v_got01")
+        turned01 = turn(0, 1, got01, identity)
+        spare_turned = in_bank(0, [P, P])
 
-        def spare_turns(count, source):
+        def spare_turns(count, got):
             for n in range(count):
-                nc.tensor.transpose(resting[:], source.bitcast(F32)[:, block(0)], identity[:])
+                nc.tensor.transpose(spare_turned[:], got.bitcast(F32)[:, block(0)], identity[:])
 
-        spare_turns(5, got01)
+        spare_turns(SPARE_TURNS[0], got01)
         weigh(nc.vector, vs_psum, 0, NQ - EARLY, EARLY)
         weigh(nc.gpsimd, vs_sbuf, 1, 0, P)
-        idle = scale_bank.tile([P, 2 * NQ], F32, name="vs_turned")
-        for n in range(3):
-            multiply(idle[:, (n % 2) * NQ : (n % 2 + 1) * NQ], k_mx[1][1], block(0), q_mx[1], slice(0, NQ))
+        spare_scores = scale_bank.tile([P, 2 * NQ], F32, name="scale_bank")
+        for n in range(SPARE_PASSES):
+            multiply(spare_scores[:, (n % 2) * NQ : (n % 2 + 1) * NQ], k_mx[1][1], block(0), q_mx[1], slice(0, NQ))
 
-        planes = keep.tile([P, PACK, P], BF16, name="planes")
+        places = keep.tile([P, PACK, P], BF16, name="places")
         for t in range(PACK):
-            nc.scalar.activation(planes[:, t, :], prob[1][:, t, P:], COPY, scale=vs_sbuf[:, 1, t : t + 1])
+            nc.scalar.activation(places[:, t, :], prob[1][:, t, P:], COPY, scale=vs_sbuf[:, 1, t : t + 1])
         lay(early[:, group(0)], turned00)
         nc.scalar.copy(
-            last[:, group(1)].rearrange("p (c i t) -> p c t i", i=4, t=PACK),
-            planes[:].rearrange("p t (c i) -> p c t i", i=4),
+            late[:, group(1)].rearrange("p (c i t) -> p c t i", i=4, t=PACK),
+            places[:].rearrange("p t (c i) -> p c t i", i=4),
         )
-        lay(v10[:], turn(1, 0, last[:, group(0)], ((0, identity_late), (1, identity))))
-        spare_turns(3, last[:, group(0)])
-        lay(last[:, group(0)], turned01)
-        lay(v11[:], turn(1, 1, own_tile("v_got11"), ((0, identity_last), (1, identity))))
+        lay(v10[:], turn(1, 0, late[:, group(0)], late_identity[0]))
+        spare_turns(SPARE_TURNS[1], late[:, group(0)])
+        lay(late[:, group(0)], turned01)
+        lay(v11[:], turn(1, 1, got_tile("v_got11"), late_identity[1]))
 
-        mx = mx_tiles("mx", 8 * P, scales_tag="identity_late")
+        mx = mx_tiles("mx", 7 * P, scales_tag="late_identity0")
         quantise(mx, block(0, 2), early[:, group(0, 2)])
         quantise(mx, block(2), early[:, group(2)])
-        quantise(mx, block(4), v10[:])
-        w10_mx = mx_tiles("w10", P, scales_tag="identity_last")
+        quantise(mx, block(3), v10[:])
+        w10_mx = mx_tiles("w10", P, scales_tag="late_identity1")
         quantise(w10_mx, block(0), early[:, group(3)])
-        quantise(mx, block(5, 2), last[:])
-        quantise(mx, block(7), v11[:])
-        w_block = ((1, 2), (3, 6))
-        v_block = ((0, 5), (4, 7))
+        quantise(mx, block(4, 2), late[:])
+        quantise(mx, block(6), v11[:])
+        w_at = (((mx, block(1)), (mx, block(2))), ((w10_mx, block(0)), (mx, block(5))))
+        v_at = ((block(0), block(4)), (block(3), block(6)))
         results = [[keep.tile([P, DV], F32, name=f"result{b}{h}") for h in range(2)] for b in range(B)]
 
         def finish(b, h, k, bank, scale_out):
-            if (b, h) == (1, 0):
-                multiply(bank[:], w10_mx, block(0), mx, block(v_block[k][b]))
-            else:
-                multiply(bank[:], mx, block(w_block[b][h]), mx, block(v_block[k][b]))
-            scale_out(results[b][h][:, block(k)], bank[:])
+            product = in_bank(bank, [P, P])
+            multiply(product[:], *w_at[b][h], mx, v_at[k][b])
+            scale_out(results[b][h][:, block(k)], product[:])
             if (b, h) == (0, 0):
                 nc.sync.dma_start(out=out[b, block(h), block(k)], in_=results[b][h][:, block(k)])
             elif k == 1:
                 nc.sync.dma_start(out=out[b, block(h), :], in_=results[b][h][:])
 
-        def by_scalar(target, bank):
-            nc.scalar.activation(target, bank, COPY, scale=OUT_SCALE)
+        def by_scalar(target, product):
+            nc.scalar.activation(target, product, COPY, scale=OUT_SCALE)
 
-        def by_vector(target, bank):
-            nc.vector.tensor_scalar_mul(target, bank, OUT_SCALE)
+        def by_vector(target, product):
+            nc.vector.tensor_scalar_mul(target, product, OUT_SCALE)
 
-        finish(0, 0, 0, in_bank(0, [P, P]), by_scalar)
-        finish(0, 1, 0, in_bank(1, [P, P]), by_scalar)
-        finish(0, 0, 1, in_bank(2, [P, P]), by_scalar)
-        finish(0, 1, 1, in_bank(3, [P, P]), by_scalar)
-        finish(1, 0, 0, in_bank(6, [P, P]), by_vector)
-        finish(1, 1, 0, in_bank(5, [P, P]), by_scalar)
-        finish(1, 0, 1, in_bank(4, [P, P]), by_vector)
-        finish(1, 1, 1, in_bank(0, [P, P]), by_scalar)
+        for k in range(2):
+            for h in range(2):
+                finish(0, h, k, 2 * k + h, by_scalar)
+        for k, bank_of in enumerate(((6, 5), (4, 0))):
+            for h, scale_out in enumerate((by_vector, by_scalar)):
+                finish(1, h, k, bank_of[h], scale_out)

@@ -58,17 +58,17 @@ def tile_attend_sigmoid_kernel(tc, qT, kT, vT, vs, kb, offs, out):
         nc.scalar.dma_start(out=vs_win[ROW:P, :], in_=vs[0:1, :])
 
         k_rows = kT.rearrange("(p j) n -> j p n", j=PACK)
-        k_win = [keep.tile([P, T], F32, name=f"k_win{j}") for j in range(PACK)]
+        k_win = [keep.tile([P, T], F32, name=f"k_win{j}", align_bytes=4096) for j in range(PACK)]
         nc.sync.dma_start(out=k_win[0][:], in_=k_rows[0])
         nc.sync.dma_start(lists[:], offs)
         for j in range(1, PACK):
             nc.sync.dma_start(out=k_win[j][:], in_=k_rows[j])
         q_rows = qT.rearrange("b (p j) q -> b p j q", j=PACK)
-        q_raw = [keep.tile([P, PACK, NQ], F32, name=f"q_raw{b}", align_bytes=64) for b in range(B)]
+        q_raw = [keep.tile([P, PACK, NQ], F32, name=f"q_raw{b}", align_bytes=4096) for b in range(B)]
         for b in range(B):
             nc.sync.dma_start(out=q_raw[b][:], in_=q_rows[b])
         v_rows = vT.rearrange("(k p) n -> k p n", p=P)
-        v_win = [keep.tile([P, T], F32, name=f"v_win{k}", align_bytes=64) for k in range(DV // P)]
+        v_win = [keep.tile([P, T], F32, name=f"v_win{k}", align_bytes=4096) for k in range(DV // P)]
         for k in range(DV // P):
             nc.sync.dma_start(out=v_win[k][:], in_=v_rows[k])
 
@@ -139,7 +139,7 @@ def tile_attend_sigmoid_kernel(tc, qT, kT, vT, vs, kb, offs, out):
         nc.scalar.copy(first_bias, kb_col[:, 1, 0:1])
 
         def mx_tiles(name, width, codes_tag=None, scales_tag=None):
-            codes = keep.tile([P, width], U32, name=f"{name}_codes", tag=codes_tag or f"{name}_codes", align_bytes=64)
+            codes = keep.tile([P, width], U32, name=f"{name}_codes", tag=codes_tag or f"{name}_codes", align_bytes=4096 if codes_tag else 64)
             scales = keep.tile([P, width], U8, name=f"{name}_scales", tag=scales_tag or f"{name}_scales", align_bytes=64)
             return codes, scales
 
@@ -159,7 +159,7 @@ def tile_attend_sigmoid_kernel(tc, qT, kT, vT, vs, kb, offs, out):
 
         q_mixed = [keep.tile([P, NQ * PACK], BF16, name=f"q_mixed{b}", align_bytes=64) for b in range(B)]
         k_mixed = [
-            keep.tile([P, N * PACK], BF16, name=f"k_mixed{b}", tag=("k_mixed0", "q_raw0")[b], align_bytes=64)
+            keep.tile([P, N * PACK], BF16, name=f"k_mixed{b}", tag=("k_mixed0", "q_raw0")[b], align_bytes=4096)
             for b in range(B)
         ]
 
@@ -280,7 +280,7 @@ def tile_attend_sigmoid_kernel(tc, qT, kT, vT, vs, kb, offs, out):
         quantise(mx, block(6), v11[:])
         w_at = (((mx, block(1)), (mx, block(2))), ((w10_mx, block(0)), (mx, block(5))))
         v_at = ((block(0), block(4)), (block(3), block(6)))
-        results = [[keep.tile([P, DV], F32, name=f"result{b}{h}") for h in range(2)] for b in range(B)]
+        results = [[keep.tile([P, DV], F32, name=f"result{b}{h}", align_bytes=1024) for h in range(2)] for b in range(B)]
 
         def finish(b, h, k, bank, scale_out):
             product = in_bank(bank, [P, P])

@@ -58,17 +58,17 @@ def tile_attend_sigmoid_kernel(tc, qT, kT, vT, vs, kb, offs, out):
         nc.scalar.dma_start(out=vs_win[ROW:P, :], in_=vs[0:1, :])
 
         k_rows = kT.rearrange("(p j) n -> j p n", j=PACK)
-        k_win = [keep.tile([P, T], F32, name=f"k_win{j}", align_bytes=4096) for j in range(PACK)]
+        k_win = [keep.tile([P, T], F32, name=f"k_win{j}") for j in range(PACK)]
         nc.sync.dma_start(out=k_win[0][:], in_=k_rows[0])
         nc.sync.dma_start(lists[:], offs)
         for j in range(1, PACK):
             nc.sync.dma_start(out=k_win[j][:], in_=k_rows[j])
         q_rows = qT.rearrange("b (p j) q -> b p j q", j=PACK)
-        q_raw = [keep.tile([P, PACK, NQ], F32, name=f"q_raw{b}", align_bytes=4096) for b in range(B)]
+        q_raw = [keep.tile([P, PACK, NQ], F32, name=f"q_raw{b}", align_bytes=64) for b in range(B)]
         for b in range(B):
             nc.sync.dma_start(out=q_raw[b][:], in_=q_rows[b])
         v_rows = vT.rearrange("(k p) n -> k p n", p=P)
-        v_win = [keep.tile([P, T], F32, name=f"v_win{k}", align_bytes=4096) for k in range(DV // P)]
+        v_win = [keep.tile([P, T], F32, name=f"v_win{k}", align_bytes=64) for k in range(DV // P)]
         for k in range(DV // P):
             nc.sync.dma_start(out=v_win[k][:], in_=v_rows[k])
 
@@ -139,7 +139,7 @@ def tile_attend_sigmoid_kernel(tc, qT, kT, vT, vs, kb, offs, out):
         nc.scalar.copy(first_bias, kb_col[:, 1, 0:1])
 
         def mx_tiles(name, width, codes_tag=None, scales_tag=None):
-            codes = keep.tile([P, width], U32, name=f"{name}_codes", tag=codes_tag or f"{name}_codes", align_bytes=4096 if codes_tag else 64)
+            codes = keep.tile([P, width], U32, name=f"{name}_codes", tag=codes_tag or f"{name}_codes", align_bytes=64)
             scales = keep.tile([P, width], U8, name=f"{name}_scales", tag=scales_tag or f"{name}_scales", align_bytes=64)
             return codes, scales
 
@@ -159,7 +159,7 @@ def tile_attend_sigmoid_kernel(tc, qT, kT, vT, vs, kb, offs, out):
 
         q_mixed = [keep.tile([P, NQ * PACK], BF16, name=f"q_mixed{b}", align_bytes=64) for b in range(B)]
         k_mixed = [
-            keep.tile([P, N * PACK], BF16, name=f"k_mixed{b}", tag=("k_mixed0", "q_raw0")[b], align_bytes=4096)
+            keep.tile([P, N * PACK], BF16, name=f"k_mixed{b}", tag=("k_mixed0", "q_raw0")[b], align_bytes=64)
             for b in range(B)
         ]
 
@@ -280,7 +280,9 @@ def tile_attend_sigmoid_kernel(tc, qT, kT, vT, vs, kb, offs, out):
         quantise(mx, block(6), v11[:])
         w_at = (((mx, block(1)), (mx, block(2))), ((w10_mx, block(0)), (mx, block(5))))
         v_at = ((block(0), block(4)), (block(3), block(6)))
-        results = [[keep.tile([P, DV], F32, name=f"result{b}{h}", align_bytes=1024) for h in range(2)] for b in range(B)]
+        results = [
+            [keep.tile([P, DV], F32, name=f"result{b}{h}", align_bytes=4 * DV) for h in range(2)] for b in range(B)
+        ]
 
         def finish(b, h, k, bank, scale_out):
             product = in_bank(bank, [P, P])

@@ -11,7 +11,7 @@ SPAN = PACK * RUN
 LIST_COLS = N // SPAN
 GROUP = P * PACK
 ROW = P - 1
-EARLY = 176
+EARLY = 128
 SPARE_PASSES = 3
 SPARE_TURNS = (5, 3)
 OUT_SCALE = 1.0 / 16.0

@@ -129,7 +129,7 @@ def tile_attend_sigmoid_kernel(tc, qT, kT, vT, vs, kb, offs, out):
                 halves(3, first, count), k_win[3][:].indirect(lists[:, first // SPAN : (first + count) // SPAN])
             )
 
-        columns = keep.tile([P, 2, B, PACK], F32, name="columns", tag="k_rounded1")
+        columns = keep.tile([P, 2, B, PACK], F32, name="columns")
         kb_col, vs_sbuf = columns[:, 0], columns[:, 1]
         early = keep.tile([P, 4 * GROUP], BF16, name="early", align_bytes=64)
         first_bias = early[:, 3 * GROUP - 2 : 3 * GROUP].bitcast(F32)

@@ -280,18 +280,23 @@ def tile_attend_sigmoid_kernel(tc, qT, kT, vT, vs, kb, offs, out):
         quantise(mx, block(6), v11[:])
         w_at = (((mx, block(1)), (mx, block(2))), ((w10_mx, block(0)), (mx, block(5))))
         v_at = ((block(0), block(4)), (block(3), block(6)))
-        results = [
-            [keep.tile([P, DV], F32, name=f"result{b}{h}", align_bytes=4 * DV) for h in range(2)] for b in range(B)
-        ]
+        results = [keep.tile([P, 2, P], F32, name=f"result{n}", align_bytes=4 * DV) for n in range(4)]
 
         def finish(b, h, k, bank, scale_out):
             product = in_bank(bank, [P, P])
             multiply(product[:], *w_at[b][h], mx, v_at[k][b])
-            scale_out(results[b][h][:, block(k)], product[:])
-            if (b, h) == (0, 0):
-                nc.sync.dma_start(out=out[b, block(h), block(k)], in_=results[b][h][:, block(k)])
-            elif k == 1:
-                nc.sync.dma_start(out=out[b, block(h), :], in_=results[b][h][:])
+            if b == 0:
+                scale_out(results[h][:, k, :], product[:])
+                if h == 0:
+                    nc.sync.dma_start(out=out[b, block(h), block(k)], in_=results[h][:, k, :])
+                elif k == 1:
+                    nc.sync.dma_start(out=out[b, block(h), :], in_=results[h][:].rearrange("p k e -> p (k e)"))
+            else:
+                scale_out(results[2 + k][:, h, :], product[:])
+                if h == 1:
+                    nc.sync.dma_start(
+                        out=out[b].rearrange("(h p) e -> p h e", h=2)[:, :, block(k)], in_=results[2 + k][:]
+                    )
 
         def by_scalar(target, product):
             nc.scalar.activation(target, product, COPY, scale=OUT_SCALE)

@@ -234,7 +234,7 @@ def tile_attend_sigmoid_kernel(tc, qT, kT, vT, vs, kb, offs, out):
 
         def lay(interleaved, turned):
             nc.scalar.copy(
-                interleaved.bitcast(F32).rearrange("p (e u) -> p e u", u=2), turned[:].rearrange("p u e -> p e u")
+                interleaved.bitcast(F32).rearrange("p (e u) -> p e u", u=2), turned.rearrange("p u e -> p e u")
             )
 
         def got_tile(name):
@@ -260,15 +260,17 @@ def tile_attend_sigmoid_kernel(tc, qT, kT, vT, vs, kb, offs, out):
         places = keep.tile([P, PACK, P], BF16, name="places")
         for t in range(PACK):
             nc.scalar.activation(places[:, t, :], prob[1][:, t, P:], COPY, scale=vs_sbuf[:, 1, t : t + 1])
-        lay(early[:, group(0)], turned00)
+        lay(early[:, group(0)], turned00[:])
         nc.scalar.copy(
             late[:, group(1)].rearrange("p (c i t) -> p c t i", i=4, t=PACK),
             places[:].rearrange("p t (c i) -> p c t i", i=4),
         )
-        lay(v10[:], turn(1, 0, late[:, group(0)], late_identity[0]))
+        lay(v10[:], turn(1, 0, late[:, group(0)], late_identity[0])[:])
         spare_turns(SPARE_TURNS[1], late[:, group(0)])
-        lay(late[:, group(0)], turned01)
-        lay(v11[:], turn(1, 1, got_tile("v_got11"), late_identity[1]))
+        lay(late[:, group(0)], turned01[:])
+        turned11 = turn(1, 1, got_tile("v_got11"), late_identity[1])
+        for half in range(2):
+            lay(v11[:, half * GROUP // 2 : (half + 1) * GROUP // 2], turned11[:, :, half * P // 2 : (half + 1) * P // 2])
 
         mx = mx_tiles("mx", 7 * P, scales_tag="late_identity0")
         quantise(mx, block(0, 2), early[:, group(0, 2)])
@@ -277,7 +279,9 @@ def tile_attend_sigmoid_kernel(tc, qT, kT, vT, vs, kb, offs, out):
         w10_mx = mx_tiles("w10", P, scales_tag="late_identity1")
         quantise(w10_mx, block(0), early[:, group(3)])
         quantise(mx, block(4, 2), late[:])
-        quantise(mx, block(6), v11[:])
+        for half in range(2):
+            first = 6 * P + half * P // 2
+            quantise(mx, slice(first, first + P // 2), v11[:, half * GROUP // 2 : (half + 1) * GROUP // 2])
         w_at = (((mx, block(1)), (mx, block(2))), ((w10_mx, block(0)), (mx, block(5))))
         v_at = ((block(0), block(4)), (block(3), block(6)))
         results = [keep.tile([P, 2, P], F32, name=f"result{n}", align_bytes=4 * DV) for n in range(4)]

@@ -68,7 +68,7 @@ def tile_attend_sigmoid_kernel(tc, qT, kT, vT, vs, kb, offs, out):
         for b in range(B):
             nc.sync.dma_start(out=q_raw[b][:], in_=q_rows[b])
         v_rows = vT.rearrange("(k p) n -> k p n", p=P)
-        v_win = [keep.tile([P, T], F32, name=f"v_win{k}", align_bytes=64) for k in range(DV // P)]
+        v_win = [keep.tile([P, T], F32, name=f"v_win{k}", align_bytes=256) for k in range(DV // P)]
         for k in range(DV // P):
             nc.sync.dma_start(out=v_win[k][:], in_=v_rows[k])
 
@@ -139,7 +139,7 @@ def tile_attend_sigmoid_kernel(tc, qT, kT, vT, vs, kb, offs, out):
         nc.scalar.copy(first_bias, kb_col[:, 1, 0:1])
 
         def mx_tiles(name, width, codes_tag=None, scales_tag=None):
-            codes = keep.tile([P, width], U32, name=f"{name}_codes", tag=codes_tag or f"{name}_codes", align_bytes=64)
+            codes = keep.tile([P, width], U32, name=f"{name}_codes", tag=codes_tag or f"{name}_codes", align_bytes=64 if codes_tag else 256)
             scales = keep.tile([P, width], U8, name=f"{name}_scales", tag=scales_tag or f"{name}_scales", align_bytes=64)
             return codes, scales
 
@@ -210,9 +210,9 @@ def tile_attend_sigmoid_kernel(tc, qT, kT, vT, vs, kb, offs, out):
         quantise_keys(1, 1)
         scores(1, 1)
 
-        late = keep.tile([P, 2 * GROUP], BF16, name="late", align_bytes=64)
+        late = keep.tile([P, 2 * GROUP], BF16, name="late", align_bytes=256)
         v10 = keep.tile([P, GROUP], BF16, name="v10", align_bytes=64)
-        v11 = keep.tile([P, GROUP], BF16, name="v11", align_bytes=64)
+        v11 = keep.tile([P, GROUP], BF16, name="v11", align_bytes=256)
 
         def weigh(engine, scales, b, first, count):
             start = GROUP + PACK * (b * NQ + first)
@@ -238,7 +238,7 @@ def tile_attend_sigmoid_kernel(tc, qT, kT, vT, vs, kb, offs, out):
             )
 
         def got_tile(name):
-            return keep.tile([P, N], BF16, name=name, align_bytes=64)[:]
+            return keep.tile([P, N], BF16, name=name, align_bytes=256)[:]
 
         weigh(nc.gpsimd, vs_sbuf, 0, 0, NQ - EARLY)
         turned00 = turn(0, 0, got_tile("v_got00"), identity)

@@ -13,7 +13,7 @@ GROUP = P * PACK
 ROW = P - 1
 EARLY = 128
 SPARE_PASSES = 3
-SPARE_TURNS = (5, 3)
+SPARE_TURNS = (4, 4)
 OUT_SCALE = 1.0 / 16.0
 FLOPS = 2 * B * NQ * N * (D + DV)
 BYTES = 4 * (B * D * NQ + D * T + DV * T + 2 * T + B * NQ * DV) + 2 * P * B * LIST_COLS

@@ -12,8 +12,8 @@ LIST_COLS = N // SPAN
 GROUP = P * PACK
 ROW = P - 1
 EARLY = 128
-SPARE_PASSES = 3
-SPARE_TURNS = (4, 4)
+SPARE_COLUMNS = (512, 256)
+SPARE_TURNS = 2
 OUT_SCALE = 1.0 / 16.0
 FLOPS = 2 * B * NQ * N * (D + DV)
 BYTES = 4 * (B * D * NQ + D * T + DV * T + 2 * T + B * NQ * DV) + 2 * P * B * LIST_COLS
@@ -180,7 +180,7 @@ def tile_attend_sigmoid_kernel(tc, qT, kT, vT, vs, kb, offs, out):
                 COPY,
             )
 
-        q_mx = [mx_tiles(f"q{b}", NQ) for b in range(B)]
+        q_mx = mx_tiles("q", B * NQ)
         k_mx = [
             [mx_tiles(f"k{b}{half}", 2 * P, codes_tag="q_raw1" if (b, half) == (1, 1) else None) for half in range(2)]
             for b in range(B)
@@ -193,19 +193,19 @@ def tile_attend_sigmoid_kernel(tc, qT, kT, vT, vs, kb, offs, out):
         def scores(b, half):
             for t in (2 * half, 2 * half + 1):
                 score = in_bank(t, [P, NQ])
-                multiply(score[:], k_mx[b][half], block(t % 2), q_mx[b], slice(0, NQ))
+                multiply(score[:], k_mx[b][half], block(t % 2), q_mx, block(2 * b, 2))
                 bias = first_bias if (b, t) == (1, 0) else kb_col[:, b, t : t + 1]
                 nc.scalar.activation(prob[b][:, t, :], score[:], SIGMOID, bias=bias)
 
         quantise_keys(0, 0)
         quantise_keys(0, 1)
-        quantise(q_mx[0], slice(0, NQ), q_mixed[0][:])
+        quantise(q_mx, block(0, 2), q_mixed[0][:])
         scores(0, 0)
         scores(0, 1)
         for half in range(2):
             nc.vector.tensor_copy(*weave_views(1, slice(2 * half, 2 * half + 2), slice(0, LIST_COLS), I32))
         quantise_keys(1, 0)
-        quantise(q_mx[1], slice(0, NQ), q_mixed[1][:])
+        quantise(q_mx, block(2, 2), q_mixed[1][:])
         scores(1, 0)
         quantise_keys(1, 1)
         scores(1, 1)
@@ -223,39 +223,31 @@ def tile_attend_sigmoid_kernel(tc, qT, kT, vT, vs, kb, offs, out):
                 MULT,
             )
 
-        def turn(k, b, got, first_identity):
+        def gather_values(k, b):
+            got = keep.tile([P, N], BF16, name=f"v_got{k}{b}", align_bytes=256)
             nc.vector.tensor_copy(
-                got.rearrange("p (u m r i) -> p m u i r", u=2, r=RUN, i=2), v_win[k][:].indirect(own_list[b])
+                got[:].rearrange("p (u m r i) -> p m u i r", u=2, r=RUN, i=2), v_win[k][:].indirect(own_list[b])
             )
-            turned = in_bank(((4, 5), (6, 4))[k][b], [P, 2, P])
+            return got[:].bitcast(F32)
+
+        def turn(turned, got, first_identity):
             for u, unit in enumerate((first_identity, identity)):
-                nc.tensor.transpose(turned[:, u, :], got.bitcast(F32)[:, block(u)], unit[:])
-            return turned
+                nc.tensor.transpose(turned[:, u, :], got[:, block(u)], unit[:])
 
         def lay(interleaved, turned):
             nc.scalar.copy(
                 interleaved.bitcast(F32).rearrange("p (e u) -> p e u", u=2), turned.rearrange("p u e -> p e u")
             )
 
-        def got_tile(name):
-            return keep.tile([P, N], BF16, name=name, align_bytes=256)[:]
-
         weigh(nc.gpsimd, vs_sbuf, 0, 0, NQ - EARLY)
-        turned00 = turn(0, 0, got_tile("v_got00"), identity)
-        got01 = got_tile("v_got01")
-        turned01 = turn(0, 1, got01, identity)
-        spare_turned = in_bank(0, [P, P])
-
-        def spare_turns(count, got):
-            for n in range(count):
-                nc.tensor.transpose(spare_turned[:], got.bitcast(F32)[:, block(0)], identity[:])
-
-        spare_turns(SPARE_TURNS[0], got01)
+        turned00 = in_bank(2, [P, 2, P])
+        turn(turned00[:], gather_values(0, 0), identity)
+        got01 = gather_values(0, 1)
         weigh(nc.vector, vs_psum, 0, NQ - EARLY, EARLY)
         weigh(nc.gpsimd, vs_sbuf, 1, 0, P)
-        spare_scores = scale_bank.tile([P, 2 * NQ], F32, name="scale_bank")
-        for n in range(SPARE_PASSES):
-            multiply(spare_scores[:, (n % 2) * NQ : (n % 2 + 1) * NQ], k_mx[1][1], block(0), q_mx[1], slice(0, NQ))
+        spare_scores = scale_bank.tile([P, B * NQ], F32, name="scale_bank")
+        for width in SPARE_COLUMNS:
+            multiply(spare_scores[:, :width], k_mx[1][1], block(0), q_mx, slice(0, width))
 
         places = keep.tile([P, PACK, P], BF16, name="places")
         for t in range(PACK):
@@ -265,10 +257,17 @@ def tile_attend_sigmoid_kernel(tc, qT, kT, vT, vs, kb, offs, out):
             late[:, group(1)].rearrange("p (c i t) -> p c t i", i=4, t=PACK),
             places[:].rearrange("p t (c i) -> p c t i", i=4),
         )
-        lay(v10[:], turn(1, 0, late[:, group(0)], late_identity[0])[:])
-        spare_turns(SPARE_TURNS[1], late[:, group(0)])
-        lay(late[:, group(0)], turned01[:])
-        turned11 = turn(1, 1, got_tile("v_got11"), late_identity[1])
+        got10 = gather_values(1, 0)
+        turned_pair = in_bank(5, [P, 2, 2, P])
+        turn(turned_pair[:, 0], got10, late_identity[0])
+        turn(turned_pair[:, 1], got01, identity)
+        spare_turned = in_bank(0, [P, P])
+        for n in range(SPARE_TURNS):
+            nc.tensor.transpose(spare_turned[:], got10[:, block(0)], identity[:])
+        lay(v10[:], turned_pair[:, 0])
+        lay(late[:, group(0)], turned_pair[:, 1])
+        turned11 = in_bank(6, [P, 2, P])
+        turn(turned11[:], gather_values(1, 1), late_identity[1])
         for half in range(2):
             lay(v11[:, half * GROUP // 2 : (half + 1) * GROUP // 2], turned11[:, :, half * P // 2 : (half + 1) * P // 2])
 
@@ -311,6 +310,6 @@ def tile_attend_sigmoid_kernel(tc, qT, kT, vT, vs, kb, offs, out):
         for k in range(2):
             for h in range(2):
                 finish(0, h, k, 2 * k + h, by_scalar)
-        for k, bank_of in enumerate(((6, 5), (4, 0))):
+        for k, bank_of in enumerate(((4, 5), (6, 0))):
             for h, scale_out in enumerate((by_vector, by_scalar)):
                 finish(1, h, k, bank_of[h], scale_out)

@@ -85,6 +85,9 @@ def tile_attend_sigmoid_kernel(tc, qT, kT, vT, vs, kb, offs, out):
         for b in range(B):
             nc.scalar.copy(late_identity[b][:], identity[:])
 
+        spare_identity = keep.tile([P, P], BF16, name="spare_identity")
+        nc.scalar.copy(spare_identity[:], identity[:])
+
         def by_place(name, got):
             dealt = keep.tile([P, B, PACK, P], F32, name=name)
             for b in range(B):
@@ -261,9 +264,9 @@ def tile_attend_sigmoid_kernel(tc, qT, kT, vT, vs, kb, offs, out):
         turned_pair = in_bank(5, [P, 2, 2, P])
         turn(turned_pair[:, 0], got10, late_identity[0])
         turn(turned_pair[:, 1], got01, identity)
-        spare_turned = in_bank(0, [P, P])
+        spare_turned = banks.tile([P, P], BF16, name="bank0")
         for n in range(SPARE_TURNS):
-            nc.tensor.transpose(spare_turned[:], got10[:, block(0)], identity[:])
+            nc.tensor.transpose(spare_turned[:], got10.bitcast(BF16)[:, block(0)], spare_identity[:])
         lay(v10[:], turned_pair[:, 0])
         lay(late[:, group(0)], turned_pair[:, 1])
         turned11 = in_bank(6, [P, 2, P])

@@ -59,9 +59,9 @@ def tile_attend_sigmoid_kernel(tc, qT, kT, vT, vs, kb, offs, out):
 
         k_rows = kT.rearrange("(p j) n -> j p n", j=PACK)
         k_win = [keep.tile([P, T], F32, name=f"k_win{j}") for j in range(PACK)]
-        nc.sync.dma_start(out=k_win[0][:], in_=k_rows[0])
+        nc.sync.dma_start(out=k_win[2][:], in_=k_rows[2])
         nc.sync.dma_start(lists[:], offs)
-        for j in range(1, PACK):
+        for j in (0, 1, 3):
             nc.sync.dma_start(out=k_win[j][:], in_=k_rows[j])
         q_rows = qT.rearrange("b (p j) q -> b p j q", j=PACK)
         q_raw = [keep.tile([P, PACK, NQ], F32, name=f"q_raw{b}", align_bytes=64) for b in range(B)]
@@ -121,23 +121,23 @@ def tile_attend_sigmoid_kernel(tc, qT, kT, vT, vs, kb, offs, out):
         def halves(j, first, count):
             return pair_halves[:, j // 2, j % 2, first // SPAN : (first + count) // SPAN]
 
+        rounded = keep.tile([P, T], BF16, name="k_rounded")
+        nc.scalar.activation(rounded[:], k_win[2][:], COPY)
+        nc.scalar.activation(halves(2, 0, B * N), rounded[:].indirect(lists[:]), COPY)
         for j in range(2):
-            nc.vector.tensor_copy(halves(j, 0, N), k_win[j][:].indirect(own_list[0]))
-            rounded = keep.tile([P, T], BF16, name=f"k_rounded{j}")
-            nc.scalar.activation(rounded[:], k_win[j][:], COPY)
-            nc.scalar.activation(halves(j, N, N), rounded[:].indirect(own_list[1]), COPY)
-        nc.vector.tensor_copy(halves(2, 0, B * N), k_win[2][:].indirect(lists[:]))
+            nc.vector.tensor_copy(halves(j, 0, B * N), k_win[j][:].indirect(lists[:]))
+        kb_col = keep.tile([P, B, PACK], F32, name="kb_col", tag="k_rounded")
+        for b in range(B):
+            nc.vector.tensor_copy(kb_col[:, b, :], kb_turned[b][:, :, ROW])
         for first, count in ((0, N // 2), (N // 2, N // 2), (N, N)):
             nc.vector.tensor_copy(
                 halves(3, first, count), k_win[3][:].indirect(lists[:, first // SPAN : (first + count) // SPAN])
             )
 
-        columns = keep.tile([P, 2, B, PACK], F32, name="columns")
-        kb_col, vs_sbuf = columns[:, 0], columns[:, 1]
+        vs_col = keep.tile([P, B, PACK], F32, name="vs_col")
+        vs_sbuf = vs_col[:]
         early = keep.tile([P, 4 * GROUP], BF16, name="early", align_bytes=64)
         first_bias = early[:, 3 * GROUP - 2 : 3 * GROUP].bitcast(F32)
-        for b in range(B):
-            nc.scalar.copy(kb_col[:, b, :], kb_turned[b][:, :, ROW])
         nc.scalar.copy(vs_sbuf, vs_psum)
         nc.scalar.copy(first_bias, kb_col[:, 1, 0:1])
 

from contextlib import ExitStack

import concourse.mybir as mybir
from concourse.masks import make_identity

B, NQ, D, DV, N, T = 2, 256, 512, 256, 512, 2048
P = 128
PACK = 4
RUN = 4
SPAN = PACK * RUN
LIST_COLS = N // SPAN
GROUP = P * PACK
ROW = P - 1
EARLY = 128
SPARE_COLUMNS = (512, 256)
SPARE_TURNS = 2
OUT_SCALE = 1.0 / 16.0
FLOPS = 2 * B * NQ * N * (D + DV)
BYTES = 4 * (B * D * NQ + D * T + DV * T + 2 * T + B * NQ * DV) + 2 * P * B * LIST_COLS

F32 = mybir.dt.float32
BF16 = mybir.dt.bfloat16
U32 = mybir.dt.uint32
I32 = mybir.dt.int32
U16 = mybir.dt.uint16
U8 = mybir.dt.uint8
FP8X4 = mybir.dt.float8_e4m3fn_x4
COPY = mybir.ActivationFunctionType.Copy
SIGMOID = mybir.ActivationFunctionType.Sigmoid
MULT = mybir.AluOpType.mult


def block(first, count=1):
    return slice(first * P, (first + count) * P)


def group(first, count=1):
    return slice(first * GROUP, (first + count) * GROUP)


def tile_attend_sigmoid_kernel(tc, qT, kT, vT, vs, kb, offs, out):
    nc = tc.nc
    with ExitStack() as ctx:
        keep = ctx.enter_context(tc.tile_pool(name="keep", bufs=1))
        banks = ctx.enter_context(tc.psum_pool(name="banks", bufs=1))

        def in_bank(n, shape):
            return banks.tile(shape, F32, name=f"bank{n}")

        scale_bank = ctx.enter_context(tc.psum_pool(name="scale_bank", bufs=1))

        lists = keep.tile([P, B * LIST_COLS], U16, name="lists")
        own_list = [lists[:, b * LIST_COLS : (b + 1) * LIST_COLS] for b in range(B)]

        kb_win = keep.tile([P, T], F32, name="kb_win")
        vs_win = keep.tile([P, T], F32, name="vs_win")
        nc.scalar.dma_start(out=kb_win[ROW:P, :], in_=kb[0:1, :])
        nc.scalar.dma_start(out=vs_win[ROW:P, :], in_=vs[0:1, :])

        k_rows = kT.rearrange("(p j) n -> j p n", j=PACK)
        k_win = [keep.tile([P, T], F32, name=f"k_win{j}") for j in range(PACK)]
        nc.sync.dma_start(out=k_win[2][:], in_=k_rows[2])
        nc.sync.dma_start(lists[:], offs)
        for j in (0, 1, 3):
            nc.sync.dma_start(out=k_win[j][:], in_=k_rows[j])
        q_rows = qT.rearrange("b (p j) q -> b p j q", j=PACK)
        q_raw = [keep.tile([P, PACK, NQ], F32, name=f"q_raw{b}", align_bytes=64) for b in range(B)]
        for b in range(B):
            nc.sync.dma_start(out=q_raw[b][:], in_=q_rows[b])
        v_rows = vT.rearrange("(k p) n -> k p n", p=P)
        v_win = [keep.tile([P, T], F32, name=f"v_win{k}", align_bytes=256) for k in range(DV // P)]
        for k in range(DV // P):
            nc.sync.dma_start(out=v_win[k][:], in_=v_rows[k])

        zero = keep.tile([P, 1], F32, name="zero")
        nc.vector.memset(zero[:], 0.0)
        warmed = keep.tile([P, 1], F32, name="warmed")
        nc.scalar.activation(warmed[:], zero[:], SIGMOID)

        nc.vector.memset(kb_win[:ROW, :], 0.0)
        nc.gpsimd.memset(vs_win[:ROW, :], 0.0)
        identity = keep.tile([P, P], F32, name="identity")
        make_identity(nc, identity[:])
        late_identity = [keep.tile([P, P], F32, name=f"late_identity{b}", align_bytes=64) for b in range(B)]
        for b in range(B):
            nc.scalar.copy(late_identity[b][:], identity[:])

        spare_identity = keep.tile([P, P], BF16, name="spare_identity")
        nc.scalar.copy(spare_identity[:], identity[:])

        def by_place(name, got):
            dealt = keep.tile([P, B, PACK, P], F32, name=name)
            for b in range(B):
                nc.gpsimd.tensor_copy(
                    dealt[:, b].rearrange("p t (m r) -> p m t r", r=RUN),
                    got[:, b * N : (b + 1) * N].rearrange("p (m t r) -> p m t r", t=PACK, r=RUN),
                )
            return dealt

        kb_got = keep.tile([P, B * N], F32, name="kb_got")
        nc.vector.tensor_copy(kb_got[:], kb_win[:].indirect(lists[:]))
        kb_dealt = by_place("kb_dealt", kb_got)
        kb_turned = []
        for b in range(B):
            turned = in_bank(b, [P, PACK, P])
            for t in range(PACK):
                nc.tensor.transpose(turned[:, t, :], kb_dealt[:, b, t, :], identity[:])
            kb_turned.append(turned)
        vs_got = keep.tile([P, B * N], F32, name="vs_got")
        nc.vector.tensor_copy(vs_got[:], vs_win[:].indirect(lists[:]))
        vs_dealt = by_place("vs_dealt", vs_got)
        vs_turned = scale_bank.tile([P, P + 2 * B * PACK], F32, name="scale_bank")
        for n in reversed(range(B * PACK)):
            b, t = divmod(n, PACK)
            nc.tensor.transpose(vs_turned[:, 2 * n : 2 * n + P], vs_dealt[:, b, t, :], identity[:])
        vs_psum = vs_turned[:, ROW : ROW + 2 * B * PACK : 2].rearrange("p (b t) -> p b t", b=B)

        k_pairs = keep.tile([P, 2 * B * N * 2], BF16, name="k_pairs", align_bytes=64)
        pair_halves = k_pairs[:].rearrange("p (c t m r half) -> p c half m t r", c=2, t=PACK, r=RUN, half=2)

        def halves(j, first, count):
            return pair_halves[:, j // 2, j % 2, first // SPAN : (first + count) // SPAN]

        rounded = keep.tile([P, T], BF16, name="k_rounded")
        nc.scalar.activation(rounded[:], k_win[2][:], COPY)
        nc.scalar.activation(halves(2, 0, B * N), rounded[:].indirect(lists[:]), COPY)
        for j in range(2):
            nc.vector.tensor_copy(halves(j, 0, B * N), k_win[j][:].indirect(lists[:]))
        kb_col = keep.tile([P, B, PACK], F32, name="kb_col", tag="k_rounded")
        for b in range(B):
            nc.vector.tensor_copy(kb_col[:, b, :], kb_turned[b][:, :, ROW])
        for first, count in ((0, N // 2), (N // 2, N // 2), (N, N)):
            nc.vector.tensor_copy(
                halves(3, first, count), k_win[3][:].indirect(lists[:, first // SPAN : (first + count) // SPAN])
            )

        vs_col = keep.tile([P, B, PACK], F32, name="vs_col")
        vs_sbuf = vs_col[:]
        early = keep.tile([P, 4 * GROUP], BF16, name="early", align_bytes=64)
        first_bias = early[:, 3 * GROUP - 2 : 3 * GROUP].bitcast(F32)
        nc.scalar.copy(vs_sbuf, vs_psum)
        nc.scalar.copy(first_bias, kb_col[:, 1, 0:1])

        def mx_tiles(name, width, codes_tag=None, scales_tag=None):
            codes = keep.tile([P, width], U32, name=f"{name}_codes", tag=codes_tag or f"{name}_codes", align_bytes=64 if codes_tag else 256)
            scales = keep.tile([P, width], U8, name=f"{name}_scales", tag=scales_tag or f"{name}_scales", align_bytes=64)
            return codes, scales

        def quantise(mx, cols, interleaved):
            nc.vector.quantize_mx(out=mx[0][:, cols].bitcast(FP8X4), scales=mx[1][:, cols], in_=interleaved)

        def multiply(target, lhs, lhs_cols, rhs, rhs_cols):
            nc.tensor.matmul_mx(
                out=target,
                lhsT=lhs[0][:, lhs_cols].bitcast(FP8X4),
                lhsT_scale=lhs[1][:, lhs_cols],
                rhs=rhs[0][:, rhs_cols].bitcast(FP8X4),
                rhs_scale=rhs[1][:, rhs_cols],
                start=True,
                stop=True,
            )

        q_mixed = [keep.tile([P, NQ * PACK], BF16, name=f"q_mixed{b}", align_bytes=64) for b in range(B)]
        k_mixed = [
            keep.tile([P, N * PACK], BF16, name=f"k_mixed{b}", tag=("k_mixed0", "q_raw0")[b], align_bytes=64)
            for b in range(B)
        ]

        def weave_views(b, tiles, spans, pair):
            return (
                k_mixed[b][:].bitcast(pair).rearrange("p (t m r c) -> p t m c r", t=PACK, r=RUN, c=2)[:, tiles, spans],
                k_pairs[:].bitcast(pair).rearrange("p (c t b m r) -> p b t m c r", c=2, t=PACK, b=B, r=RUN)[
                    :, b, tiles, spans
                ],
            )

        nc.scalar.copy(*weave_views(0, slice(0, PACK), slice(0, LIST_COLS // 2), U32))
        nc.gpsimd.tensor_copy(*weave_views(0, slice(0, PACK), slice(LIST_COLS // 2, LIST_COLS), U32))
        for b in range(B):
            nc.scalar.activation(
                q_mixed[b][:].rearrange("p (c i j) -> p c j i", i=4, j=PACK),
                q_raw[b][:].rearrange("p j (c i) -> p c j i", i=4),
                COPY,
            )

        q_mx = mx_tiles("q", B * NQ)
        k_mx = [
            [mx_tiles(f"k{b}{half}", 2 * P, codes_tag="q_raw1" if (b, half) == (1, 1) else None) for half in range(2)]
            for b in range(B)
        ]
        prob = [keep.tile([P, PACK, NQ], F32, name=f"prob{b}") for b in range(B)]

        def quantise_keys(b, half):
            quantise(k_mx[b][half], block(0, 2), k_mixed[b][:, group(2 * half, 2)])

        def scores(b, half):
            for t in (2 * half, 2 * half + 1):
                score = in_bank(t, [P, NQ])
                multiply(score[:], k_mx[b][half], block(t % 2), q_mx, block(2 * b, 2))
                bias = first_bias if (b, t) == (1, 0) else kb_col[:, b, t : t + 1]
                nc.scalar.activation(prob[b][:, t, :], score[:], SIGMOID, bias=bias)

        quantise_keys(0, 0)
        quantise_keys(0, 1)
        quantise(q_mx, block(0, 2), q_mixed[0][:])
        scores(0, 0)
        scores(0, 1)
        for half in range(2):
            nc.vector.tensor_copy(*weave_views(1, slice(2 * half, 2 * half + 2), slice(0, LIST_COLS), I32))
        quantise_keys(1, 0)
        quantise(q_mx, block(2, 2), q_mixed[1][:])
        scores(1, 0)
        quantise_keys(1, 1)
        scores(1, 1)

        late = keep.tile([P, 2 * GROUP], BF16, name="late", align_bytes=256)
        v10 = keep.tile([P, GROUP], BF16, name="v10", align_bytes=64)
        v11 = keep.tile([P, GROUP], BF16, name="v11", align_bytes=256)

        def weigh(engine, scales, b, first, count):
            start = GROUP + PACK * (b * NQ + first)
            engine.tensor_tensor(
                early[:, start : start + PACK * count].rearrange("p (c i t) -> p c t i", i=4, t=PACK),
                prob[b][:, :, first : first + count].rearrange("p t (c i) -> p c t i", i=4),
                scales[:, b, :].unsqueeze(1).unsqueeze(3).to_broadcast([P, count // 4, PACK, 4]),
                MULT,
            )

        def gather_values(k, b):
            got = keep.tile([P, N], BF16, name=f"v_got{k}{b}", align_bytes=256)
            nc.vector.tensor_copy(
                got[:].rearrange("p (u m r i) -> p m u i r", u=2, r=RUN, i=2), v_win[k][:].indirect(own_list[b])
            )
            return got[:].bitcast(F32)

        def turn(turned, got, first_identity):
            for u, unit in enumerate((first_identity, identity)):
                nc.tensor.transpose(turned[:, u, :], got[:, block(u)], unit[:])

        def lay(interleaved, turned):
            nc.scalar.copy(
                interleaved.bitcast(F32).rearrange("p (e u) -> p e u", u=2), turned.rearrange("p u e -> p e u")
            )

        weigh(nc.gpsimd, vs_sbuf, 0, 0, NQ - EARLY)
        turned00 = in_bank(2, [P, 2, P])
        turn(turned00[:], gather_values(0, 0), identity)
        got01 = gather_values(0, 1)
        weigh(nc.vector, vs_psum, 0, NQ - EARLY, EARLY)
        weigh(nc.gpsimd, vs_sbuf, 1, 0, P)
        spare_scores = scale_bank.tile([P, B * NQ], F32, name="scale_bank")
        for width in SPARE_COLUMNS:
            multiply(spare_scores[:, :width], k_mx[1][1], block(0), q_mx, slice(0, width))

        places = keep.tile([P, PACK, P], BF16, name="places")
        for t in range(PACK):
            nc.scalar.activation(places[:, t, :], prob[1][:, t, P:], COPY, scale=vs_sbuf[:, 1, t : t + 1])
        lay(early[:, group(0)], turned00[:])
        nc.scalar.copy(
            late[:, group(1)].rearrange("p (c i t) -> p c t i", i=4, t=PACK),
            places[:].rearrange("p t (c i) -> p c t i", i=4),
        )
        got10 = gather_values(1, 0)
        turned_pair = in_bank(5, [P, 2, 2, P])
        turn(turned_pair[:, 0], got10, late_identity[0])
        turn(turned_pair[:, 1], got01, identity)
        spare_turned = banks.tile([P, P], BF16, name="bank0")
        for n in range(SPARE_TURNS):
            nc.tensor.transpose(spare_turned[:], got10.bitcast(BF16)[:, block(0)], spare_identity[:])
        lay(v10[:], turned_pair[:, 0])
        lay(late[:, group(0)], turned_pair[:, 1])
        turned11 = in_bank(6, [P, 2, P])
        turn(turned11[:], gather_values(1, 1), late_identity[1])
        for half in range(2):
            lay(v11[:, half * GROUP // 2 : (half + 1) * GROUP // 2], turned11[:, :, half * P // 2 : (half + 1) * P // 2])

        mx = mx_tiles("mx", 7 * P, scales_tag="late_identity0")
        quantise(mx, block(0, 2), early[:, group(0, 2)])
        quantise(mx, block(2), early[:, group(2)])
        quantise(mx, block(3), v10[:])
        w10_mx = mx_tiles("w10", P, scales_tag="late_identity1")
        quantise(w10_mx, block(0), early[:, group(3)])
        quantise(mx, block(4, 2), late[:])
        for half in range(2):
            first = 6 * P + half * P // 2
            quantise(mx, slice(first, first + P // 2), v11[:, half * GROUP // 2 : (half + 1) * GROUP // 2])
        w_at = (((mx, block(1)), (mx, block(2))), ((w10_mx, block(0)), (mx, block(5))))
        v_at = ((block(0), block(4)), (block(3), block(6)))
        results = [keep.tile([P, 2, P], F32, name=f"result{n}", align_bytes=4 * DV) for n in range(4)]

        def finish(b, h, k, bank, scale_out):
            product = in_bank(bank, [P, P])
            multiply(product[:], *w_at[b][h], mx, v_at[k][b])
            if b == 0:
                scale_out(results[h][:, k, :], product[:])
                if h == 0:
                    nc.sync.dma_start(out=out[b, block(h), block(k)], in_=results[h][:, k, :])
                elif k == 1:
                    nc.sync.dma_start(out=out[b, block(h), :], in_=results[h][:].rearrange("p k e -> p (k e)"))
            else:
                scale_out(results[2 + k][:, h, :], product[:])
                if h == 1:
                    nc.sync.dma_start(
                        out=out[b].rearrange("(h p) e -> p h e", h=2)[:, :, block(k)], in_=results[2 + k][:]
                    )

        def by_scalar(target, product):
            nc.scalar.activation(target, product, COPY, scale=OUT_SCALE)

        def by_vector(target, product):
            nc.vector.tensor_scalar_mul(target, product, OUT_SCALE)

        for k in range(2):
            for h in range(2):
                finish(0, h, k, 2 * k + h, by_scalar)
        for k, bank_of in enumerate(((4, 5), (6, 0))):
            for h, scale_out in enumerate((by_vector, by_scalar)):
                finish(1, h, k, bank_of[h], scale_out)
